import numpy as np
import ml_dtypes


def mxq(x, axis, fmt="e4m3"):
    dtype, down = {"e4m3": (ml_dtypes.float8_e4m3fn, 7), "e5m2": (ml_dtypes.float8_e5m2, 14)}[fmt]
    v = np.moveaxis(np.asarray(x, np.float32).astype(ml_dtypes.bfloat16).astype(np.float64), axis, -1)
    blocks = v.reshape(v.shape[:-1] + (-1, 32))
    amax = np.abs(blocks).max(-1, keepdims=True)
    byte = np.maximum(np.where(amax > 0, np.frexp(amax)[1] - 1 + 127, 0) - down, 1)
    scale = np.exp2(byte - 127.0)
    codes = (blocks / scale).astype(np.float32).astype(dtype).astype(np.float64)
    return np.moveaxis((codes * scale).reshape(v.shape), -1, axis)


WIDE = False


def mx_kscale(k):
    if not WIDE:
        return np.ones(k)
    levels = np.array([24, -24, 12, -12, 0])
    if k % 512:
        return np.exp2(np.random.permutation(np.resize(levels, k // 32))).repeat(32)
    a = np.empty((k // 512, 16))
    for p in range(k // 512):
        a[p, :8] = np.random.permutation(np.resize(levels, 8))
        for g in range(8):
            far = levels[np.abs(levels - a[p, g]) >= 10]
            a[p, g + 8] = far[np.random.randint(len(far))]
    return np.exp2(a.ravel()).repeat(32)


def f64(x):
    return np.asarray(x).astype(np.float64)


def striped(idx):
    return np.tile(idx.reshape(-1, 16).T, (8, 1)).astype(np.uint16)


def unstriped(offs):
    return offs[:16].T.reshape(-1).astype(np.int64)


E2M1 = np.array([0.0, 0.5, 1.0, 1.5, 2.0, 3.0, 4.0, 6.0, -0.0, -0.5, -1.0, -1.5, -2.0, -3.0, -4.0, -6.0])


def pack_weight(w, fmt):
    k, n = w.shape
    w = f64(np.asarray(w, np.float32).astype(ml_dtypes.bfloat16)).reshape(k // 32, 32, n)
    amax = np.abs(w).max(1)
    if fmt == "e4m3":
        byte = np.frexp(amax)[1] - 1 + 127 - 7
    else:
        mant, ex = np.frexp(amax / 6.0)
        byte = np.where(mant > 0.5, ex, ex - 1) + 127
    byte = np.clip(np.where(amax > 0, byte, 1), 1, 254)
    scaled = (w * np.exp2(127.0 - byte)[:, None, :]).reshape(k, n).astype(np.float32)
    by_word = np.ascontiguousarray(scaled.reshape(k // 512, 128, 4, n).transpose(0, 1, 3, 2))
    if fmt == "e4m3":
        words = by_word.astype(ml_dtypes.float8_e4m3fn).view(np.uint8)
    else:
        c = by_word.astype(ml_dtypes.float4_e2m1fn).view(np.uint8) & 0xF
        words = (c[..., 0::2] | (c[..., 1::2] << 4)).reshape(k // 512, 128, 2 * n)
    return np.ascontiguousarray(words), np.ascontiguousarray(byte.astype(np.uint8).reshape(k // 512, 16, n))


def unpack_weight(words, scales, fmt):
    g, _, n = scales.shape
    words = np.ascontiguousarray(words).reshape(g, 128, n, -1)
    if fmt == "e4m3":
        vals = words.view(ml_dtypes.float8_e4m3fn).astype(np.float64)
    else:
        nib = np.empty((g, 128, n, 4), np.uint8)
        nib[..., 0::2] = words & 0xF
        nib[..., 1::2] = words >> 4
        vals = E2M1[nib]
    vals = vals * np.repeat(np.exp2(scales.astype(np.float64) - 127.0), 8, axis=1)[..., None]
    return vals.transpose(0, 1, 3, 2).reshape(g * 512, n)


def gelu(f):
    return 0.5 * f * (1.0 + np.tanh(np.sqrt(2.0 / np.pi) * (f + 0.044715 * f**3)))


K, R, N, T, J = 512, 1024, 512, 2048, 1024


def setup_inputs():
    n = np.random.standard_normal
    s = mx_kscale(K)[:, None]
    u = mx_kscale(R)[:, None]
    wd = n((R, N)) / np.sqrt(R) / u
    wd4 = pack_weight(wd, "e2m1")
    wdrest = wd - unpack_weight(*wd4, "e2m1")
    p_tab = pack_weight(n((K, T)) * s, "e4m3")
    p_wg = pack_weight(n((K, R)) / np.sqrt(K) / s, "e4m3")
    p_wd8 = pack_weight(wdrest, "e4m3")
    return {
        "tab_words": p_tab[0],
        "tab_scales": p_tab[1],
        "wg_words": p_wg[0],
        "wg_scales": p_wg[1],
        "wu": (n((K, R)) / np.sqrt(K) / s * u.T).astype(np.float32),
        "wd4_words": wd4[0],
        "wd4_scales": wd4[1],
        "wd8_words": p_wd8[0],
        "wd8_scales": p_wd8[1],
        "res": (n((N, J))).astype(np.float32),
        "offs": striped(np.random.permutation(T)[:J]),
    }


def reference(tab_words, tab_scales, wg_words, wg_scales, wu, wd4_words, wd4_scales, wd8_words, wd8_scales, res, offs):
    idx = unstriped(offs)
    tab_ = unpack_weight(tab_words, tab_scales, "e4m3")[:, idx]
    wg_ = unpack_weight(wg_words, wg_scales, "e4m3")
    wu_ = mxq(f64(wu), 0, "e4m3")
    ga = wg_.T @ tab_
    ub = wu_.T @ tab_
    h = gelu(ga) * ub
    h_ = mxq(h, 0, "e4m3")
    wd4_ = unpack_weight(wd4_words, wd4_scales, "e2m1")
    wd8_ = unpack_weight(wd8_words, wd8_scales, "e4m3")
    y = wd4_.T @ h_ + wd8_.T @ h_
    return f64(res) + y

@@ -1,0 +1,278 @@
+from contextlib import ExitStack
+
+import concourse.mybir as mybir
+
+K, R, N, T, J = 512, 1024, 512, 2048, 1024
+FLOPS = 2 * K * R * J * 2 + 2 * R * N * J * 2
+
+F32 = mybir.dt.float32
+BF16 = mybir.dt.bfloat16
+I32 = mybir.dt.int32
+U32 = mybir.dt.uint32
+U16 = mybir.dt.uint16
+U8 = mybir.dt.uint8
+FP8X4 = mybir.dt.float8_e4m3fn_x4
+FP4X4 = mybir.dt.float4_e2m1fn_x4
+GELU = mybir.ActivationFunctionType.Gelu_apprx_tanh
+MULT = mybir.AluOpType.mult
+ADD = mybir.AluOpType.add
+
+P = 128
+PACK = 4
+PASS = P * PACK
+HALVES = R // PASS
+JH = 512
+JT = 128
+GATHER = 256
+WU_CHUNK = 256
+WG_ROW = 4
+WD8_ROW = 4
+CFG = {"mts":"v","mwds":"v","mwgs":"v","ts":"aaaa","wgs":"ssaa","wd4s":"gggg","wd8s":"ssss","vb":4,"hb":3,"round":"aaag","add":"vvvvvvvv","loads":"mwgs wg0 mts mwarm mwds wgs tab ts offs warm wu0 wu1 wg1 wd4s wu2 wu3 wd4 wd8 wd8s res0 res1","gab":"ABCABCABCABCABCA","ubb":"DEFDEFDEFDEFDEFD","yb":"GHGHGHBC","prog":"S W0 G0 R0 R1 G1 Q0 g0 g1 g2 u0 g3 W1 u1 g4 R2 R3 u2 g5 Q1 u3 g6 G2 u4 q00 g7 u5 g8 u6 g9 G3 u7 g10 d00 d01 u8 q10 g11 u9 g12 u10 g13 d10 d11 u11 g14 u12 q20 g15 u13 d02 d12 d03 d13 u14 q31 u15 q32 d20 d21 d22 d23 d30 d31 d32 d33"}
+
+
+def tile_list_gmlpt_gelu_res_res_kernel(
+    tc, tab_words, tab_scales, wg_words, wg_scales, wu, wd4_words, wd4_scales, wd8_words, wd8_scales, res, offs, out
+):
+    nc = tc.nc
+    with ExitStack() as ctx:
+        keep = ctx.enter_context(tc.tile_pool(name="keep", bufs=1))
+        ring = ctx.enter_context(tc.tile_pool(name="ring", bufs=2))
+        psum = ctx.enter_context(tc.psum_pool(name="psum", bufs=1))
+
+        offsets = keep.tile([P, J // 16], U16, name="offsets")
+        tab_w = keep.tile([P, T], U32, name="tab_w", align_bytes=64)
+        tab_s = keep.tile([P, T], U8, name="tab_s", align_bytes=64)
+        wg_raw = keep.tile([P, HALVES, PASS], I32, name="wg_raw", align_bytes=64)
+        wgs_raw = keep.tile([P, PASS], U8, name="wgs_raw", align_bytes=64)
+        wg_w = keep.tile([P, HALVES, PACK, P], I32, name="wg_w", align_bytes=64)
+        wg_s = keep.tile([P, PACK, P], U8, name="wg_s", align_bytes=64)
+        wu_raw = [keep.tile([P, PACK, WU_CHUNK], F32, name="wu_raw%d" % c, align_bytes=64) for c in range(R // WU_CHUNK)]
+        wu_bf = [keep.tile([P, PACK, P, PACK], BF16, name="wu_bf%d" % b, align_bytes=64) for b in range(HALVES)]
+        wu_w = keep.tile([P, HALVES, PASS], U32, name="wu_w", align_bytes=64)
+        wu_s = keep.tile([P, HALVES, PASS], U8, name="wu_s", align_bytes=64)
+        wd4_w = keep.tile([P, HALVES, 2 * N], U8, name="wd4_w", align_bytes=64)
+        wd8_w = keep.tile([P, HALVES, N], U32, name="wd8_w", align_bytes=64)
+        wd_s = keep.tile([P, HALVES, N], U8, name="wd_s", align_bytes=64)
+        res_sb = [keep.tile([P, N // P, JH], F32, name="res%d" % jh, align_bytes=64) for jh in range(J // JH)]
+        v_w = {}
+        v_s = {}
+        warm = keep.tile([P, 16], F32, name="warm", align_bytes=64)
+
+        def load_wg(b):
+            src = wg_words[0].rearrange("p r i -> p (r i)")[:, b * PASS * 4 : (b + 1) * PASS * 4].bitcast(I32)
+            nc.sync.dma_start(wg_raw[:, b, :], src)
+
+        def load_wu(c):
+            src = wu.rearrange("(p i) r -> p i r", i=PACK)[:, :, c * WU_CHUNK : (c + 1) * WU_CHUNK]
+            nc.sync.dma_start(wu_raw[c][:], src)
+
+        eng = dict(s=nc.sync, a=nc.scalar, g=nc.gpsimd, v=nc.vector)
+
+        def load_ts(e):
+            for r in range(4):
+                src = tab_scales[0].rearrange("(q r) t -> r q t", r=4)[r].bitcast(I32)
+                eng[e[r]].dma_start(tab_s[r:P:32, :].bitcast(I32), src)
+
+        def load_wgs(e):
+            for q in range(4):
+                src = wg_scales[0][4 * q : 4 * q + 4, :].rearrange("r (b c) -> b r c", b=HALVES).bitcast(I32)
+                row = 32 * q + WG_ROW
+                eng[e[q]].dma_start(wgs_raw[row : row + 4 * HALVES, :].bitcast(I32), src)
+
+        def load_wds(e, scales, row):
+            for r in range(4):
+                src = scales.rearrange("a (q r) n -> r q a n", r=4)[r].bitcast(I32)
+                eng[e[r]].dma_start(wd_s[row + r : P : 32, :, :].bitcast(I32), src)
+
+        def load_res(jh):
+            src = res.rearrange("(c p) j -> p c j", p=P)[:, :, jh * JH : (jh + 1) * JH]
+            nc.sync.dma_start(res_sb[jh][:], src)
+
+        loads = dict(
+            mts=lambda: eng[CFG["mts"]].memset(tab_s[:].bitcast(I32), 0),
+            mwarm=lambda: nc.vector.memset(warm[:, 0:8], 0.0),
+            mwds=lambda: eng[CFG["mwds"]].memset(wd_s[:].rearrange("p a n -> p (a n)").bitcast(I32), 0),
+            mwgs=lambda: eng[CFG["mwgs"]].memset(wgs_raw[:].bitcast(I32), 0),
+            tab=lambda: nc.sync.dma_start(tab_w[:].bitcast(I32), tab_words[0].rearrange("p t i -> p (t i)").bitcast(I32)),
+            offs=lambda: nc.sync.dma_start(offsets[:], offs),
+            ts=lambda: load_ts(CFG["ts"]),
+            wgs=lambda: load_wgs(CFG["wgs"]),
+            wd4s=lambda: load_wds(CFG["wd4s"], wd4_scales, 0),
+            wd8s=lambda: load_wds(CFG["wd8s"], wd8_scales, WD8_ROW),
+            warm=lambda: nc.scalar.activation(warm[:, 8:16], warm[:, 0:8], GELU),
+            wg0=lambda: load_wg(0),
+            wg1=lambda: load_wg(1),
+            wu0=lambda: load_wu(0),
+            wu1=lambda: load_wu(1),
+            wu2=lambda: load_wu(2),
+            wu3=lambda: load_wu(3),
+            wd4=lambda: nc.sync.dma_start(wd4_w[:].bitcast(I32), wd4_words.rearrange("a p c -> p a c").bitcast(I32)),
+            wd8=lambda: nc.sync.dma_start(wd8_w[:].bitcast(I32), wd8_words.rearrange("a p n i -> p a (n i)").bitcast(I32)),
+            res0=lambda: load_res(0),
+            res1=lambda: load_res(1),
+        )
+        for name in CFG["loads"].split():
+            loads[name]()
+
+        def gather(s):
+            cols = offsets[:, s * GATHER // 16 : (s + 1) * GATHER // 16]
+            v_w[s] = ring.tile([P, GATHER], U32, name="v_w", bufs=CFG["vb"], align_bytes=64)
+            v_s[s] = ring.tile([P, GATHER], U8, name="v_s", bufs=CFG["vb"], align_bytes=64)
+            nc.vector.tensor_copy(v_w[s][:], tab_w[:].indirect(cols))
+            nc.vector.tensor_copy(v_s[s][:], tab_s[:].indirect(cols))
+
+        def permute_wg_words(b):
+            nc.vector.tensor_copy(
+                wg_w[:, b, :, :].rearrange("p t m -> p m t"), wg_raw[:, b, :].rearrange("p (m t) -> p m t", t=PACK)
+            )
+
+        def permute_wg_scales():
+            nc.vector.tensor_copy(
+                wg_s[:].rearrange("p t m -> p m t"), wgs_raw[:].rearrange("p (m t) -> p m t", t=PACK)
+            )
+
+        def round_wu(c):
+            b, part = divmod(c, PASS // WU_CHUNK)
+            ms = WU_CHUNK // PACK
+            dst = wu_bf[b][:, :, part * ms : (part + 1) * ms, :]
+            if CFG["round"][c] == "g":
+                src = wu_raw[c][:].rearrange("p i (m t) -> p m t i", t=PACK)
+                nc.gpsimd.tensor_scalar(dst.rearrange("p t m i -> p m t i"), src, 1.0, 0.0, MULT, ADD)
+            else:
+                src = wu_raw[c][:].rearrange("p i (m t) -> p m i t", t=PACK)
+                nc.scalar.copy(dst.rearrange("p t m i -> p m i t"), src)
+
+        def quantize_wu(b):
+            nc.vector.quantize_mx(
+                out=wu_w[:, b, :].bitcast(FP8X4),
+                scales=wu_s[:, b, :],
+                in_=wu_bf[b][:].rearrange("p t m i -> p (t m i)"),
+            )
+
+        def table_cols(jt):
+            s, at = divmod(jt * JT, GATHER)
+            return v_w[s][:, at : at + JT].bitcast(FP8X4), v_s[s][:, at : at + JT]
+
+        gates = {}
+
+        def gate(u):
+            jt, b = units[u]
+            words, scales = table_cols(jt)
+            bank = psum.tile([P, PACK, JT], F32, name="ga", tag=CFG["gab"][u])
+            for t in range(PACK):
+                nc.tensor.matmul_mx(
+                    out=bank[:, t, :],
+                    lhsT=wg_w[:, b, t, :].bitcast(FP8X4),
+                    lhsT_scale=wg_s[WG_ROW + 4 * b : P, t, :],
+                    rhs=words,
+                    rhs_scale=scales,
+                    start=True,
+                    stop=True,
+                )
+            g = ring.tile([P, JT, PACK], F32, name="g", bufs=16)
+            nc.scalar.activation(g[:], bank[:].rearrange("p t j -> p j t"), GELU)
+            gates[u] = g
+
+        def up(u, h_bf):
+            jt, b = units[u]
+            words, scales = table_cols(jt)
+            bank = psum.tile([P, PACK, JT], F32, name="ub", tag=CFG["ubb"][u])
+            for t in range(PACK):
+                nc.tensor.matmul_mx(
+                    out=bank[:, t, :],
+                    lhsT=wu_w[:, b, t * P : (t + 1) * P].bitcast(FP8X4),
+                    lhsT_scale=wu_s[:, b, t * P : (t + 1) * P],
+                    rhs=words,
+                    rhs_scale=scales,
+                    start=True,
+                    stop=True,
+                )
+            at = jt * JT % JH
+            nc.vector.tensor_tensor(h_bf[:, at : at + JT, :], bank[:].rearrange("p t j -> p j t"), gates[u][:], MULT)
+
+        def new_h_codes():
+            h_w = ring.tile([P, JH], U32, name="h_w", align_bytes=64, bufs=4)
+            h_s = ring.tile([P, JH], U8, name="h_s", align_bytes=64, bufs=4)
+            return h_w, h_s
+
+        def quantize_h(h_bf, h_w, h_s, j0, j1):
+            nc.vector.quantize_mx(
+                out=h_w[:, j0:j1].bitcast(FP8X4),
+                scales=h_s[:, j0:j1],
+                in_=h_bf[:, j0:j1, :].rearrange("p j t -> p (j t)"),
+            )
+
+        sums = {}
+
+        def down(grp, nt, h_w, h_s):
+            jh, b = divmod(grp, HALVES)
+            if b == 0:
+                sums[nt] = psum.tile([P, JH], F32, name="y%d" % nt, tag=CFG["yb"][jh * 4 + nt])
+            cols = slice(nt * P, (nt + 1) * P)
+            nc.tensor.matmul_mx(
+                out=sums[nt][:],
+                lhsT=wd4_w[:, b, 2 * nt * P : 2 * (nt + 1) * P].bitcast(FP4X4),
+                lhsT_scale=wd_s[:, b, cols],
+                rhs=h_w[:].bitcast(FP8X4),
+                rhs_scale=h_s[:],
+                start=(b == 0),
+                stop=False,
+            )
+            nc.tensor.matmul_mx(
+                out=sums[nt][:],
+                lhsT=wd8_w[:, b, cols].bitcast(FP8X4),
+                lhsT_scale=wd_s[WD8_ROW:P, b, cols],
+                rhs=h_w[:].bitcast(FP8X4),
+                rhs_scale=h_s[:],
+                start=False,
+                stop=(b == HALVES - 1),
+            )
+            if b == HALVES - 1:
+                o = ring.tile([P, JH], F32, name="o", bufs=8)
+                if CFG["add"][jh * 4 + nt] == "g":
+                    y_sb = ring.tile([P, JH], F32, name="y_sb", bufs=4)
+                    nc.scalar.copy(y_sb[:], sums[nt][:])
+                    nc.gpsimd.tensor_tensor(o[:], y_sb[:], res_sb[jh][:, nt, :], ADD)
+                else:
+                    nc.vector.tensor_tensor(o[:], sums[nt][:], res_sb[jh][:, nt, :], ADD)
+                nc.sync.dma_start(out[cols, jh * JH : (jh + 1) * JH], o[:])
+
+        per_group = JH // JT
+        units = [(jh * per_group + i, b) for jh in range(J // JH) for b in range(HALVES) for i in range(per_group)]
+        h_tiles = {}
+        codes = {}
+
+        def do_up(u):
+            grp = u // per_group
+            if grp not in h_tiles:
+                h_tiles[grp] = ring.tile([P, JH, PACK], BF16, name="h_bf", align_bytes=64, bufs=CFG["hb"])
+            up(u, h_tiles[grp])
+
+        def do_q(grp, part):
+            if grp not in codes:
+                codes[grp] = new_h_codes()
+            j0, j1 = [(0, JH), (0, JH // 2), (JH // 2, JH)][part]
+            quantize_h(h_tiles[grp], *codes[grp], j0, j1)
+
+        for w in CFG["prog"].split():
+            k, a = w[0], w[1:]
+            if k == "G":
+                gather(int(a))
+            elif k == "S":
+                permute_wg_scales()
+            elif k == "W":
+                permute_wg_words(int(a))
+            elif k == "R":
+                round_wu(int(a))
+            elif k == "Q":
+                quantize_wu(int(a))
+            elif k == "g":
+                gate(int(a))
+            elif k == "u":
+                do_up(int(a))
+            elif k == "q":
+                do_q(int(a[0]), int(a[1]))
+            elif k == "d":
+                down(int(a[0]), int(a[1]), *codes[int(a[0])])
+            elif k == "L":
+                loads[a]()

@@ -27,7 +27,7 @@ GATHER = 256
 WU_CHUNK = 256
 WG_ROW = 4
 WD8_ROW = 4
-CFG = {"mts":"v","mwds":"v","mwgs":"v","ts":"aaaa","wgs":"ssaa","wd4s":"gggg","wd8s":"ssss","vb":4,"hb":3,"round":"aaag","add":"vvvvvvvv","loads":"mwgs wg0 mts mwarm mwds wgs tab ts offs warm wu0 wu1 wg1 wd4s wu2 wu3 wd4 wd8 wd8s res0 res1","gab":"ABCABCABCABCABCA","ubb":"DEFDEFDEFDEFDEFD","yb":"GHGHGHBC","prog":"S W0 G0 R0 R1 G1 Q0 g0 g1 g2 u0 g3 W1 u1 g4 R2 R3 u2 g5 Q1 u3 g6 G2 u4 q00 g7 u5 g8 u6 g9 G3 u7 g10 d00 d01 u8 q10 g11 u9 g12 u10 g13 d10 d11 u11 g14 u12 q20 g15 u13 d02 d12 d03 d13 u14 q31 u15 q32 d20 d21 d22 d23 d30 d31 d32 d33"}
+CFG = {"mts":"v","mwds":"v","mwgs":"v","ts":"aaaa","wgs":"ssaa","wd4s":"gggg","wd8s":"ssss","vb":4,"hb":3,"round":"avaa","add":"vvvvvvvw","loads":"mwgs wg0 mts mwarm mwds wgs tab ts offs warm wu0 wu1 wg1 wd4s wu2 wu3 wd4 wd8 wd8s res0 res1","gab":"ABCABCABCABCABCA","ubb":"DEFDEFDEFDEFDEFD","yb":"GHGHGHBC","prog":"S W0 G0 G1 R0 R1 Q0 g0 g1 G2 G3 u0 W1 R2 R3 g2 u1 g3 u2 Q1 g4 u3 g5 u4 q00 g6 u5 g7 u6 g8 d00 u7 g9 d01 u8 q10 g10 u9 g11 u10 g12 d10 u11 g13 d11 u12 q20 g14 d02 d12 u13 g15 d03 d13 u14 q31 u15 q32 d20 d21 d22 d23 d30 d31 d32 d33","vt":["vt0","vt1","vt2","vt3"],"wide":1,"vs":["vs0","vs1","vs2","vs3"]}
 
 
 def tile_list_gmlpt_gelu_res_res_kernel(
@@ -47,7 +47,7 @@ def tile_list_gmlpt_gelu_res_res_kernel(
         wg_w = keep.tile([P, HALVES, PACK, P], I32, name="wg_w", align_bytes=64)
         wg_s = keep.tile([P, PACK, P], U8, name="wg_s", align_bytes=64)
         wu_raw = [keep.tile([P, PACK, WU_CHUNK], F32, name="wu_raw%d" % c, align_bytes=64) for c in range(R // WU_CHUNK)]
-        wu_bf = [keep.tile([P, PACK, P, PACK], BF16, name="wu_bf%d" % b, align_bytes=64) for b in range(HALVES)]
+        wu_bf = [keep.tile([P, PACK, P, PACK], BF16, name="wu_bf%d" % b, tag="wu_bf%d" % b, align_bytes=64) for b in range(HALVES)]
         wu_w = keep.tile([P, HALVES, PASS], U32, name="wu_w", align_bytes=64)
         wu_s = keep.tile([P, HALVES, PASS], U8, name="wu_s", align_bytes=64)
         wd4_w = keep.tile([P, HALVES, 2 * N], U8, name="wd4_w", align_bytes=64)
@@ -116,10 +116,10 @@ def tile_list_gmlpt_gelu_res_res_kernel(
 
         def gather(s):
             cols = offsets[:, s * GATHER // 16 : (s + 1) * GATHER // 16]
-            v_w[s] = ring.tile([P, GATHER], U32, name="v_w", bufs=CFG["vb"], align_bytes=64)
-            v_s[s] = ring.tile([P, GATHER], U8, name="v_s", bufs=CFG["vb"], align_bytes=64)
-            nc.vector.tensor_copy(v_w[s][:], tab_w[:].indirect(cols))
-            nc.vector.tensor_copy(v_s[s][:], tab_s[:].indirect(cols))
+            v_w[s] = keep.tile([P, GATHER], U32, name="v_w%d" % s, tag=CFG["vt"][s], align_bytes=64)[:]
+            v_s[s] = keep.tile([P, GATHER], U8, name="v_s%d" % s, tag=CFG["vs"][s], align_bytes=64)[:]
+            nc.vector.tensor_copy(v_w[s], tab_w[:].indirect(cols))
+            nc.vector.tensor_copy(v_s[s], tab_s[:].indirect(cols))
 
         def permute_wg_words(b):
             nc.vector.tensor_copy(
@@ -128,7 +128,7 @@ def tile_list_gmlpt_gelu_res_res_kernel(
 
         def permute_wg_scales():
             nc.vector.tensor_copy(
-                wg_s[:].rearrange("p t m -> p m t"), wgs_raw[:].rearrange("p (m t) -> p m t", t=PACK)
+                wg_s[:], wgs_raw[:].rearrange("p (m t) -> p t m", t=PACK)
             )
 
         def round_wu(c):
@@ -138,9 +138,12 @@ def tile_list_gmlpt_gelu_res_res_kernel(
             if CFG["round"][c] == "g":
                 src = wu_raw[c][:].rearrange("p i (m t) -> p m t i", t=PACK)
                 nc.gpsimd.tensor_scalar(dst.rearrange("p t m i -> p m t i"), src, 1.0, 0.0, MULT, ADD)
+            elif CFG["round"][c] == "v":
+                src = wu_raw[c][:].rearrange("p i (m t) -> p m t i", t=PACK)
+                nc.vector.tensor_copy(dst.rearrange("p t m i -> p m t i"), src)
             else:
-                src = wu_raw[c][:].rearrange("p i (m t) -> p m i t", t=PACK)
-                nc.scalar.copy(dst.rearrange("p t m i -> p m i t"), src)
+                src = wu_raw[c][:].rearrange("p i (m t) -> p m t i", t=PACK)
+                nc.scalar.copy(dst.rearrange("p t m i -> p m t i"), src)
 
         def quantize_wu(b):
             nc.vector.quantize_mx(
@@ -154,6 +157,24 @@ def tile_list_gmlpt_gelu_res_res_kernel(
             return v_w[s][:, at : at + JT].bitcast(FP8X4), v_s[s][:, at : at + JT]
 
         gates = {}
+
+        def gate_wide(u):
+            jt, b = units[u]
+            s, tp = divmod(jt, 2)
+            bank = psum.tile([P, 2, GATHER], F32, name="ga", tag=CFG["gab"][u])
+            for e in range(2):
+                nc.tensor.matmul_mx(
+                    out=bank[:, e, :],
+                    lhsT=wg_w[:, b, 2 * tp + e, :].bitcast(FP8X4),
+                    lhsT_scale=wg_s[WG_ROW + 4 * b : P, 2 * tp + e, :],
+                    rhs=v_w[s].bitcast(FP8X4),
+                    rhs_scale=v_s[s],
+                    start=True,
+                    stop=True,
+                )
+            if tp == 0:
+                gates[u // 2] = keep.tile([P, 2, GATHER, 2], F32, name="g%d" % (u // 2), tag="g%d" % (u // 2), align_bytes=64)
+            nc.scalar.activation(gates[u // 2][:, tp, :, :], bank[:].rearrange("p e j -> p j e"), GELU)
 
         def gate(u):
             jt, b = units[u]
@@ -188,7 +209,15 @@ def tile_list_gmlpt_gelu_res_res_kernel(
                     stop=True,
                 )
             at = jt * JT % JH
-            nc.vector.tensor_tensor(h_bf[:, at : at + JT, :], bank[:].rearrange("p t j -> p j t"), gates[u][:], MULT)
+            if CFG["wide"]:
+                nc.vector.tensor_tensor(
+                    h_bf[:, at : at + JT, :].rearrange("p j (tp e) -> p j tp e", e=2),
+                    bank[:].rearrange("p (tp e) j -> p j tp e", e=2),
+                    gates[u // 2][:, :, u % 2 * JT : (u % 2 + 1) * JT, :].rearrange("p tp j e -> p j tp e"),
+                    MULT,
+                )
+            else:
+                nc.vector.tensor_tensor(h_bf[:, at : at + JT, :], bank[:].rearrange("p t j -> p j t"), gates[u][:], MULT)
 
         def new_h_codes():
             h_w = ring.tile([P, JH], U32, name="h_w", align_bytes=64, bufs=4)
@@ -204,38 +233,47 @@ def tile_list_gmlpt_gelu_res_res_kernel(
 
         sums = {}
 
-        def down(grp, nt, h_w, h_s):
+        def down(grp, nt, h_w, h_s, j0=0, j1=JH):
             jh, b = divmod(grp, HALVES)
             if b == 0:
                 sums[nt] = psum.tile([P, JH], F32, name="y%d" % nt, tag=CFG["yb"][jh * 4 + nt])
             cols = slice(nt * P, (nt + 1) * P)
+            closing = b == HALVES - 1 and j1 == JH
             nc.tensor.matmul_mx(
-                out=sums[nt][:],
+                out=sums[nt][:, j0:j1],
                 lhsT=wd4_w[:, b, 2 * nt * P : 2 * (nt + 1) * P].bitcast(FP4X4),
                 lhsT_scale=wd_s[:, b, cols],
-                rhs=h_w[:].bitcast(FP8X4),
-                rhs_scale=h_s[:],
+                rhs=h_w[:, j0:j1].bitcast(FP8X4),
+                rhs_scale=h_s[:, j0:j1],
                 start=(b == 0),
                 stop=False,
             )
             nc.tensor.matmul_mx(
-                out=sums[nt][:],
+                out=sums[nt][:, j0:j1],
                 lhsT=wd8_w[:, b, cols].bitcast(FP8X4),
                 lhsT_scale=wd_s[WD8_ROW:P, b, cols],
-                rhs=h_w[:].bitcast(FP8X4),
-                rhs_scale=h_s[:],
+                rhs=h_w[:, j0:j1].bitcast(FP8X4),
+                rhs_scale=h_s[:, j0:j1],
                 start=False,
-                stop=(b == HALVES - 1),
+                stop=closing,
             )
-            if b == HALVES - 1:
+            if closing:
                 o = ring.tile([P, JH], F32, name="o", bufs=8)
-                if CFG["add"][jh * 4 + nt] == "g":
+                how = CFG["add"][jh * 4 + nt]
+                if how == "g":
                     y_sb = ring.tile([P, JH], F32, name="y_sb", bufs=4)
                     nc.scalar.copy(y_sb[:], sums[nt][:])
-                    nc.gpsimd.tensor_tensor(o[:], y_sb[:], res_sb[jh][:, nt, :], ADD)
-                else:
-                    nc.vector.tensor_tensor(o[:], sums[nt][:], res_sb[jh][:, nt, :], ADD)
-                nc.sync.dma_start(out[cols, jh * JH : (jh + 1) * JH], o[:])
+                width = JH if how == "v" else JH // 2
+                for at in range(0, JH, width):
+                    piece = slice(at, at + width)
+                    if how == "g":
+                        nc.gpsimd.tensor_tensor(o[:, piece], y_sb[:, piece], res_sb[jh][:, nt, piece], ADD)
+                    else:
+                        nc.vector.tensor_tensor(o[:, piece], sums[nt][:, piece], res_sb[jh][:, nt, piece], ADD)
+                    if how == "w":
+                        nc.sync.dma_start(out[cols, jh * JH + at : jh * JH + at + width], o[:, piece])
+                if how != "w":
+                    nc.sync.dma_start(out[cols, jh * JH : (jh + 1) * JH], o[:])
 
         per_group = JH // JT
         units = [(jh * per_group + i, b) for jh in range(J // JH) for b in range(HALVES) for i in range(per_group)]
@@ -245,13 +283,13 @@ def tile_list_gmlpt_gelu_res_res_kernel(
         def do_up(u):
             grp = u // per_group
             if grp not in h_tiles:
-                h_tiles[grp] = ring.tile([P, JH, PACK], BF16, name="h_bf", align_bytes=64, bufs=CFG["hb"])
+                h_tiles[grp] = keep.tile([P, JH, PACK], BF16, name="h%d" % grp, tag="h%d" % grp, align_bytes=64)
             up(u, h_tiles[grp])
 
         def do_q(grp, part):
             if grp not in codes:
                 codes[grp] = new_h_codes()
-            j0, j1 = [(0, JH), (0, JH // 2), (JH // 2, JH)][part]
+            j0, j1 = [(0, JH), (0, JH // 2), (JH // 2, JH), (JH // 2, 3 * JT), (3 * JT, JH)][part]
             quantize_h(h_tiles[grp], *codes[grp], j0, j1)
 
         for w in CFG["prog"].split():
@@ -267,12 +305,15 @@ def tile_list_gmlpt_gelu_res_res_kernel(
             elif k == "Q":
                 quantize_wu(int(a))
             elif k == "g":
-                gate(int(a))
+                (gate_wide if CFG["wide"] else gate)(int(a))
             elif k == "u":
                 do_up(int(a))
             elif k == "q":
                 do_q(int(a[0]), int(a[1]))
             elif k == "d":
                 down(int(a[0]), int(a[1]), *codes[int(a[0])])
+            elif k == "e":
+                for nt in range(N // P):
+                    down(3, nt, *codes[3], int(a) * JT, (int(a) + 1) * JT)
             elif k == "L":
                 loads[a]()

@@ -27,7 +27,7 @@ GATHER = 256
 WU_CHUNK = 256
 WG_ROW = 4
 WD8_ROW = 4
-CFG = {"mts":"v","mwds":"v","mwgs":"v","ts":"aaaa","wgs":"ssaa","wd4s":"gggg","wd8s":"ssss","vb":4,"hb":3,"round":"avaa","add":"vvvvvvvw","loads":"mwgs wg0 mts mwarm mwds wgs tab ts offs warm wu0 wu1 wg1 wd4s wu2 wu3 wd4 wd8 wd8s res0 res1","gab":"ABCABCABCABCABCA","ubb":"DEFDEFDEFDEFDEFD","yb":"GHGHGHBC","prog":"S W0 G0 G1 R0 R1 Q0 g0 g1 G2 G3 u0 W1 R2 R3 g2 u1 g3 u2 Q1 g4 u3 g5 u4 q00 g6 u5 g7 u6 g8 d00 u7 g9 d01 u8 q10 g10 u9 g11 u10 g12 d10 u11 g13 d11 u12 q20 g14 d02 d12 u13 g15 d03 d13 u14 q31 u15 q32 d20 d21 d22 d23 d30 d31 d32 d33","vt":["vt0","vt1","vt2","vt3"],"wide":1,"vs":["vs0","vs1","vs2","vs3"]}
+CFG = {"mts":"v","mwds":"v","mwgs":"v","ts":"aaaa","wgs":"ssaa","wd4s":"aaaa","wd8s":"ssss","vb":4,"hb":3,"round":"avva","add":"vvvvvvvw","loads":"mwgs wg0 mts mwarm mwds wgs tab ts offs warm wu0 wu1 wg1 wd4s wu2 wu3 wd4 wd8 wd8s res0 res1","gab":"ABCABCABCABCABCA","ubb":"DEFDEFDEFDEFDEFD","yb":"GHABCDGH","prog":"S W0 G0 G1 R0 R1 Q0 W1 R2 R3 Q1 G2 g0 g1 g2 g3 u0 g4 u1 g5 u2 g6 u3 G3 g7 u4 q00 g8 u5 g9 u6 g10 u7 g11 u8 q10 g12 u9 g13 u10 g14 u11 g15 u12 q20 u13 u14 q31 u15 q32 d00 d01 d10 d11 d02 d12 d03 d13 d20 d21 d30 d31 d22 d32 d23 d33","vt":["vt0","vt1","vt2","wu_raw3"],"wide":1,"vs":["vs0","vs1","wu_raw1","wu_raw2"],"gt":["wu_raw0","wu_bf0","g2","g3","g4","g5","g6","g7"],"name":"L4 g3=3 ql1 b vvvvvvvw"}
 
 
 def tile_list_gmlpt_gelu_res_res_kernel(
@@ -46,7 +46,7 @@ def tile_list_gmlpt_gelu_res_res_kernel(
         wgs_raw = keep.tile([P, PASS], U8, name="wgs_raw", align_bytes=64)
         wg_w = keep.tile([P, HALVES, PACK, P], I32, name="wg_w", align_bytes=64)
         wg_s = keep.tile([P, PACK, P], U8, name="wg_s", align_bytes=64)
-        wu_raw = [keep.tile([P, PACK, WU_CHUNK], F32, name="wu_raw%d" % c, align_bytes=64) for c in range(R // WU_CHUNK)]
+        wu_raw = [keep.tile([P, PACK, WU_CHUNK], F32, name="wu_raw%d" % c, tag="wu_raw%d" % c, align_bytes=64) for c in range(R // WU_CHUNK)]
         wu_bf = [keep.tile([P, PACK, P, PACK], BF16, name="wu_bf%d" % b, tag="wu_bf%d" % b, align_bytes=64) for b in range(HALVES)]
         wu_w = keep.tile([P, HALVES, PASS], U32, name="wu_w", align_bytes=64)
         wu_s = keep.tile([P, HALVES, PASS], U8, name="wu_s", align_bytes=64)
@@ -173,7 +173,7 @@ def tile_list_gmlpt_gelu_res_res_kernel(
                     stop=True,
                 )
             if tp == 0:
-                gates[u // 2] = keep.tile([P, 2, GATHER, 2], F32, name="g%d" % (u // 2), tag="g%d" % (u // 2), align_bytes=64)
+                gates[u // 2] = keep.tile([P, 2, GATHER, 2], F32, name="g%d" % (u // 2), tag=CFG["gt"][u // 2], align_bytes=64)
             nc.scalar.activation(gates[u // 2][:, tp, :, :], bank[:].rearrange("p e j -> p j e"), GELU)
 
         def gate(u):

@@ -21,13 +21,24 @@ P = 128
 PACK = 4
 PASS = P * PACK
 HALVES = R // PASS
-JH = 512
-JT = 128
-GATHER = 256
+QUADRANT = 32
+BANKS = 8
+SLICE = 256
+UNIT = 128
+SPAN = 512
 WU_CHUNK = 256
 WG_ROW = 4
 WD8_ROW = 4
-CFG = {"mts":"v","mwds":"v","mwgs":"v","ts":"aaaa","wgs":"ssaa","wd4s":"aaaa","wd8s":"ssss","vb":4,"hb":3,"round":"avva","add":"vvvvvvvw","loads":"mwgs wg0 mts mwarm mwds wgs tab ts offs warm wu0 wu1 wg1 wd4s wu2 wu3 wd4 wd8 wd8s res0 res1","gab":"ABCABCABCABCABCA","ubb":"DEFDEFDEFDEFDEFD","yb":"GHABCDGH","prog":"S W0 G0 G1 R0 R1 Q0 W1 R2 R3 Q1 G2 g0 g1 g2 g3 u0 g4 u1 g5 u2 g6 u3 G3 g7 u4 q00 g8 u5 g9 u6 g10 u7 g11 u8 q10 g12 u9 g13 u10 g14 u11 g15 u12 q20 u13 u14 q31 u15 q32 d00 d01 d10 d11 d02 d12 d03 d13 d20 d21 d30 d31 d22 d32 d23 d33","vt":["vt0","vt1","vt2","wu_raw3"],"wide":1,"vs":["vs0","vs1","wu_raw1","wu_raw2"],"gt":["wu_raw0","wu_bf0","g2","g3","g4","g5","g6","g7"],"name":"L4 g3=3 ql1 b vvvvvvvw"}
+
+UNITS_PER_GROUP = SPAN // UNIT
+UNITS = [
+    (span * UNITS_PER_GROUP + i, b) for span in range(J // SPAN) for b in range(HALVES) for i in range(UNITS_PER_GROUP)
+]
+GROUPS = len(UNITS) // UNITS_PER_GROUP
+GATE_LEAD = 3
+QUANTIZE_LAG = 2
+DOWN_AFTER_UNIT = {9: (0, 0), 10: (0, 1), 11: (0, 2), 12: (1, 0), 13: (0, 3)}
+DOWN_AT_END = [(1, 1), (1, 2), (2, 0), (2, 1), (1, 3), (2, 2), (3, 0), (3, 1), (3, 2), (2, 3), (3, 3)]
 
 
 def tile_list_gmlpt_gelu_res_res_kernel(
@@ -36,114 +47,92 @@ def tile_list_gmlpt_gelu_res_res_kernel(
     nc = tc.nc
     with ExitStack() as ctx:
         keep = ctx.enter_context(tc.tile_pool(name="keep", bufs=1))
-        ring = ctx.enter_context(tc.tile_pool(name="ring", bufs=2))
         psum = ctx.enter_context(tc.psum_pool(name="psum", bufs=1))
 
+        def sbuf(name, shape, dtype, tag=None):
+            return keep.tile(shape, dtype, name=name, tag=tag or name, align_bytes=64)
+
         offsets = keep.tile([P, J // 16], U16, name="offsets")
-        tab_w = keep.tile([P, T], U32, name="tab_w", align_bytes=64)
-        tab_s = keep.tile([P, T], U8, name="tab_s", align_bytes=64)
-        wg_raw = keep.tile([P, HALVES, PASS], I32, name="wg_raw", align_bytes=64)
-        wgs_raw = keep.tile([P, PASS], U8, name="wgs_raw", align_bytes=64)
-        wg_w = keep.tile([P, HALVES, PACK, P], I32, name="wg_w", align_bytes=64)
-        wg_s = keep.tile([P, PACK, P], U8, name="wg_s", align_bytes=64)
-        wu_raw = [keep.tile([P, PACK, WU_CHUNK], F32, name="wu_raw%d" % c, tag="wu_raw%d" % c, align_bytes=64) for c in range(R // WU_CHUNK)]
-        wu_bf = [keep.tile([P, PACK, P, PACK], BF16, name="wu_bf%d" % b, tag="wu_bf%d" % b, align_bytes=64) for b in range(HALVES)]
-        wu_w = keep.tile([P, HALVES, PASS], U32, name="wu_w", align_bytes=64)
-        wu_s = keep.tile([P, HALVES, PASS], U8, name="wu_s", align_bytes=64)
-        wd4_w = keep.tile([P, HALVES, 2 * N], U8, name="wd4_w", align_bytes=64)
-        wd8_w = keep.tile([P, HALVES, N], U32, name="wd8_w", align_bytes=64)
-        wd_s = keep.tile([P, HALVES, N], U8, name="wd_s", align_bytes=64)
-        res_sb = [keep.tile([P, N // P, JH], F32, name="res%d" % jh, align_bytes=64) for jh in range(J // JH)]
-        v_w = {}
-        v_s = {}
-        warm = keep.tile([P, 16], F32, name="warm", align_bytes=64)
+        tab_w = sbuf("tab_w", [P, T], U32)
+        tab_s = sbuf("tab_s", [P, T], U8)
+        wg_w_raw = sbuf("wg_w_raw", [P, HALVES, PASS], I32)
+        wg_s_raw = sbuf("wg_s_raw", [P, PASS], U8)
+        wg_w = sbuf("wg_w", [P, HALVES, PACK, P], I32)
+        wg_s = sbuf("wg_s", [P, PACK, P], U8)
+        wu_raw = [sbuf("wu_raw%d" % c, [P, PACK, WU_CHUNK], F32) for c in range(R // WU_CHUNK)]
+        wu_bf = [sbuf("wu_bf%d" % b, [P, PACK, P, PACK], BF16) for b in range(HALVES)]
+        wu_w = sbuf("wu_w", [P, HALVES, PASS], U32)
+        wu_s = sbuf("wu_s", [P, HALVES, PASS], U8)
+        wd4_w = sbuf("wd4_w", [P, HALVES, 2 * N], U8)
+        wd8_w = sbuf("wd8_w", [P, HALVES, N], U32)
+        wd_s = sbuf("wd_s", [P, HALVES, N], U8)
+        res_sb = [sbuf("res%d" % span, [P, N // P, SPAN], F32) for span in range(J // SPAN)]
+        v_w = [sbuf("v_w%d" % s, [P, SLICE], U32) for s in range(J // SLICE)]
+        v_s = [sbuf("v_s%d" % s, [P, SLICE], U8) for s in range(J // SLICE)]
+        h_bf = [sbuf("h_bf%d" % group, [P, SPAN, PACK], BF16) for group in range(GROUPS)]
+        h_w = [sbuf("h_w%d" % group, [P, SPAN], U32) for group in range(GROUPS)]
+        h_s = [sbuf("h_s%d" % group, [P, SPAN], U8) for group in range(GROUPS)]
+        warm = sbuf("warm", [P, 2, 8], F32)
 
         def load_wg(b):
-            src = wg_words[0].rearrange("p r i -> p (r i)")[:, b * PASS * 4 : (b + 1) * PASS * 4].bitcast(I32)
-            nc.sync.dma_start(wg_raw[:, b, :], src)
+            words = wg_words[0].rearrange("p r i -> p (r i)").bitcast(I32)
+            nc.sync.dma_start(wg_w_raw[:, b, :], words[:, b * PASS : (b + 1) * PASS])
 
         def load_wu(c):
-            src = wu.rearrange("(p i) r -> p i r", i=PACK)[:, :, c * WU_CHUNK : (c + 1) * WU_CHUNK]
-            nc.sync.dma_start(wu_raw[c][:], src)
+            rows = wu.rearrange("(p i) r -> p i r", i=PACK)
+            nc.sync.dma_start(wu_raw[c][:], rows[:, :, c * WU_CHUNK : (c + 1) * WU_CHUNK])
 
-        eng = dict(s=nc.sync, a=nc.scalar, g=nc.gpsimd, v=nc.vector)
-
-        def load_ts(e):
+        def load_wd_scales(engine, scales, row):
             for r in range(4):
-                src = tab_scales[0].rearrange("(q r) t -> r q t", r=4)[r].bitcast(I32)
-                eng[e[r]].dma_start(tab_s[r:P:32, :].bitcast(I32), src)
+                rows = scales.rearrange("a (q r) n -> r q a n", r=4)[r]
+                engine.dma_start(wd_s[row + r : P : QUADRANT, :, :].bitcast(I32), rows.bitcast(I32))
 
-        def load_wgs(e):
-            for q in range(4):
-                src = wg_scales[0][4 * q : 4 * q + 4, :].rearrange("r (b c) -> b r c", b=HALVES).bitcast(I32)
-                row = 32 * q + WG_ROW
-                eng[e[q]].dma_start(wgs_raw[row : row + 4 * HALVES, :].bitcast(I32), src)
-
-        def load_wds(e, scales, row):
-            for r in range(4):
-                src = scales.rearrange("a (q r) n -> r q a n", r=4)[r].bitcast(I32)
-                eng[e[r]].dma_start(wd_s[row + r : P : 32, :, :].bitcast(I32), src)
-
-        def load_res(jh):
-            src = res.rearrange("(c p) j -> p c j", p=P)[:, :, jh * JH : (jh + 1) * JH]
-            nc.sync.dma_start(res_sb[jh][:], src)
-
-        loads = dict(
-            mts=lambda: eng[CFG["mts"]].memset(tab_s[:].bitcast(I32), 0),
-            mwarm=lambda: nc.vector.memset(warm[:, 0:8], 0.0),
-            mwds=lambda: eng[CFG["mwds"]].memset(wd_s[:].rearrange("p a n -> p (a n)").bitcast(I32), 0),
-            mwgs=lambda: eng[CFG["mwgs"]].memset(wgs_raw[:].bitcast(I32), 0),
-            tab=lambda: nc.sync.dma_start(tab_w[:].bitcast(I32), tab_words[0].rearrange("p t i -> p (t i)").bitcast(I32)),
-            offs=lambda: nc.sync.dma_start(offsets[:], offs),
-            ts=lambda: load_ts(CFG["ts"]),
-            wgs=lambda: load_wgs(CFG["wgs"]),
-            wd4s=lambda: load_wds(CFG["wd4s"], wd4_scales, 0),
-            wd8s=lambda: load_wds(CFG["wd8s"], wd8_scales, WD8_ROW),
-            warm=lambda: nc.scalar.activation(warm[:, 8:16], warm[:, 0:8], GELU),
-            wg0=lambda: load_wg(0),
-            wg1=lambda: load_wg(1),
-            wu0=lambda: load_wu(0),
-            wu1=lambda: load_wu(1),
-            wu2=lambda: load_wu(2),
-            wu3=lambda: load_wu(3),
-            wd4=lambda: nc.sync.dma_start(wd4_w[:].bitcast(I32), wd4_words.rearrange("a p c -> p a c").bitcast(I32)),
-            wd8=lambda: nc.sync.dma_start(wd8_w[:].bitcast(I32), wd8_words.rearrange("a p n i -> p a (n i)").bitcast(I32)),
-            res0=lambda: load_res(0),
-            res1=lambda: load_res(1),
-        )
-        for name in CFG["loads"].split():
-            loads[name]()
+        nc.vector.memset(wg_s_raw[:].bitcast(I32), 0)
+        load_wg(0)
+        nc.vector.memset(tab_s[:].bitcast(I32), 0)
+        nc.vector.memset(warm[:, 0, :], 0.0)
+        nc.vector.memset(wd_s[:].rearrange("p a n -> p (a n)").bitcast(I32), 0)
+        for q, engine in enumerate((nc.sync, nc.sync, nc.scalar, nc.scalar)):
+            rows = wg_scales[0][4 * q : 4 * q + 4, :].rearrange("r (b c) -> b r c", b=HALVES)
+            first = QUADRANT * q + WG_ROW
+            engine.dma_start(wg_s_raw[first : first + 4 * HALVES, :].bitcast(I32), rows.bitcast(I32))
+        nc.sync.dma_start(tab_w[:].bitcast(I32), tab_words[0].rearrange("p t i -> p (t i)").bitcast(I32))
+        for r in range(4):
+            rows = tab_scales[0].rearrange("(q r) t -> r q t", r=4)[r]
+            nc.scalar.dma_start(tab_s[r:P:QUADRANT, :].bitcast(I32), rows.bitcast(I32))
+        nc.sync.dma_start(offsets[:], offs)
+        nc.scalar.activation(warm[:, 1, :], warm[:, 0, :], GELU)
+        load_wu(0)
+        load_wu(1)
+        load_wg(1)
+        load_wd_scales(nc.scalar, wd4_scales, 0)
+        load_wu(2)
+        load_wu(3)
+        nc.sync.dma_start(wd4_w[:].bitcast(I32), wd4_words.rearrange("a p c -> p a c").bitcast(I32))
+        nc.sync.dma_start(wd8_w[:].bitcast(I32), wd8_words.rearrange("a p n i -> p a (n i)").bitcast(I32))
+        load_wd_scales(nc.sync, wd8_scales, WD8_ROW)
+        for span in range(J // SPAN):
+            rows = res.rearrange("(c p) j -> p c j", p=P)
+            nc.sync.dma_start(res_sb[span][:], rows[:, :, span * SPAN : (span + 1) * SPAN])
 
         def gather(s):
-            cols = offsets[:, s * GATHER // 16 : (s + 1) * GATHER // 16]
-            v_w[s] = keep.tile([P, GATHER], U32, name="v_w%d" % s, tag=CFG["vt"][s], align_bytes=64)[:]
-            v_s[s] = keep.tile([P, GATHER], U8, name="v_s%d" % s, tag=CFG["vs"][s], align_bytes=64)[:]
-            nc.vector.tensor_copy(v_w[s], tab_w[:].indirect(cols))
-            nc.vector.tensor_copy(v_s[s], tab_s[:].indirect(cols))
+            entries = offsets[:, s * SLICE // 16 : (s + 1) * SLICE // 16]
+            nc.vector.tensor_copy(v_w[s][:], tab_w[:].indirect(entries))
+            nc.vector.tensor_copy(v_s[s][:], tab_s[:].indirect(entries))
 
-        def permute_wg_words(b):
-            nc.vector.tensor_copy(
-                wg_w[:, b, :, :].rearrange("p t m -> p m t"), wg_raw[:, b, :].rearrange("p (m t) -> p m t", t=PACK)
-            )
-
-        def permute_wg_scales():
-            nc.vector.tensor_copy(
-                wg_s[:], wgs_raw[:].rearrange("p (m t) -> p t m", t=PACK)
-            )
+        def reorder_wg_words(b):
+            src = wg_w_raw[:, b, :].rearrange("p (m t) -> p m t", t=PACK)
+            nc.vector.tensor_copy(wg_w[:, b, :, :].rearrange("p t m -> p m t"), src)
 
         def round_wu(c):
             b, part = divmod(c, PASS // WU_CHUNK)
-            ms = WU_CHUNK // PACK
-            dst = wu_bf[b][:, :, part * ms : (part + 1) * ms, :]
-            if CFG["round"][c] == "g":
-                src = wu_raw[c][:].rearrange("p i (m t) -> p m t i", t=PACK)
-                nc.gpsimd.tensor_scalar(dst.rearrange("p t m i -> p m t i"), src, 1.0, 0.0, MULT, ADD)
-            elif CFG["round"][c] == "v":
-                src = wu_raw[c][:].rearrange("p i (m t) -> p m t i", t=PACK)
-                nc.vector.tensor_copy(dst.rearrange("p t m i -> p m t i"), src)
+            count = WU_CHUNK // PACK
+            dst = wu_bf[b][:, :, part * count : (part + 1) * count, :].rearrange("p t m i -> p m t i")
+            src = wu_raw[c][:].rearrange("p i (m t) -> p m t i", t=PACK)
+            if c == len(wu_raw) - 1:
+                nc.vector.tensor_copy(dst, src)
             else:
-                src = wu_raw[c][:].rearrange("p i (m t) -> p m t i", t=PACK)
-                nc.scalar.copy(dst.rearrange("p t m i -> p m t i"), src)
+                nc.scalar.copy(dst, src)
 
         def quantize_wu(b):
             nc.vector.quantize_mx(
@@ -152,168 +141,127 @@ def tile_list_gmlpt_gelu_res_res_kernel(
                 in_=wu_bf[b][:].rearrange("p t m i -> p (t m i)"),
             )
 
-        def table_cols(jt):
-            s, at = divmod(jt * JT, GATHER)
-            return v_w[s][:, at : at + JT].bitcast(FP8X4), v_s[s][:, at : at + JT]
+        nc.vector.tensor_copy(wg_s[:], wg_s_raw[:].rearrange("p (m t) -> p t m", t=PACK))
+        reorder_wg_words(0)
+        for s in range(J // SLICE):
+            gather(s)
+        round_wu(0)
+        round_wu(1)
+        quantize_wu(0)
+        reorder_wg_words(1)
+        round_wu(2)
+        round_wu(3)
+        quantize_wu(1)
 
+        free_banks = ["bank%d" % i for i in range(BANKS)]
+
+        def take_bank():
+            bank = free_banks[0]
+            free_banks.remove(bank)
+            return bank
+
+        gate_tags = {0: "wu_raw1", 1: "wu_raw0"}
         gates = {}
 
-        def gate_wide(u):
-            jt, b = units[u]
-            s, tp = divmod(jt, 2)
-            bank = psum.tile([P, 2, GATHER], F32, name="ga", tag=CFG["gab"][u])
+        def gate(u):
+            tile_j, b = UNITS[u]
+            s, pair = divmod(tile_j, SLICE // UNIT)
+            bank = take_bank()
+            ga = psum.tile([P, 2, SLICE], F32, name="ga", tag=bank)
             for e in range(2):
                 nc.tensor.matmul_mx(
-                    out=bank[:, e, :],
-                    lhsT=wg_w[:, b, 2 * tp + e, :].bitcast(FP8X4),
-                    lhsT_scale=wg_s[WG_ROW + 4 * b : P, 2 * tp + e, :],
-                    rhs=v_w[s].bitcast(FP8X4),
-                    rhs_scale=v_s[s],
+                    out=ga[:, e, :],
+                    lhsT=wg_w[:, b, 2 * pair + e, :].bitcast(FP8X4),
+                    lhsT_scale=wg_s[WG_ROW + 4 * b : P, 2 * pair + e, :],
+                    rhs=v_w[s][:].bitcast(FP8X4),
+                    rhs_scale=v_s[s][:],
                     start=True,
                     stop=True,
                 )
-            if tp == 0:
-                gates[u // 2] = keep.tile([P, 2, GATHER, 2], F32, name="g%d" % (u // 2), tag=CFG["gt"][u // 2], align_bytes=64)
-            nc.scalar.activation(gates[u // 2][:, tp, :, :], bank[:].rearrange("p e j -> p j e"), GELU)
+            if pair == 0:
+                gates[u // 2] = sbuf("gate%d" % (u // 2), [P, 2, SLICE, 2], F32, gate_tags.get(u // 2))
+            nc.scalar.activation(gates[u // 2][:, pair, :, :], ga[:].rearrange("p e j -> p j e"), GELU)
+            free_banks.append(bank)
 
-        def gate(u):
-            jt, b = units[u]
-            words, scales = table_cols(jt)
-            bank = psum.tile([P, PACK, JT], F32, name="ga", tag=CFG["gab"][u])
+        def up(u):
+            tile_j, b = UNITS[u]
+            s, at = divmod(tile_j * UNIT, SLICE)
+            bank = take_bank()
+            ub = psum.tile([P, PACK, UNIT], F32, name="ub", tag=bank)
             for t in range(PACK):
                 nc.tensor.matmul_mx(
-                    out=bank[:, t, :],
-                    lhsT=wg_w[:, b, t, :].bitcast(FP8X4),
-                    lhsT_scale=wg_s[WG_ROW + 4 * b : P, t, :],
-                    rhs=words,
-                    rhs_scale=scales,
-                    start=True,
-                    stop=True,
-                )
-            g = ring.tile([P, JT, PACK], F32, name="g", bufs=16)
-            nc.scalar.activation(g[:], bank[:].rearrange("p t j -> p j t"), GELU)
-            gates[u] = g
-
-        def up(u, h_bf):
-            jt, b = units[u]
-            words, scales = table_cols(jt)
-            bank = psum.tile([P, PACK, JT], F32, name="ub", tag=CFG["ubb"][u])
-            for t in range(PACK):
-                nc.tensor.matmul_mx(
-                    out=bank[:, t, :],
+                    out=ub[:, t, :],
                     lhsT=wu_w[:, b, t * P : (t + 1) * P].bitcast(FP8X4),
                     lhsT_scale=wu_s[:, b, t * P : (t + 1) * P],
-                    rhs=words,
-                    rhs_scale=scales,
+                    rhs=v_w[s][:, at : at + UNIT].bitcast(FP8X4),
+                    rhs_scale=v_s[s][:, at : at + UNIT],
                     start=True,
                     stop=True,
                 )
-            at = jt * JT % JH
-            if CFG["wide"]:
-                nc.vector.tensor_tensor(
-                    h_bf[:, at : at + JT, :].rearrange("p j (tp e) -> p j tp e", e=2),
-                    bank[:].rearrange("p (tp e) j -> p j tp e", e=2),
-                    gates[u // 2][:, :, u % 2 * JT : (u % 2 + 1) * JT, :].rearrange("p tp j e -> p j tp e"),
-                    MULT,
-                )
-            else:
-                nc.vector.tensor_tensor(h_bf[:, at : at + JT, :], bank[:].rearrange("p t j -> p j t"), gates[u][:], MULT)
+            first = tile_j * UNIT % SPAN
+            nc.vector.tensor_tensor(
+                h_bf[u // UNITS_PER_GROUP][:, first : first + UNIT, :].rearrange("p j (pair e) -> p j pair e", e=2),
+                ub[:].rearrange("p (pair e) j -> p j pair e", e=2),
+                gates[u // 2][:, :, at : at + UNIT, :].rearrange("p pair j e -> p j pair e"),
+                MULT,
+            )
+            free_banks.append(bank)
 
-        def new_h_codes():
-            h_w = ring.tile([P, JH], U32, name="h_w", align_bytes=64, bufs=4)
-            h_s = ring.tile([P, JH], U8, name="h_s", align_bytes=64, bufs=4)
-            return h_w, h_s
-
-        def quantize_h(h_bf, h_w, h_s, j0, j1):
+        def quantize_h(group, j0, j1):
             nc.vector.quantize_mx(
-                out=h_w[:, j0:j1].bitcast(FP8X4),
-                scales=h_s[:, j0:j1],
-                in_=h_bf[:, j0:j1, :].rearrange("p j t -> p (j t)"),
+                out=h_w[group][:, j0:j1].bitcast(FP8X4),
+                scales=h_s[group][:, j0:j1],
+                in_=h_bf[group][:, j0:j1, :].rearrange("p j t -> p (j t)"),
             )
 
         sums = {}
 
-        def down(grp, nt, h_w, h_s, j0=0, j1=JH):
-            jh, b = divmod(grp, HALVES)
+        def down(group, tile_n):
+            span, b = divmod(group, HALVES)
             if b == 0:
-                sums[nt] = psum.tile([P, JH], F32, name="y%d" % nt, tag=CFG["yb"][jh * 4 + nt])
-            cols = slice(nt * P, (nt + 1) * P)
-            closing = b == HALVES - 1 and j1 == JH
+                bank = take_bank()
+                sums[tile_n] = (bank, psum.tile([P, SPAN], F32, name="y", tag=bank))
+            bank, y = sums[tile_n]
+            rows = slice(tile_n * P, (tile_n + 1) * P)
             nc.tensor.matmul_mx(
-                out=sums[nt][:, j0:j1],
-                lhsT=wd4_w[:, b, 2 * nt * P : 2 * (nt + 1) * P].bitcast(FP4X4),
-                lhsT_scale=wd_s[:, b, cols],
-                rhs=h_w[:, j0:j1].bitcast(FP8X4),
-                rhs_scale=h_s[:, j0:j1],
+                out=y[:],
+                lhsT=wd4_w[:, b, 2 * tile_n * P : 2 * (tile_n + 1) * P].bitcast(FP4X4),
+                lhsT_scale=wd_s[:, b, rows],
+                rhs=h_w[group][:].bitcast(FP8X4),
+                rhs_scale=h_s[group][:],
                 start=(b == 0),
                 stop=False,
             )
             nc.tensor.matmul_mx(
-                out=sums[nt][:, j0:j1],
-                lhsT=wd8_w[:, b, cols].bitcast(FP8X4),
-                lhsT_scale=wd_s[WD8_ROW:P, b, cols],
-                rhs=h_w[:, j0:j1].bitcast(FP8X4),
-                rhs_scale=h_s[:, j0:j1],
+                out=y[:],
+                lhsT=wd8_w[:, b, rows].bitcast(FP8X4),
+                lhsT_scale=wd_s[WD8_ROW:P, b, rows],
+                rhs=h_w[group][:].bitcast(FP8X4),
+                rhs_scale=h_s[group][:],
                 start=False,
-                stop=closing,
+                stop=(b == HALVES - 1),
             )
-            if closing:
-                o = ring.tile([P, JH], F32, name="o", bufs=8)
-                how = CFG["add"][jh * 4 + nt]
-                if how == "g":
-                    y_sb = ring.tile([P, JH], F32, name="y_sb", bufs=4)
-                    nc.scalar.copy(y_sb[:], sums[nt][:])
-                width = JH if how == "v" else JH // 2
-                for at in range(0, JH, width):
-                    piece = slice(at, at + width)
-                    if how == "g":
-                        nc.gpsimd.tensor_tensor(o[:, piece], y_sb[:, piece], res_sb[jh][:, nt, piece], ADD)
-                    else:
-                        nc.vector.tensor_tensor(o[:, piece], sums[nt][:, piece], res_sb[jh][:, nt, piece], ADD)
-                    if how == "w":
-                        nc.sync.dma_start(out[cols, jh * JH + at : jh * JH + at + width], o[:, piece])
-                if how != "w":
-                    nc.sync.dma_start(out[cols, jh * JH : (jh + 1) * JH], o[:])
+            if b == HALVES - 1:
+                result = sbuf("result%d_%d" % (span, tile_n), [P, SPAN], F32)
+                width = SPAN // 2 if (group, tile_n) == DOWN_AT_END[-1] else SPAN
+                for j0 in range(0, SPAN, width):
+                    piece = slice(j0, j0 + width)
+                    nc.vector.tensor_tensor(result[:, piece], y[:, piece], res_sb[span][:, tile_n, piece], ADD)
+                    nc.sync.dma_start(out[rows, span * SPAN + j0 : span * SPAN + j0 + width], result[:, piece])
+                free_banks.append(bank)
 
-        per_group = JH // JT
-        units = [(jh * per_group + i, b) for jh in range(J // JH) for b in range(HALVES) for i in range(per_group)]
-        h_tiles = {}
-        codes = {}
-
-        def do_up(u):
-            grp = u // per_group
-            if grp not in h_tiles:
-                h_tiles[grp] = keep.tile([P, JH, PACK], BF16, name="h%d" % grp, tag="h%d" % grp, align_bytes=64)
-            up(u, h_tiles[grp])
-
-        def do_q(grp, part):
-            if grp not in codes:
-                codes[grp] = new_h_codes()
-            j0, j1 = [(0, JH), (0, JH // 2), (JH // 2, JH), (JH // 2, 3 * JT), (3 * JT, JH)][part]
-            quantize_h(h_tiles[grp], *codes[grp], j0, j1)
-
-        for w in CFG["prog"].split():
-            k, a = w[0], w[1:]
-            if k == "G":
-                gather(int(a))
-            elif k == "S":
-                permute_wg_scales()
-            elif k == "W":
-                permute_wg_words(int(a))
-            elif k == "R":
-                round_wu(int(a))
-            elif k == "Q":
-                quantize_wu(int(a))
-            elif k == "g":
-                (gate_wide if CFG["wide"] else gate)(int(a))
-            elif k == "u":
-                do_up(int(a))
-            elif k == "q":
-                do_q(int(a[0]), int(a[1]))
-            elif k == "d":
-                down(int(a[0]), int(a[1]), *codes[int(a[0])])
-            elif k == "e":
-                for nt in range(N // P):
-                    down(3, nt, *codes[3], int(a) * JT, (int(a) + 1) * JT)
-            elif k == "L":
-                loads[a]()
+        for u in range(GATE_LEAD):
+            gate(u)
+        for u in range(len(UNITS)):
+            up(u)
+            done, rest = divmod(u + 1 - QUANTIZE_LAG, UNITS_PER_GROUP)
+            if done > 0 and rest == 0:
+                quantize_h(done - 1, 0, SPAN)
+            if u + GATE_LEAD < len(UNITS):
+                gate(u + GATE_LEAD)
+            if u in DOWN_AFTER_UNIT:
+                down(*DOWN_AFTER_UNIT[u])
+        quantize_h(GROUPS - 1, 0, SPAN // 2)
+        quantize_h(GROUPS - 1, SPAN // 2, SPAN)
+        for group, tile_n in DOWN_AT_END:
+            down(group, tile_n)

@@ -35,10 +35,11 @@ UNITS = [
     (span * UNITS_PER_GROUP + i, b) for span in range(J // SPAN) for b in range(HALVES) for i in range(UNITS_PER_GROUP)
 ]
 GROUPS = len(UNITS) // UNITS_PER_GROUP
-GATE_LEAD = 3
-QUANTIZE_LAG = 2
-DOWN_AFTER_UNIT = {9: (0, 0), 10: (0, 1), 11: (0, 2), 12: (1, 0), 13: (0, 3)}
-DOWN_AT_END = [(1, 1), (1, 2), (2, 0), (2, 1), (1, 3), (2, 2), (3, 0), (3, 1), (3, 2), (2, 3), (3, 3)]
+GATE_LEAD = BANKS
+QUANTIZE_LAG = 1
+DOWN_AFTER_UNIT = {7: [(0, 0)], 8: [(0, 1)], 11: [(1, 0), (1, 1), (0, 2)], 13: [(1, 2)], 14: [(0, 3)]}
+DOWN_AT_END = [(2, 0), (2, 1), (2, 2), (1, 3), (3, 0), (3, 1), (3, 2), (2, 3), (3, 3)]
+GPSIMD_ADDS = [(1, 0), (1, 1)]
 
 
 def tile_list_gmlpt_gelu_res_res_kernel(
@@ -67,7 +68,8 @@ def tile_list_gmlpt_gelu_res_res_kernel(
         wd8_w = sbuf("wd8_w", [P, HALVES, N], U32)
         wd_s = sbuf("wd_s", [P, HALVES, N], U8)
         res_sb = [sbuf("res%d" % span, [P, N // P, SPAN], F32) for span in range(J // SPAN)]
-        v_w = [sbuf("v_w%d" % s, [P, SLICE], U32) for s in range(J // SLICE)]
+        v_w = [sbuf("v_w%d" % s, [P, SLICE], U32) for s in range(J // SLICE - 1)]
+        v_w.append(sbuf("v_w_last", [P, SLICE], U32, "wu_bf0"))
         v_s = [sbuf("v_s%d" % s, [P, SLICE], U8) for s in range(J // SLICE)]
         h_bf = [sbuf("h_bf%d" % group, [P, SPAN, PACK], BF16) for group in range(GROUPS)]
         h_w = [sbuf("h_w%d" % group, [P, SPAN], U32) for group in range(GROUPS)]
@@ -129,10 +131,12 @@ def tile_list_gmlpt_gelu_res_res_kernel(
             count = WU_CHUNK // PACK
             dst = wu_bf[b][:, :, part * count : (part + 1) * count, :].rearrange("p t m i -> p m t i")
             src = wu_raw[c][:].rearrange("p i (m t) -> p m t i", t=PACK)
-            if c == len(wu_raw) - 1:
+            if b == 0:
+                nc.scalar.copy(dst, src)
+            elif part == 0:
                 nc.vector.tensor_copy(dst, src)
             else:
-                nc.scalar.copy(dst, src)
+                nc.gpsimd.tensor_scalar(dst, src, 1.0, 0.0, MULT, ADD)
 
         def quantize_wu(b):
             nc.vector.quantize_mx(
@@ -143,11 +147,12 @@ def tile_list_gmlpt_gelu_res_res_kernel(
 
         nc.vector.tensor_copy(wg_s[:], wg_s_raw[:].rearrange("p (m t) -> p t m", t=PACK))
         reorder_wg_words(0)
-        for s in range(J // SLICE):
+        for s in range(J // SLICE - 1):
             gather(s)
         round_wu(0)
         round_wu(1)
         quantize_wu(0)
+        gather(J // SLICE - 1)
         reorder_wg_words(1)
         round_wu(2)
         round_wu(3)
@@ -243,11 +248,21 @@ def tile_list_gmlpt_gelu_res_res_kernel(
             )
             if b == HALVES - 1:
                 result = sbuf("result%d_%d" % (span, tile_n), [P, SPAN], F32)
-                width = SPAN // 2 if (group, tile_n) == DOWN_AT_END[-1] else SPAN
-                for j0 in range(0, SPAN, width):
-                    piece = slice(j0, j0 + width)
-                    nc.vector.tensor_tensor(result[:, piece], y[:, piece], res_sb[span][:, tile_n, piece], ADD)
-                    nc.sync.dma_start(out[rows, span * SPAN + j0 : span * SPAN + j0 + width], result[:, piece])
+                tokens = out[rows, span * SPAN : (span + 1) * SPAN]
+                pieces = (slice(0, SPAN // 2), slice(SPAN // 2, SPAN))
+                if (group, tile_n) in GPSIMD_ADDS:
+                    y_sb = sbuf("y_sb%d" % tile_n, [P, SPAN], F32)
+                    nc.scalar.copy(y_sb[:], y[:])
+                    for piece in pieces:
+                        nc.gpsimd.tensor_tensor(result[:, piece], y_sb[:, piece], res_sb[span][:, tile_n, piece], ADD)
+                    nc.sync.dma_start(tokens, result[:])
+                elif (group, tile_n) == DOWN_AT_END[-1]:
+                    for piece in pieces:
+                        nc.vector.tensor_tensor(result[:, piece], y[:, piece], res_sb[span][:, tile_n, piece], ADD)
+                        nc.sync.dma_start(tokens[:, piece], result[:, piece])
+                else:
+                    nc.vector.tensor_tensor(result[:], y[:], res_sb[span][:, tile_n, :], ADD)
+                    nc.sync.dma_start(tokens, result[:])
                 free_banks.append(bank)
 
         for u in range(GATE_LEAD):
@@ -259,8 +274,8 @@ def tile_list_gmlpt_gelu_res_res_kernel(
                 quantize_h(done - 1, 0, SPAN)
             if u + GATE_LEAD < len(UNITS):
                 gate(u + GATE_LEAD)
-            if u in DOWN_AFTER_UNIT:
-                down(*DOWN_AFTER_UNIT[u])
+            for group, tile_n in DOWN_AFTER_UNIT.get(u, []):
+                down(group, tile_n)
         quantize_h(GROUPS - 1, 0, SPAN // 2)
         quantize_h(GROUPS - 1, SPAN // 2, SPAN)
         for group, tile_n in DOWN_AT_END:

@@ -38,8 +38,9 @@ GROUPS = len(UNITS) // UNITS_PER_GROUP
 GATE_LEAD = BANKS
 QUANTIZE_LAG = 1
 DOWN_AFTER_UNIT = {7: [(0, 0)], 8: [(0, 1)], 11: [(1, 0), (1, 1), (0, 2)], 13: [(1, 2)], 14: [(0, 3)]}
-DOWN_AT_END = [(2, 0), (2, 1), (2, 2), (1, 3), (3, 0), (3, 1), (3, 2), (2, 3), (3, 3)]
+DOWN_AT_END = [(2, 0), (2, 1), (2, 2), (1, 3), (3, 0), (3, 1), (3, 2)]
 GPSIMD_ADDS = [(1, 0), (1, 1)]
+GPSIMD_UNIT = 8
 
 
 def tile_list_gmlpt_gelu_res_res_kernel(
@@ -204,12 +205,14 @@ def tile_list_gmlpt_gelu_res_res_kernel(
                     stop=True,
                 )
             first = tile_j * UNIT % SPAN
-            nc.vector.tensor_tensor(
-                h_bf[u // UNITS_PER_GROUP][:, first : first + UNIT, :].rearrange("p j (pair e) -> p j pair e", e=2),
-                ub[:].rearrange("p (pair e) j -> p j pair e", e=2),
-                gates[u // 2][:, :, at : at + UNIT, :].rearrange("p pair j e -> p j pair e"),
-                MULT,
-            )
+            h = h_bf[u // UNITS_PER_GROUP][:, first : first + UNIT, :].rearrange("p j (pair e) -> p j pair e", e=2)
+            gelus = gates[u // 2][:, :, at : at + UNIT, :].rearrange("p pair j e -> p j pair e")
+            if u == GPSIMD_UNIT:
+                ub_sb = sbuf("ub_sb", [P, UNIT, PACK], F32)
+                nc.scalar.copy(ub_sb[:], ub[:].rearrange("p t j -> p j t"))
+                nc.gpsimd.tensor_tensor(h, ub_sb[:].rearrange("p j (pair e) -> p j pair e", e=2), gelus, MULT)
+            else:
+                nc.vector.tensor_tensor(h, ub[:].rearrange("p (pair e) j -> p j pair e", e=2), gelus, MULT)
             free_banks.append(bank)
 
         def quantize_h(group, j0, j1):
@@ -256,14 +259,39 @@ def tile_list_gmlpt_gelu_res_res_kernel(
                     for piece in pieces:
                         nc.gpsimd.tensor_tensor(result[:, piece], y_sb[:, piece], res_sb[span][:, tile_n, piece], ADD)
                     nc.sync.dma_start(tokens, result[:])
-                elif (group, tile_n) == DOWN_AT_END[-1]:
-                    for piece in pieces:
-                        nc.vector.tensor_tensor(result[:, piece], y[:, piece], res_sb[span][:, tile_n, piece], ADD)
-                        nc.sync.dma_start(tokens[:, piece], result[:, piece])
                 else:
                     nc.vector.tensor_tensor(result[:], y[:], res_sb[span][:, tile_n, :], ADD)
                     nc.sync.dma_start(tokens, result[:])
                 free_banks.append(bank)
+
+        def last_tile(j0, width):
+            span, tile_n = J // SPAN - 1, N // P - 1
+            y = psum.tile([P, width], F32, name="y_last", tag=take_bank())
+            rows = slice(tile_n * P, (tile_n + 1) * P)
+            for b in range(HALVES):
+                group = span * HALVES + b
+                for at in range(0, width, UNIT):
+                    nc.tensor.matmul_mx(
+                        out=y[:, at : at + UNIT],
+                        lhsT=wd4_w[:, b, 2 * tile_n * P : 2 * (tile_n + 1) * P].bitcast(FP4X4),
+                        lhsT_scale=wd_s[:, b, rows],
+                        rhs=h_w[group][:, j0 + at : j0 + at + UNIT].bitcast(FP8X4),
+                        rhs_scale=h_s[group][:, j0 + at : j0 + at + UNIT],
+                        start=(b == 0 and at == 0),
+                        stop=False,
+                    )
+                nc.tensor.matmul_mx(
+                    out=y[:],
+                    lhsT=wd8_w[:, b, rows].bitcast(FP8X4),
+                    lhsT_scale=wd_s[WD8_ROW:P, b, rows],
+                    rhs=h_w[group][:, j0 : j0 + width].bitcast(FP8X4),
+                    rhs_scale=h_s[group][:, j0 : j0 + width],
+                    start=False,
+                    stop=(b == HALVES - 1),
+                )
+            result = sbuf("result_last%d" % j0, [P, width], F32)
+            nc.vector.tensor_tensor(result[:], y[:], res_sb[span][:, tile_n, j0 : j0 + width], ADD)
+            nc.sync.dma_start(out[rows, span * SPAN + j0 : span * SPAN + j0 + width], result[:])
 
         for u in range(GATE_LEAD):
             gate(u)
@@ -280,3 +308,5 @@ def tile_list_gmlpt_gelu_res_res_kernel(
         quantize_h(GROUPS - 1, SPAN // 2, SPAN)
         for group, tile_n in DOWN_AT_END:
             down(group, tile_n)
+        for j0 in range(0, SPAN, SPAN // 2):
+            last_tile(j0, SPAN // 2)

@@ -22,6 +22,8 @@ PACK = 4
 PASS = P * PACK
 HALVES = R // PASS
 QUADRANT = 32
+BLOCKS = 4
+LIST_ROWS = 16
 BANKS = 8
 SLICE = 256
 UNIT = 128
@@ -37,10 +39,9 @@ UNITS = [
 GROUPS = len(UNITS) // UNITS_PER_GROUP
 GATE_LEAD = BANKS
 QUANTIZE_LAG = 1
-DOWN_AFTER_UNIT = {7: [(0, 0)], 8: [(0, 1)], 11: [(1, 0), (1, 1), (0, 2)], 13: [(1, 2)], 14: [(0, 3)]}
-DOWN_AT_END = [(2, 0), (2, 1), (2, 2), (1, 3), (3, 0), (3, 1), (3, 2)]
 GPSIMD_ADDS = [(1, 0), (1, 1)]
-GPSIMD_UNIT = 8
+GPSIMD_UNIT = len(UNITS) - GATE_LEAD
+LAST_WIDTH = SPAN // 2
 
 
 def tile_list_gmlpt_gelu_res_res_kernel(
@@ -54,7 +55,7 @@ def tile_list_gmlpt_gelu_res_res_kernel(
         def sbuf(name, shape, dtype, tag=None):
             return keep.tile(shape, dtype, name=name, tag=tag or name, align_bytes=64)
 
-        offsets = keep.tile([P, J // 16], U16, name="offsets")
+        offsets = keep.tile([P, J // LIST_ROWS], U16, name="offsets")
         tab_w = sbuf("tab_w", [P, T], U32)
         tab_s = sbuf("tab_s", [P, T], U8)
         wg_w_raw = sbuf("wg_w_raw", [P, HALVES, PASS], I32)
@@ -82,27 +83,27 @@ def tile_list_gmlpt_gelu_res_res_kernel(
             nc.sync.dma_start(wg_w_raw[:, b, :], words[:, b * PASS : (b + 1) * PASS])
 
         def load_wu(c):
-            rows = wu.rearrange("(p i) r -> p i r", i=PACK)
-            nc.sync.dma_start(wu_raw[c][:], rows[:, :, c * WU_CHUNK : (c + 1) * WU_CHUNK])
+            src = wu.rearrange("(p i) r -> p i r", i=PACK)
+            nc.sync.dma_start(wu_raw[c][:], src[:, :, c * WU_CHUNK : (c + 1) * WU_CHUNK])
 
         def load_wd_scales(engine, scales, row):
-            for r in range(4):
-                rows = scales.rearrange("a (q r) n -> r q a n", r=4)[r]
-                engine.dma_start(wd_s[row + r : P : QUADRANT, :, :].bitcast(I32), rows.bitcast(I32))
+            for block in range(BLOCKS):
+                src = scales.rearrange("a (quad block) n -> block quad a n", block=BLOCKS)[block]
+                engine.dma_start(wd_s[row + block : P : QUADRANT, :, :].bitcast(I32), src.bitcast(I32))
 
         nc.vector.memset(wg_s_raw[:].bitcast(I32), 0)
         load_wg(0)
         nc.vector.memset(tab_s[:].bitcast(I32), 0)
         nc.vector.memset(warm[:, 0, :], 0.0)
         nc.vector.memset(wd_s[:].rearrange("p a n -> p (a n)").bitcast(I32), 0)
-        for q, engine in enumerate((nc.sync, nc.sync, nc.scalar, nc.scalar)):
-            rows = wg_scales[0][4 * q : 4 * q + 4, :].rearrange("r (b c) -> b r c", b=HALVES)
-            first = QUADRANT * q + WG_ROW
-            engine.dma_start(wg_s_raw[first : first + 4 * HALVES, :].bitcast(I32), rows.bitcast(I32))
-        nc.sync.dma_start(tab_w[:].bitcast(I32), tab_words[0].rearrange("p t i -> p (t i)").bitcast(I32))
-        for r in range(4):
-            rows = tab_scales[0].rearrange("(q r) t -> r q t", r=4)[r]
-            nc.scalar.dma_start(tab_s[r:P:QUADRANT, :].bitcast(I32), rows.bitcast(I32))
+        for quad, engine in enumerate((nc.sync, nc.sync, nc.scalar, nc.scalar)):
+            src = wg_scales[0][BLOCKS * quad : BLOCKS * (quad + 1), :].rearrange("block (b c) -> b block c", b=HALVES)
+            partition = QUADRANT * quad + WG_ROW
+            engine.dma_start(wg_s_raw[partition : partition + BLOCKS * HALVES, :].bitcast(I32), src.bitcast(I32))
+        nc.sync.dma_start(tab_w[:].bitcast(I32), tab_words[0].rearrange("p col i -> p (col i)").bitcast(I32))
+        for block in range(BLOCKS):
+            src = tab_scales[0].rearrange("(quad block) col -> block quad col", block=BLOCKS)[block]
+            nc.scalar.dma_start(tab_s[block:P:QUADRANT, :].bitcast(I32), src.bitcast(I32))
         nc.sync.dma_start(offsets[:], offs)
         nc.scalar.activation(warm[:, 1, :], warm[:, 0, :], GELU)
         load_wu(0)
@@ -115,11 +116,11 @@ def tile_list_gmlpt_gelu_res_res_kernel(
         nc.sync.dma_start(wd8_w[:].bitcast(I32), wd8_words.rearrange("a p n i -> p a (n i)").bitcast(I32))
         load_wd_scales(nc.sync, wd8_scales, WD8_ROW)
         for span in range(J // SPAN):
-            rows = res.rearrange("(c p) j -> p c j", p=P)
-            nc.sync.dma_start(res_sb[span][:], rows[:, :, span * SPAN : (span + 1) * SPAN])
+            src = res.rearrange("(tile p) j -> p tile j", p=P)
+            nc.sync.dma_start(res_sb[span][:], src[:, :, span * SPAN : (span + 1) * SPAN])
 
         def gather(s):
-            entries = offsets[:, s * SLICE // 16 : (s + 1) * SLICE // 16]
+            entries = offsets[:, s * SLICE // LIST_ROWS : (s + 1) * SLICE // LIST_ROWS]
             nc.vector.tensor_copy(v_w[s][:], tab_w[:].indirect(entries))
             nc.vector.tensor_copy(v_s[s][:], tab_s[:].indirect(entries))
 
@@ -178,7 +179,7 @@ def tile_list_gmlpt_gelu_res_res_kernel(
                 nc.tensor.matmul_mx(
                     out=ga[:, e, :],
                     lhsT=wg_w[:, b, 2 * pair + e, :].bitcast(FP8X4),
-                    lhsT_scale=wg_s[WG_ROW + 4 * b : P, 2 * pair + e, :],
+                    lhsT_scale=wg_s[WG_ROW + BLOCKS * b : P, 2 * pair + e, :],
                     rhs=v_w[s][:].bitcast(FP8X4),
                     rhs_scale=v_s[s][:],
                     start=True,
@@ -252,11 +253,10 @@ def tile_list_gmlpt_gelu_res_res_kernel(
             if b == HALVES - 1:
                 result = sbuf("result%d_%d" % (span, tile_n), [P, SPAN], F32)
                 tokens = out[rows, span * SPAN : (span + 1) * SPAN]
-                pieces = (slice(0, SPAN // 2), slice(SPAN // 2, SPAN))
                 if (group, tile_n) in GPSIMD_ADDS:
                     y_sb = sbuf("y_sb%d" % tile_n, [P, SPAN], F32)
                     nc.scalar.copy(y_sb[:], y[:])
-                    for piece in pieces:
+                    for piece in (slice(0, SPAN // 2), slice(SPAN // 2, SPAN)):
                         nc.gpsimd.tensor_tensor(result[:, piece], y_sb[:, piece], res_sb[span][:, tile_n, piece], ADD)
                     nc.sync.dma_start(tokens, result[:])
                 else:
@@ -264,8 +264,8 @@ def tile_list_gmlpt_gelu_res_res_kernel(
                     nc.sync.dma_start(tokens, result[:])
                 free_banks.append(bank)
 
-        def last_tile(j0, width):
-            span, tile_n = J // SPAN - 1, N // P - 1
+        def last_tile(j0):
+            span, tile_n, width = J // SPAN - 1, N // P - 1, LAST_WIDTH
             y = psum.tile([P, width], F32, name="y_last", tag=take_bank())
             rows = slice(tile_n * P, (tile_n + 1) * P)
             for b in range(HALVES):
@@ -293,6 +293,13 @@ def tile_list_gmlpt_gelu_res_res_kernel(
             nc.vector.tensor_tensor(result[:], y[:], res_sb[span][:, tile_n, j0 : j0 + width], ADD)
             nc.sync.dma_start(out[rows, span * SPAN + j0 : span * SPAN + j0 + width], result[:])
 
+        first_span_steps = [(b, tile_n) for b in range(HALVES) for tile_n in (0, 1)]
+        first_span_steps.extend([(b, tile_n) for tile_n in (2, 3) for b in range(HALVES)])
+        last_gate_unit = len(UNITS) - GATE_LEAD - 1
+        third_group_end = 3 * UNITS_PER_GROUP - 1
+        step_units = [last_gate_unit, last_gate_unit + 1, third_group_end]
+        step_units.extend(range(third_group_end, len(UNITS) - 1))
+
         for u in range(GATE_LEAD):
             gate(u)
         for u in range(len(UNITS)):
@@ -302,11 +309,16 @@ def tile_list_gmlpt_gelu_res_res_kernel(
                 quantize_h(done - 1, 0, SPAN)
             if u + GATE_LEAD < len(UNITS):
                 gate(u + GATE_LEAD)
-            for group, tile_n in DOWN_AFTER_UNIT.get(u, []):
-                down(group, tile_n)
-        quantize_h(GROUPS - 1, 0, SPAN // 2)
-        quantize_h(GROUPS - 1, SPAN // 2, SPAN)
-        for group, tile_n in DOWN_AT_END:
-            down(group, tile_n)
-        for j0 in range(0, SPAN, SPAN // 2):
-            last_tile(j0, SPAN // 2)
+            if u == len(UNITS) - 1:
+                quantize_h(GROUPS - 1, 0, SPAN // 2)
+                quantize_h(GROUPS - 1, SPAN // 2, SPAN)
+            for after, step in zip(step_units, first_span_steps):
+                if after == u:
+                    down(*step)
+        for tile_n in range(N // P - 1):
+            down(GROUPS - 2, tile_n)
+        down(*first_span_steps[-1])
+        for tile_n in range(N // P - 1):
+            down(GROUPS - 1, tile_n)
+        for j0 in range(0, SPAN, LAST_WIDTH):
+            last_tile(j0)

@@ -24,24 +24,15 @@ HALVES = R // PASS
 QUADRANT = 32
 BLOCKS = 4
 LIST_ROWS = 16
-BANKS = 8
 SLICE = 256
 UNIT = 128
 SPAN = 512
+SPANS = J // SPAN
 WU_CHUNK = 256
 WG_ROW = 4
 WD8_ROW = 4
-
-UNITS_PER_GROUP = SPAN // UNIT
-UNITS = [
-    (span * UNITS_PER_GROUP + i, b) for span in range(J // SPAN) for b in range(HALVES) for i in range(UNITS_PER_GROUP)
-]
-GROUPS = len(UNITS) // UNITS_PER_GROUP
-GATE_LEAD = BANKS
-QUANTIZE_LAG = 1
-GPSIMD_ADDS = [(1, 0), (1, 1)]
-GPSIMD_UNIT = len(UNITS) - GATE_LEAD
 LAST_WIDTH = SPAN // 2
+GPSIMD_ADDS = [(0, 0), (0, 1)]
 
 
 def tile_list_gmlpt_gelu_res_res_kernel(
@@ -58,267 +49,306 @@ def tile_list_gmlpt_gelu_res_res_kernel(
         offsets = keep.tile([P, J // LIST_ROWS], U16, name="offsets")
         tab_w = sbuf("tab_w", [P, T], U32)
         tab_s = sbuf("tab_s", [P, T], U8)
-        wg_w_raw = sbuf("wg_w_raw", [P, HALVES, PASS], I32)
+        wg_w_raw = [sbuf("wg_w_raw%d" % b, [P, PASS], I32) for b in range(HALVES)]
         wg_s_raw = sbuf("wg_s_raw", [P, PASS], U8)
-        wg_w = sbuf("wg_w", [P, HALVES, PACK, P], I32)
+        wg_w = [sbuf("wg_w%d" % b, [P, PACK, P], I32) for b in range(HALVES)]
         wg_s = sbuf("wg_s", [P, PACK, P], U8)
         wu_raw = [sbuf("wu_raw%d" % c, [P, PACK, WU_CHUNK], F32) for c in range(R // WU_CHUNK)]
         wu_bf = [sbuf("wu_bf%d" % b, [P, PACK, P, PACK], BF16) for b in range(HALVES)]
-        wu_w = sbuf("wu_w", [P, HALVES, PASS], U32)
-        wu_s = sbuf("wu_s", [P, HALVES, PASS], U8)
+        wu_w = [sbuf("wu_w%d" % b, [P, PASS], U32) for b in range(HALVES)]
+        wu_s = [sbuf("wu_s%d" % b, [P, PASS], U8) for b in range(HALVES)]
         wd4_w = sbuf("wd4_w", [P, HALVES, 2 * N], U8)
-        wd8_w = sbuf("wd8_w", [P, HALVES, N], U32)
-        wd_s = sbuf("wd_s", [P, HALVES, N], U8)
-        res_sb = [sbuf("res%d" % span, [P, N // P, SPAN], F32) for span in range(J // SPAN)]
-        v_w = [sbuf("v_w%d" % s, [P, SLICE], U32) for s in range(J // SLICE - 1)]
-        v_w.append(sbuf("v_w_last", [P, SLICE], U32, "wu_bf0"))
-        v_s = [sbuf("v_s%d" % s, [P, SLICE], U8) for s in range(J // SLICE)]
-        h_bf = [sbuf("h_bf%d" % group, [P, SPAN, PACK], BF16) for group in range(GROUPS)]
-        h_w = [sbuf("h_w%d" % group, [P, SPAN], U32) for group in range(GROUPS)]
-        h_s = [sbuf("h_s%d" % group, [P, SPAN], U8) for group in range(GROUPS)]
+        wd8_w = [sbuf("wd8_w%d" % b, [P, N], U32) for b in range(HALVES)]
+        wd4_s = sbuf("wd4_s", [P, HALVES, N], U8)
+        wd8_s = sbuf("wd8_s", [P, HALVES, N], U8)
+        res_sb = [sbuf("res%d" % span, [P, N // P, SPAN], F32) for span in range(SPANS)]
+        v_s = sbuf("v_s", [P, J], U8)
+        v_first = sbuf("v_first", [P, SLICE], U32)
+        h_bf = {}
+        h_w = {}
+        h_s = {}
+        for b in range(HALVES):
+            for span in range(SPANS):
+                h_bf[b, span] = sbuf("h_bf%d%d" % (b, span), [P, SPAN, PACK], BF16)
+                h_w[b, span] = sbuf("h_w%d%d" % (b, span), [P, SPAN], U32)
+                h_s[b, span] = sbuf("h_s%d%d" % (b, span), [P, SPAN], U8)
         warm = sbuf("warm", [P, 2, 8], F32)
 
         def load_wg(b):
             words = wg_words[0].rearrange("p r i -> p (r i)").bitcast(I32)
-            nc.sync.dma_start(wg_w_raw[:, b, :], words[:, b * PASS : (b + 1) * PASS])
+            nc.sync.dma_start(wg_w_raw[b][:], words[:, b * PASS : (b + 1) * PASS])
 
         def load_wu(c):
             src = wu.rearrange("(p i) r -> p i r", i=PACK)
             nc.sync.dma_start(wu_raw[c][:], src[:, :, c * WU_CHUNK : (c + 1) * WU_CHUNK])
 
-        def load_wd_scales(engine, scales, row):
+        def load_wd_scales(engine, wd_s, scales, row):
             for block in range(BLOCKS):
                 src = scales.rearrange("a (quad block) n -> block quad a n", block=BLOCKS)[block]
                 engine.dma_start(wd_s[row + block : P : QUADRANT, :, :].bitcast(I32), src.bitcast(I32))
 
-        nc.vector.memset(wg_s_raw[:].bitcast(I32), 0)
-        load_wg(0)
+        def load_wd8(b):
+            nc.sync.dma_start(wd8_w[b][:].bitcast(I32), wd8_words[b].rearrange("p n i -> p (n i)").bitcast(I32))
+
         nc.vector.memset(tab_s[:].bitcast(I32), 0)
+        nc.vector.memset(wg_s_raw[:].bitcast(I32), 0)
+        nc.vector.memset(wd8_s[:].rearrange("p a n -> p (a n)").bitcast(I32), 0)
+        nc.vector.memset(wd4_s[:].rearrange("p a n -> p (a n)").bitcast(I32), 0)
         nc.vector.memset(warm[:, 0, :], 0.0)
-        nc.vector.memset(wd_s[:].rearrange("p a n -> p (a n)").bitcast(I32), 0)
-        for quad, engine in enumerate((nc.sync, nc.sync, nc.scalar, nc.scalar)):
+        nc.sync.dma_start(offsets[:], offs)
+        load_wg(0)
+        for block, engine in enumerate((nc.sync, nc.scalar, nc.sync, nc.scalar)):
+            src = tab_scales[0].rearrange("(quad block) col -> block quad col", block=BLOCKS)[block]
+            engine.dma_start(tab_s[block:P:QUADRANT, :].bitcast(I32), src.bitcast(I32))
+        nc.sync.dma_start(tab_w[:].bitcast(I32), tab_words[0].rearrange("p col i -> p (col i)").bitcast(I32))
+        for quad in range(P // QUADRANT):
             src = wg_scales[0][BLOCKS * quad : BLOCKS * (quad + 1), :].rearrange("block (b c) -> b block c", b=HALVES)
             partition = QUADRANT * quad + WG_ROW
-            engine.dma_start(wg_s_raw[partition : partition + BLOCKS * HALVES, :].bitcast(I32), src.bitcast(I32))
-        nc.sync.dma_start(tab_w[:].bitcast(I32), tab_words[0].rearrange("p col i -> p (col i)").bitcast(I32))
-        for block in range(BLOCKS):
-            src = tab_scales[0].rearrange("(quad block) col -> block quad col", block=BLOCKS)[block]
-            nc.scalar.dma_start(tab_s[block:P:QUADRANT, :].bitcast(I32), src.bitcast(I32))
-        nc.sync.dma_start(offsets[:], offs)
+            nc.sync.dma_start(wg_s_raw[partition : partition + BLOCKS * HALVES, :].bitcast(I32), src.bitcast(I32))
+        load_wd_scales(nc.gpsimd, wd8_s, wd8_scales, WD8_ROW)
         nc.scalar.activation(warm[:, 1, :], warm[:, 0, :], GELU)
         load_wu(0)
         load_wu(1)
         load_wg(1)
-        load_wd_scales(nc.scalar, wd4_scales, 0)
         load_wu(2)
         load_wu(3)
+        load_wd8(0)
         nc.sync.dma_start(wd4_w[:].bitcast(I32), wd4_words.rearrange("a p c -> p a c").bitcast(I32))
-        nc.sync.dma_start(wd8_w[:].bitcast(I32), wd8_words.rearrange("a p n i -> p a (n i)").bitcast(I32))
-        load_wd_scales(nc.sync, wd8_scales, WD8_ROW)
-        for span in range(J // SPAN):
+        load_wd_scales(nc.sync, wd4_s, wd4_scales, 0)
+        load_wd8(1)
+        for span in range(SPANS):
             src = res.rearrange("(tile p) j -> p tile j", p=P)
             nc.sync.dma_start(res_sb[span][:], src[:, :, span * SPAN : (span + 1) * SPAN])
 
-        def gather(s):
-            entries = offsets[:, s * SLICE // LIST_ROWS : (s + 1) * SLICE // LIST_ROWS]
-            nc.vector.tensor_copy(v_w[s][:], tab_w[:].indirect(entries))
-            nc.vector.tensor_copy(v_s[s][:], tab_s[:].indirect(entries))
+        def entries(j0, j1):
+            return offsets[:, j0 // LIST_ROWS : j1 // LIST_ROWS]
 
         def reorder_wg_words(b):
-            src = wg_w_raw[:, b, :].rearrange("p (m t) -> p m t", t=PACK)
-            nc.vector.tensor_copy(wg_w[:, b, :, :].rearrange("p t m -> p m t"), src)
+            src = wg_w_raw[b][:].rearrange("p (m t) -> p m t", t=PACK)
+            nc.vector.tensor_copy(wg_w[b][:].rearrange("p t m -> p m t"), src)
 
-        def round_wu(c):
+        def round_wu(c, copy, m0=0, m1=WU_CHUNK // PACK):
             b, part = divmod(c, PASS // WU_CHUNK)
-            count = WU_CHUNK // PACK
-            dst = wu_bf[b][:, :, part * count : (part + 1) * count, :].rearrange("p t m i -> p m t i")
-            src = wu_raw[c][:].rearrange("p i (m t) -> p m t i", t=PACK)
-            if b == 0:
-                nc.scalar.copy(dst, src)
-            elif part == 0:
-                nc.vector.tensor_copy(dst, src)
-            else:
-                nc.gpsimd.tensor_scalar(dst, src, 1.0, 0.0, MULT, ADD)
+            first = part * WU_CHUNK // PACK
+            dst = wu_bf[b][:, :, first + m0 : first + m1, :].rearrange("p t m i -> p m t i")
+            copy(dst, wu_raw[c][:, :, PACK * m0 : PACK * m1].rearrange("p i (m t) -> p m t i", t=PACK))
 
         def quantize_wu(b):
             nc.vector.quantize_mx(
-                out=wu_w[:, b, :].bitcast(FP8X4),
-                scales=wu_s[:, b, :],
+                out=wu_w[b][:].bitcast(FP8X4),
+                scales=wu_s[b][:],
                 in_=wu_bf[b][:].rearrange("p t m i -> p (t m i)"),
             )
 
-        nc.vector.tensor_copy(wg_s[:], wg_s_raw[:].rearrange("p (m t) -> p t m", t=PACK))
+        def gather_words(dst, j0):
+            nc.vector.tensor_copy(dst, tab_w[:].indirect(entries(j0, j0 + SLICE)))
+
         reorder_wg_words(0)
-        for s in range(J // SLICE - 1):
-            gather(s)
-        round_wu(0)
-        round_wu(1)
-        quantize_wu(0)
-        gather(J // SLICE - 1)
-        reorder_wg_words(1)
-        round_wu(2)
-        round_wu(3)
-        quantize_wu(1)
+        for j0 in range(0, J, SPAN):
+            nc.vector.tensor_copy(v_s[:, j0 : j0 + SPAN], tab_s[:].indirect(entries(j0, j0 + SPAN)))
+        gather_words(v_first[:], 0)
+        nc.vector.tensor_copy(wg_s[:], wg_s_raw[:].rearrange("p (m t) -> p t m", t=PACK))
+        v_rest = sbuf("v_rest", [P, J - 2 * SLICE], U32, "wg_s_raw")
+        for j0 in range(SLICE, J - SLICE, SLICE):
+            gather_words(v_rest[:, j0 - SLICE : j0], j0)
+        v_last = []
 
-        free_banks = ["bank%d" % i for i in range(BANKS)]
+        def gather_last():
+            v_last.append(sbuf("v_last", [P, SLICE], U32, "wu_bf0"))
+            gather_words(v_last[0][:], J - SLICE)
 
-        def take_bank():
-            bank = free_banks[0]
-            free_banks.remove(bank)
-            return bank
+        def words(j0, width):
+            if j0 < SLICE:
+                return v_first[:, j0 : j0 + width].bitcast(FP8X4)
+            if j0 >= J - SLICE:
+                return v_last[0][:, j0 - (J - SLICE) : j0 - (J - SLICE) + width].bitcast(FP8X4)
+            return v_rest[:, j0 - SLICE : j0 - SLICE + width].bitcast(FP8X4)
 
-        gate_tags = {0: "wu_raw1", 1: "wu_raw0"}
+        def scales(j0, width):
+            return v_s[:, j0 : j0 + width]
+
+        def gpsimd_round(dst, src):
+            nc.gpsimd.tensor_scalar(dst, src, 1.0, 0.0, MULT, ADD)
+
         gates = {}
 
-        def gate(u):
-            tile_j, b = UNITS[u]
-            s, pair = divmod(tile_j, SLICE // UNIT)
-            bank = take_bank()
-            ga = psum.tile([P, 2, SLICE], F32, name="ga", tag=bank)
+        def gate(g, bank):
+            b, rest = divmod(g, 8)
+            s, pair = divmod(rest, 2)
+            ga = psum.tile([P, 2, SLICE], F32, name="ga", tag="bank%d" % bank)
             for e in range(2):
                 nc.tensor.matmul_mx(
                     out=ga[:, e, :],
-                    lhsT=wg_w[:, b, 2 * pair + e, :].bitcast(FP8X4),
+                    lhsT=wg_w[b][:, 2 * pair + e, :].bitcast(FP8X4),
                     lhsT_scale=wg_s[WG_ROW + BLOCKS * b : P, 2 * pair + e, :],
-                    rhs=v_w[s][:].bitcast(FP8X4),
-                    rhs_scale=v_s[s][:],
+                    rhs=words(s * SLICE, SLICE),
+                    rhs_scale=scales(s * SLICE, SLICE),
                     start=True,
                     stop=True,
                 )
             if pair == 0:
-                gates[u // 2] = sbuf("gate%d" % (u // 2), [P, 2, SLICE, 2], F32, gate_tags.get(u // 2))
-            nc.scalar.activation(gates[u // 2][:, pair, :, :], ga[:].rearrange("p e j -> p j e"), GELU)
-            free_banks.append(bank)
+                gates[b, s] = sbuf("gate%d%d" % (b, s), [P, 2, SLICE, 2], F32)
+            nc.scalar.activation(gates[b, s][:, pair, :, :], ga[:].rearrange("p e j -> p j e"), GELU)
 
-        def up(u):
-            tile_j, b = UNITS[u]
-            s, at = divmod(tile_j * UNIT, SLICE)
-            bank = take_bank()
-            ub = psum.tile([P, PACK, UNIT], F32, name="ub", tag=bank)
+        def up(u, bank):
+            b, tile_j = divmod(u, 8)
+            j0 = tile_j * UNIT
+            s, at = divmod(j0, SLICE)
+            span, first = divmod(j0, SPAN)
+            ub = psum.tile([P, PACK, UNIT], F32, name="ub", tag="bank%d" % bank)
             for t in range(PACK):
                 nc.tensor.matmul_mx(
                     out=ub[:, t, :],
-                    lhsT=wu_w[:, b, t * P : (t + 1) * P].bitcast(FP8X4),
-                    lhsT_scale=wu_s[:, b, t * P : (t + 1) * P],
-                    rhs=v_w[s][:, at : at + UNIT].bitcast(FP8X4),
-                    rhs_scale=v_s[s][:, at : at + UNIT],
+                    lhsT=wu_w[b][:, t * P : (t + 1) * P].bitcast(FP8X4),
+                    lhsT_scale=wu_s[b][:, t * P : (t + 1) * P],
+                    rhs=words(j0, UNIT),
+                    rhs_scale=scales(j0, UNIT),
                     start=True,
                     stop=True,
                 )
-            first = tile_j * UNIT % SPAN
-            h = h_bf[u // UNITS_PER_GROUP][:, first : first + UNIT, :].rearrange("p j (pair e) -> p j pair e", e=2)
-            gelus = gates[u // 2][:, :, at : at + UNIT, :].rearrange("p pair j e -> p j pair e")
-            if u == GPSIMD_UNIT:
-                ub_sb = sbuf("ub_sb", [P, UNIT, PACK], F32)
-                nc.scalar.copy(ub_sb[:], ub[:].rearrange("p t j -> p j t"))
-                nc.gpsimd.tensor_tensor(h, ub_sb[:].rearrange("p j (pair e) -> p j pair e", e=2), gelus, MULT)
-            else:
-                nc.vector.tensor_tensor(h, ub[:].rearrange("p (pair e) j -> p j pair e", e=2), gelus, MULT)
-            free_banks.append(bank)
+            h = h_bf[b, span][:, first : first + UNIT, :].rearrange("p j (pair e) -> p j pair e", e=2)
+            gelus = gates[b, s][:, :, at : at + UNIT, :].rearrange("p pair j e -> p j pair e")
+            nc.vector.tensor_tensor(h, ub[:].rearrange("p (pair e) j -> p j pair e", e=2), gelus, MULT)
 
-        def quantize_h(group, j0, j1):
+        def quantize_h(b, span, j0=0, j1=SPAN):
             nc.vector.quantize_mx(
-                out=h_w[group][:, j0:j1].bitcast(FP8X4),
-                scales=h_s[group][:, j0:j1],
-                in_=h_bf[group][:, j0:j1, :].rearrange("p j t -> p (j t)"),
+                out=h_w[b, span][:, j0:j1].bitcast(FP8X4),
+                scales=h_s[b, span][:, j0:j1],
+                in_=h_bf[b, span][:, j0:j1, :].rearrange("p j t -> p (j t)"),
             )
 
         sums = {}
+        late = []
 
-        def down(group, tile_n):
-            span, b = divmod(group, HALVES)
+        def finish(y, span, tile_n, j0, width):
+            at = span * SPAN + j0
+            res_part = res_sb[span][:, tile_n, j0 : j0 + width]
+            if (span, tile_n) in GPSIMD_ADDS:
+                y_sb = sbuf("y_sb%d" % tile_n, [P, width], F32)
+                nc.scalar.copy(y_sb[:], y[:])
+                if not late:
+                    late.append(sbuf("late", [P, len(GPSIMD_ADDS), width], F32, "h_bf01"))
+                result = late[0][:, GPSIMD_ADDS.index((span, tile_n)), :]
+                nc.gpsimd.tensor_tensor(result, y_sb[:], res_part, ADD)
+                nc.sync.dma_start(out[tile_n * P : (tile_n + 1) * P, at : at + width], result)
+                return
+            result = sbuf("result%d_%d_%d" % (span, tile_n, j0), [P, width], F32)
+            nc.vector.tensor_tensor(result[:], y[:], res_part, ADD)
+            nc.sync.dma_start(out[tile_n * P : (tile_n + 1) * P, at : at + width], result[:])
+
+        def down8(b, span, tile_n, bank=None):
             if b == 0:
-                bank = take_bank()
-                sums[tile_n] = (bank, psum.tile([P, SPAN], F32, name="y", tag=bank))
-            bank, y = sums[tile_n]
+                sums[span, tile_n] = psum.tile([P, SPAN], F32, name="y", tag="bank%d" % bank)
             rows = slice(tile_n * P, (tile_n + 1) * P)
             nc.tensor.matmul_mx(
-                out=y[:],
-                lhsT=wd4_w[:, b, 2 * tile_n * P : 2 * (tile_n + 1) * P].bitcast(FP4X4),
-                lhsT_scale=wd_s[:, b, rows],
-                rhs=h_w[group][:].bitcast(FP8X4),
-                rhs_scale=h_s[group][:],
+                out=sums[span, tile_n][:],
+                lhsT=wd8_w[b][:, rows].bitcast(FP8X4),
+                lhsT_scale=wd8_s[WD8_ROW:P, b, rows],
+                rhs=h_w[b, span][:].bitcast(FP8X4),
+                rhs_scale=h_s[b, span][:],
                 start=(b == 0),
                 stop=False,
             )
+
+        def down4(b, span, tile_n):
+            rows = slice(tile_n * P, (tile_n + 1) * P)
             nc.tensor.matmul_mx(
-                out=y[:],
-                lhsT=wd8_w[:, b, rows].bitcast(FP8X4),
-                lhsT_scale=wd_s[WD8_ROW:P, b, rows],
-                rhs=h_w[group][:].bitcast(FP8X4),
-                rhs_scale=h_s[group][:],
+                out=sums[span, tile_n][:],
+                lhsT=wd4_w[:, b, 2 * tile_n * P : 2 * (tile_n + 1) * P].bitcast(FP4X4),
+                lhsT_scale=wd4_s[:, b, rows],
+                rhs=h_w[b, span][:].bitcast(FP8X4),
+                rhs_scale=h_s[b, span][:],
                 start=False,
                 stop=(b == HALVES - 1),
             )
             if b == HALVES - 1:
-                result = sbuf("result%d_%d" % (span, tile_n), [P, SPAN], F32)
-                tokens = out[rows, span * SPAN : (span + 1) * SPAN]
-                if (group, tile_n) in GPSIMD_ADDS:
-                    y_sb = sbuf("y_sb%d" % tile_n, [P, SPAN], F32)
-                    nc.scalar.copy(y_sb[:], y[:])
-                    for piece in (slice(0, SPAN // 2), slice(SPAN // 2, SPAN)):
-                        nc.gpsimd.tensor_tensor(result[:, piece], y_sb[:, piece], res_sb[span][:, tile_n, piece], ADD)
-                    nc.sync.dma_start(tokens, result[:])
-                else:
-                    nc.vector.tensor_tensor(result[:], y[:], res_sb[span][:, tile_n, :], ADD)
-                    nc.sync.dma_start(tokens, result[:])
-                free_banks.append(bank)
+                finish(sums[span, tile_n], span, tile_n, 0, SPAN)
 
-        def last_tile(j0):
-            span, tile_n, width = J // SPAN - 1, N // P - 1, LAST_WIDTH
-            y = psum.tile([P, width], F32, name="y_last", tag=take_bank())
+        def down(b, span, tile_n, bank=None):
+            down8(b, span, tile_n, bank)
+            down4(b, span, tile_n)
+
+        def last_tile(j0, bank):
+            span, tile_n, width = SPANS - 1, N // P - 1, LAST_WIDTH
+            y = psum.tile([P, width], F32, name="y_last", tag="bank%d" % bank)
             rows = slice(tile_n * P, (tile_n + 1) * P)
             for b in range(HALVES):
-                group = span * HALVES + b
                 for at in range(0, width, UNIT):
                     nc.tensor.matmul_mx(
                         out=y[:, at : at + UNIT],
                         lhsT=wd4_w[:, b, 2 * tile_n * P : 2 * (tile_n + 1) * P].bitcast(FP4X4),
-                        lhsT_scale=wd_s[:, b, rows],
-                        rhs=h_w[group][:, j0 + at : j0 + at + UNIT].bitcast(FP8X4),
-                        rhs_scale=h_s[group][:, j0 + at : j0 + at + UNIT],
+                        lhsT_scale=wd4_s[:, b, rows],
+                        rhs=h_w[b, span][:, j0 + at : j0 + at + UNIT].bitcast(FP8X4),
+                        rhs_scale=h_s[b, span][:, j0 + at : j0 + at + UNIT],
                         start=(b == 0 and at == 0),
                         stop=False,
                     )
                 nc.tensor.matmul_mx(
                     out=y[:],
-                    lhsT=wd8_w[:, b, rows].bitcast(FP8X4),
-                    lhsT_scale=wd_s[WD8_ROW:P, b, rows],
-                    rhs=h_w[group][:, j0 : j0 + width].bitcast(FP8X4),
-                    rhs_scale=h_s[group][:, j0 : j0 + width],
+                    lhsT=wd8_w[b][:, rows].bitcast(FP8X4),
+                    lhsT_scale=wd8_s[WD8_ROW:P, b, rows],
+                    rhs=h_w[b, span][:, j0 : j0 + width].bitcast(FP8X4),
+                    rhs_scale=h_s[b, span][:, j0 : j0 + width],
                     start=False,
                     stop=(b == HALVES - 1),
                 )
-            result = sbuf("result_last%d" % j0, [P, width], F32)
-            nc.vector.tensor_tensor(result[:], y[:], res_sb[span][:, tile_n, j0 : j0 + width], ADD)
-            nc.sync.dma_start(out[rows, span * SPAN + j0 : span * SPAN + j0 + width], result[:])
+            finish(y, span, tile_n, j0, width)
 
-        first_span_steps = [(b, tile_n) for b in range(HALVES) for tile_n in (0, 1)]
-        first_span_steps.extend([(b, tile_n) for tile_n in (2, 3) for b in range(HALVES)])
-        last_gate_unit = len(UNITS) - GATE_LEAD - 1
-        third_group_end = 3 * UNITS_PER_GROUP - 1
-        step_units = [last_gate_unit, last_gate_unit + 1, third_group_end]
-        step_units.extend(range(third_group_end, len(UNITS) - 1))
-
-        for u in range(GATE_LEAD):
-            gate(u)
-        for u in range(len(UNITS)):
-            up(u)
-            done, rest = divmod(u + 1 - QUANTIZE_LAG, UNITS_PER_GROUP)
-            if done > 0 and rest == 0:
-                quantize_h(done - 1, 0, SPAN)
-            if u + GATE_LEAD < len(UNITS):
-                gate(u + GATE_LEAD)
-            if u == len(UNITS) - 1:
-                quantize_h(GROUPS - 1, 0, SPAN // 2)
-                quantize_h(GROUPS - 1, SPAN // 2, SPAN)
-            for after, step in zip(step_units, first_span_steps):
-                if after == u:
-                    down(*step)
-        for tile_n in range(N // P - 1):
-            down(GROUPS - 2, tile_n)
-        down(*first_span_steps[-1])
-        for tile_n in range(N // P - 1):
-            down(GROUPS - 1, tile_n)
-        for j0 in range(0, SPAN, LAST_WIDTH):
-            last_tile(j0)
+        for g in range(6):
+            gate(g, g)
+        round_wu(0, nc.vector.tensor_copy)
+        round_wu(1, nc.vector.tensor_copy)
+        reorder_wg_words(1)
+        quantize_wu(0)
+        gather_last()
+        gate(8, 0)
+        gate(9, 1)
+        round_wu(2, gpsimd_round, 0, 32)
+        round_wu(2, nc.scalar.copy, 32, 64)
+        round_wu(3, gpsimd_round)
+        up(0, 6)
+        up(1, 7)
+        for u in range(2, 5):
+            up(u, u)
+        quantize_wu(1)
+        quantize_h(0, 0)
+        up(5, 5)
+        gate(10, 6)
+        gate(11, 7)
+        gate(6, 0)
+        gate(7, 1)
+        gate(12, 2)
+        gate(13, 3)
+        gate(14, 6)
+        gate(15, 4)
+        up(8, 7)
+        up(9, 0)
+        up(10, 1)
+        up(11, 2)
+        quantize_h(1, 0, 0, SPAN // 2)
+        quantize_h(1, 0, SPAN // 2, SPAN)
+        up(6, 0)
+        up(7, 1)
+        down(0, 0, 0, 5)
+        down(0, 0, 1, 3)
+        down(0, 0, 2, 7)
+        down(0, 0, 3, 6)
+        down(1, 0, 0)
+        up(12, 2)
+        quantize_h(0, 1)
+        down(1, 0, 1)
+        up(13, 4)
+        up(14, 0)
+        down(1, 0, 2)
+        up(15, 1)
+        quantize_h(1, 1, 0, SPAN // 2)
+        quantize_h(1, 1, SPAN // 2, SPAN)
+        down(1, 0, 3)
+        down(0, 1, 0, 5)
+        down(0, 1, 1, 3)
+        down(0, 1, 2, 2)
+        down(1, 1, 0)
+        down(1, 1, 1)
+        down(1, 1, 2)
+        last_tile(0, 6)
+        last_tile(LAST_WIDTH, 5)

@@ -28,7 +28,7 @@ SLICE = 256
 UNIT = 128
 SPAN = 512
 SPANS = J // SPAN
-WU_CHUNK = 256
+WU_CHUNKS = [(0, 320), (320, 512), (512, 768), (768, 1024)]
 WG_ROW = 4
 WD8_ROW = 4
 LAST_WIDTH = SPAN // 2
@@ -41,6 +41,7 @@ def tile_list_gmlpt_gelu_res_res_kernel(
     nc = tc.nc
     with ExitStack() as ctx:
         keep = ctx.enter_context(tc.tile_pool(name="keep", bufs=1))
+        shared = ctx.enter_context(tc.tile_pool(name="shared", bufs=1))
         psum = ctx.enter_context(tc.psum_pool(name="psum", bufs=1))
 
         def sbuf(name, shape, dtype, tag=None):
@@ -53,8 +54,13 @@ def tile_list_gmlpt_gelu_res_res_kernel(
         wg_s_raw = sbuf("wg_s_raw", [P, PASS], U8)
         wg_w = [sbuf("wg_w%d" % b, [P, PACK, P], I32) for b in range(HALVES)]
         wg_s = sbuf("wg_s", [P, PACK, P], U8)
-        wu_raw = [sbuf("wu_raw%d" % c, [P, PACK, WU_CHUNK], F32) for c in range(R // WU_CHUNK)]
-        wu_bf = [sbuf("wu_bf%d" % b, [P, PACK, P, PACK], BF16) for b in range(HALVES)]
+        gate_bytes = 4 * PACK * SLICE
+        first_bytes = 4 * PACK * WU_CHUNKS[0][1]
+        gate_offsets = {0: 0, 2: gate_bytes + first_bytes - 128}
+        wu_raw = [shared.tile([P, PACK, WU_CHUNKS[0][1]], F32, name="wu_raw0", align_bytes=64, offset=gate_bytes - 64)]
+        for c, (c0, c1) in enumerate(WU_CHUNKS[1:]):
+            wu_raw.append(sbuf("wu_raw%d" % (c + 1), [P, PACK, c1 - c0], F32))
+        wu_bf = [sbuf("wu_bf0", [P, PACK, P, PACK], BF16)]
         wu_w = [sbuf("wu_w%d" % b, [P, PASS], U32) for b in range(HALVES)]
         wu_s = [sbuf("wu_s%d" % b, [P, PASS], U8) for b in range(HALVES)]
         wd4_w = sbuf("wd4_w", [P, HALVES, 2 * N], U8)
@@ -80,7 +86,7 @@ def tile_list_gmlpt_gelu_res_res_kernel(
 
         def load_wu(c):
             src = wu.rearrange("(p i) r -> p i r", i=PACK)
-            nc.sync.dma_start(wu_raw[c][:], src[:, :, c * WU_CHUNK : (c + 1) * WU_CHUNK])
+            nc.sync.dma_start(wu_raw[c][:], src[:, :, WU_CHUNKS[c][0] : WU_CHUNKS[c][1]])
 
         def load_wd_scales(engine, wd_s, scales, row):
             for block in range(BLOCKS):
@@ -127,11 +133,11 @@ def tile_list_gmlpt_gelu_res_res_kernel(
             src = wg_w_raw[b][:].rearrange("p (m t) -> p m t", t=PACK)
             nc.vector.tensor_copy(wg_w[b][:].rearrange("p t m -> p m t"), src)
 
-        def round_wu(c, copy, m0=0, m1=WU_CHUNK // PACK):
-            b, part = divmod(c, PASS // WU_CHUNK)
-            first = part * WU_CHUNK // PACK
-            dst = wu_bf[b][:, :, first + m0 : first + m1, :].rearrange("p t m i -> p m t i")
-            copy(dst, wu_raw[c][:, :, PACK * m0 : PACK * m1].rearrange("p i (m t) -> p m t i", t=PACK))
+        def round_wu(c, copy, c0, c1):
+            b, first = divmod(c0, PASS)
+            at = c0 - WU_CHUNKS[c][0]
+            dst = wu_bf[b][:, :, first // PACK : (first + c1 - c0) // PACK, :].rearrange("p t m i -> p m t i")
+            copy(dst, wu_raw[c][:, :, at : at + c1 - c0].rearrange("p i (m t) -> p m t i", t=PACK))
 
         def quantize_wu(b):
             nc.vector.quantize_mx(
@@ -148,20 +154,13 @@ def tile_list_gmlpt_gelu_res_res_kernel(
             nc.vector.tensor_copy(v_s[:, j0 : j0 + SPAN], tab_s[:].indirect(entries(j0, j0 + SPAN)))
         gather_words(v_first[:], 0)
         nc.vector.tensor_copy(wg_s[:], wg_s_raw[:].rearrange("p (m t) -> p t m", t=PACK))
-        v_rest = sbuf("v_rest", [P, J - 2 * SLICE], U32, "wg_s_raw")
-        for j0 in range(SLICE, J - SLICE, SLICE):
+        v_rest = sbuf("v_rest", [P, J - SLICE], U32, "wg_s_raw")
+        for j0 in range(SLICE, J, SLICE):
             gather_words(v_rest[:, j0 - SLICE : j0], j0)
-        v_last = []
-
-        def gather_last():
-            v_last.append(sbuf("v_last", [P, SLICE], U32, "wu_bf0"))
-            gather_words(v_last[0][:], J - SLICE)
 
         def words(j0, width):
             if j0 < SLICE:
                 return v_first[:, j0 : j0 + width].bitcast(FP8X4)
-            if j0 >= J - SLICE:
-                return v_last[0][:, j0 - (J - SLICE) : j0 - (J - SLICE) + width].bitcast(FP8X4)
             return v_rest[:, j0 - SLICE : j0 - SLICE + width].bitcast(FP8X4)
 
         def scales(j0, width):
@@ -186,7 +185,11 @@ def tile_list_gmlpt_gelu_res_res_kernel(
                     start=True,
                     stop=True,
                 )
-            if pair == 0:
+            if g in gate_offsets:
+                gates[b, s] = shared.tile(
+                    [P, 2, SLICE, 2], F32, name="gate%d%d" % (b, s), align_bytes=64, offset=gate_offsets[g]
+                )
+            elif pair == 0:
                 gates[b, s] = sbuf("gate%d%d" % (b, s), [P, 2, SLICE, 2], F32)
             nc.scalar.activation(gates[b, s][:, pair, :, :], ga[:].rearrange("p e j -> p j e"), GELU)
 
@@ -294,61 +297,58 @@ def tile_list_gmlpt_gelu_res_res_kernel(
                 )
             finish(y, span, tile_n, j0, width)
 
-        for g in range(6):
+        round_wu(0, nc.scalar.copy, 0, 320)
+        round_wu(1, nc.scalar.copy, 320, 384)
+        round_wu(1, gpsimd_round, 384, 512)
+        for g in range(8):
             gate(g, g)
-        round_wu(0, nc.vector.tensor_copy)
-        round_wu(1, nc.vector.tensor_copy)
-        reorder_wg_words(1)
         quantize_wu(0)
-        gather_last()
-        gate(8, 0)
-        gate(9, 1)
-        round_wu(2, gpsimd_round, 0, 32)
-        round_wu(2, nc.scalar.copy, 32, 64)
-        round_wu(3, gpsimd_round)
-        up(0, 6)
-        up(1, 7)
-        for u in range(2, 5):
+        reorder_wg_words(1)
+        wu_bf.append(sbuf("wu_bf1", [P, PACK, P, PACK], BF16, "wu_bf0"))
+        round_wu(2, gpsimd_round, 512, 768)
+        round_wu(3, gpsimd_round, 768, 1024)
+        for u in range(4):
             up(u, u)
+        up(4, 0)
         quantize_wu(1)
         quantize_h(0, 0)
-        up(5, 5)
-        gate(10, 6)
-        gate(11, 7)
-        gate(6, 0)
-        gate(7, 1)
-        gate(12, 2)
-        gate(13, 3)
-        gate(14, 6)
+        gate(8, 4)
+        up(5, 1)
+        gate(9, 5)
+        gate(10, 2)
+        gate(11, 6)
+        gate(12, 3)
+        gate(13, 7)
+        gate(14, 0)
         gate(15, 4)
-        up(8, 7)
-        up(9, 0)
-        up(10, 1)
-        up(11, 2)
+        up(8, 5)
+        up(9, 2)
+        up(10, 6)
+        up(11, 3)
         quantize_h(1, 0, 0, SPAN // 2)
         quantize_h(1, 0, SPAN // 2, SPAN)
-        up(6, 0)
-        up(7, 1)
-        down(0, 0, 0, 5)
-        down(0, 0, 1, 3)
+        up(6, 2)
+        up(7, 6)
+        down(0, 0, 0, 1)
+        down(0, 0, 1, 5)
         down(0, 0, 2, 7)
-        down(0, 0, 3, 6)
+        down(0, 0, 3, 0)
         down(1, 0, 0)
-        up(12, 2)
+        up(12, 3)
         quantize_h(0, 1)
         down(1, 0, 1)
         up(13, 4)
-        up(14, 0)
+        up(14, 2)
         down(1, 0, 2)
-        up(15, 1)
+        up(15, 6)
         quantize_h(1, 1, 0, SPAN // 2)
         quantize_h(1, 1, SPAN // 2, SPAN)
         down(1, 0, 3)
-        down(0, 1, 0, 5)
-        down(0, 1, 1, 3)
-        down(0, 1, 2, 2)
+        down(0, 1, 0, 1)
+        down(0, 1, 1, 5)
+        down(0, 1, 2, 3)
         down(1, 1, 0)
         down(1, 1, 1)
         down(1, 1, 2)
-        last_tile(0, 6)
-        last_tile(LAST_WIDTH, 5)
+        last_tile(0, 0)
+        last_tile(LAST_WIDTH, 1)

@@ -53,7 +53,6 @@ def tile_list_gmlpt_gelu_res_res_kernel(
         wg_w_raw = [sbuf("wg_w_raw%d" % b, [P, PASS], I32) for b in range(HALVES)]
         wg_s_raw = sbuf("wg_s_raw", [P, PASS], U8)
         wg_w = [sbuf("wg_w%d" % b, [P, PACK, P], I32) for b in range(HALVES)]
-        wg_s = sbuf("wg_s", [P, PACK, P], U8)
         gate_bytes = 4 * PACK * SLICE
         first_bytes = 4 * PACK * WU_CHUNKS[0][1]
         gate_offsets = {0: 0, 2: gate_bytes + first_bytes - 128}
@@ -69,7 +68,7 @@ def tile_list_gmlpt_gelu_res_res_kernel(
         wd8_s = sbuf("wd8_s", [P, HALVES, N], U8)
         res_sb = [sbuf("res%d" % span, [P, N // P, SPAN], F32) for span in range(SPANS)]
         v_s = sbuf("v_s", [P, J], U8)
-        v_first = sbuf("v_first", [P, SLICE], U32)
+        v_w = sbuf("v_w", [P, J], U32)
         h_bf = {}
         h_w = {}
         h_s = {}
@@ -93,24 +92,28 @@ def tile_list_gmlpt_gelu_res_res_kernel(
                 src = scales.rearrange("a (quad block) n -> block quad a n", block=BLOCKS)[block]
                 engine.dma_start(wd_s[row + block : P : QUADRANT, :, :].bitcast(I32), src.bitcast(I32))
 
+        def load_wg_scales(engine, quad):
+            src = wg_scales[0][BLOCKS * quad : BLOCKS * (quad + 1), :].rearrange("block (b c) -> b block c", b=HALVES)
+            partition = QUADRANT * quad + WG_ROW
+            engine.dma_start(wg_s_raw[partition : partition + BLOCKS * HALVES, :].bitcast(I32), src.bitcast(I32))
+
         def load_wd8(b):
             nc.sync.dma_start(wd8_w[b][:].bitcast(I32), wd8_words[b].rearrange("p n i -> p (n i)").bitcast(I32))
 
-        nc.vector.memset(tab_s[:].bitcast(I32), 0)
         nc.vector.memset(wg_s_raw[:].bitcast(I32), 0)
+        nc.vector.memset(tab_s[:].bitcast(I32), 0)
         nc.vector.memset(wd8_s[:].rearrange("p a n -> p (a n)").bitcast(I32), 0)
         nc.vector.memset(wd4_s[:].rearrange("p a n -> p (a n)").bitcast(I32), 0)
         nc.vector.memset(warm[:, 0, :], 0.0)
         nc.sync.dma_start(offsets[:], offs)
+        for quad, engine in enumerate((nc.scalar, nc.sync, nc.gpsimd)):
+            load_wg_scales(engine, quad)
         load_wg(0)
-        for block, engine in enumerate((nc.sync, nc.scalar, nc.sync, nc.scalar)):
+        for block, engine in enumerate((nc.scalar, nc.scalar, nc.sync, nc.scalar)):
             src = tab_scales[0].rearrange("(quad block) col -> block quad col", block=BLOCKS)[block]
             engine.dma_start(tab_s[block:P:QUADRANT, :].bitcast(I32), src.bitcast(I32))
+        load_wg_scales(nc.sync, 3)
         nc.sync.dma_start(tab_w[:].bitcast(I32), tab_words[0].rearrange("p col i -> p (col i)").bitcast(I32))
-        for quad in range(P // QUADRANT):
-            src = wg_scales[0][BLOCKS * quad : BLOCKS * (quad + 1), :].rearrange("block (b c) -> b block c", b=HALVES)
-            partition = QUADRANT * quad + WG_ROW
-            nc.sync.dma_start(wg_s_raw[partition : partition + BLOCKS * HALVES, :].bitcast(I32), src.bitcast(I32))
         load_wd_scales(nc.gpsimd, wd8_s, wd8_scales, WD8_ROW)
         nc.scalar.activation(warm[:, 1, :], warm[:, 0, :], GELU)
         load_wu(0)
@@ -152,16 +155,13 @@ def tile_list_gmlpt_gelu_res_res_kernel(
         reorder_wg_words(0)
         for j0 in range(0, J, SPAN):
             nc.vector.tensor_copy(v_s[:, j0 : j0 + SPAN], tab_s[:].indirect(entries(j0, j0 + SPAN)))
-        gather_words(v_first[:], 0)
+        wg_s = sbuf("wg_s", [P, PACK, P], U8, "tab_s")
         nc.vector.tensor_copy(wg_s[:], wg_s_raw[:].rearrange("p (m t) -> p t m", t=PACK))
-        v_rest = sbuf("v_rest", [P, J - SLICE], U32, "wg_s_raw")
-        for j0 in range(SLICE, J, SLICE):
-            gather_words(v_rest[:, j0 - SLICE : j0], j0)
+        for j0 in range(0, J, SLICE):
+            gather_words(v_w[:, j0 : j0 + SLICE], j0)
 
         def words(j0, width):
-            if j0 < SLICE:
-                return v_first[:, j0 : j0 + width].bitcast(FP8X4)
-            return v_rest[:, j0 - SLICE : j0 - SLICE + width].bitcast(FP8X4)
+            return v_w[:, j0 : j0 + width].bitcast(FP8X4)
 
         def scales(j0, width):
             return v_s[:, j0 : j0 + width]

@@ -28,11 +28,11 @@ SLICE = 256
 UNIT = 128
 SPAN = 512
 SPANS = J // SPAN
-WU_CHUNKS = [(0, 320), (320, 512), (512, 768), (768, 1024)]
+WU_CHUNKS = [(0, 304), (304, 512), (512, 768), (768, 1024)]
 WG_ROW = 4
 WD8_ROW = 4
 LAST_WIDTH = SPAN // 2
-GPSIMD_ADDS = [(0, 0), (0, 1)]
+GPSIMD_ADDS = {(0, 0): [(0, 512, "h_bf01")]}
 
 
 def tile_list_gmlpt_gelu_res_res_kernel(
@@ -54,11 +54,18 @@ def tile_list_gmlpt_gelu_res_res_kernel(
         wg_s_raw = sbuf("wg_s_raw", [P, PASS], U8)
         wg_w = [sbuf("wg_w%d" % b, [P, PACK, P], I32) for b in range(HALVES)]
         gate_bytes = 4 * PACK * SLICE
-        first_bytes = 4 * PACK * WU_CHUNKS[0][1]
-        gate_offsets = {0: 0, 2: gate_bytes + first_bytes - 128}
-        wu_raw = [shared.tile([P, PACK, WU_CHUNKS[0][1]], F32, name="wu_raw0", align_bytes=64, offset=gate_bytes - 64)]
-        for c, (c0, c1) in enumerate(WU_CHUNKS[1:]):
-            wu_raw.append(sbuf("wu_raw%d" % (c + 1), [P, PACK, c1 - c0], F32))
+        gate_offsets = {}
+        wu_raw = []
+        place = 0
+        for c, (c0, c1) in enumerate(WU_CHUNKS[:2]):
+            gate_offsets[4 * c] = place
+            wu_raw.append(
+                shared.tile([P, PACK, c1 - c0], F32, name="wu_raw%d" % c, align_bytes=64, offset=place + gate_bytes - 64)
+            )
+            gate_offsets[4 * c + 2] = place + gate_bytes + 4 * PACK * (c1 - c0) - 128
+            place = gate_offsets[4 * c + 2] + gate_bytes
+        for c, (c0, c1) in enumerate(WU_CHUNKS[2:]):
+            wu_raw.append(sbuf("wu_raw%d" % (c + 2), [P, PACK, c1 - c0], F32))
         wu_bf = [sbuf("wu_bf0", [P, PACK, P, PACK], BF16)]
         wu_w = [sbuf("wu_w%d" % b, [P, PASS], U32) for b in range(HALVES)]
         wu_s = [sbuf("wu_s%d" % b, [P, PASS], U8) for b in range(HALVES)]
@@ -87,8 +94,8 @@ def tile_list_gmlpt_gelu_res_res_kernel(
             src = wu.rearrange("(p i) r -> p i r", i=PACK)
             nc.sync.dma_start(wu_raw[c][:], src[:, :, WU_CHUNKS[c][0] : WU_CHUNKS[c][1]])
 
-        def load_wd_scales(engine, wd_s, scales, row):
-            for block in range(BLOCKS):
+        def load_wd_scales(engines, wd_s, scales, row):
+            for block, engine in enumerate(engines):
                 src = scales.rearrange("a (quad block) n -> block quad a n", block=BLOCKS)[block]
                 engine.dma_start(wd_s[row + block : P : QUADRANT, :, :].bitcast(I32), src.bitcast(I32))
 
@@ -114,8 +121,8 @@ def tile_list_gmlpt_gelu_res_res_kernel(
             engine.dma_start(tab_s[block:P:QUADRANT, :].bitcast(I32), src.bitcast(I32))
         load_wg_scales(nc.sync, 3)
         nc.sync.dma_start(tab_w[:].bitcast(I32), tab_words[0].rearrange("p col i -> p (col i)").bitcast(I32))
-        load_wd_scales(nc.gpsimd, wd8_s, wd8_scales, WD8_ROW)
         nc.scalar.activation(warm[:, 1, :], warm[:, 0, :], GELU)
+        load_wd_scales((nc.gpsimd, nc.gpsimd, nc.scalar, nc.scalar), wd8_s, wd8_scales, WD8_ROW)
         load_wu(0)
         load_wu(1)
         load_wg(1)
@@ -123,7 +130,7 @@ def tile_list_gmlpt_gelu_res_res_kernel(
         load_wu(3)
         load_wd8(0)
         nc.sync.dma_start(wd4_w[:].bitcast(I32), wd4_words.rearrange("a p c -> p a c").bitcast(I32))
-        load_wd_scales(nc.sync, wd4_s, wd4_scales, 0)
+        load_wd_scales((nc.sync,) * BLOCKS, wd4_s, wd4_scales, 0)
         load_wd8(1)
         for span in range(SPANS):
             src = res.rearrange("(tile p) j -> p tile j", p=P)
@@ -136,11 +143,11 @@ def tile_list_gmlpt_gelu_res_res_kernel(
             src = wg_w_raw[b][:].rearrange("p (m t) -> p m t", t=PACK)
             nc.vector.tensor_copy(wg_w[b][:].rearrange("p t m -> p m t"), src)
 
-        def round_wu(c, copy, c0, c1):
+        def round_wu(c, copy, c0, c1, walk="m i t"):
             b, first = divmod(c0, PASS)
             at = c0 - WU_CHUNKS[c][0]
-            dst = wu_bf[b][:, :, first // PACK : (first + c1 - c0) // PACK, :].rearrange("p t m i -> p m t i")
-            copy(dst, wu_raw[c][:, :, at : at + c1 - c0].rearrange("p i (m t) -> p m t i", t=PACK))
+            dst = wu_bf[b][:, :, first // PACK : (first + c1 - c0) // PACK, :].rearrange("p t m i -> p " + walk)
+            copy(dst, wu_raw[c][:, :, at : at + c1 - c0].rearrange("p i (m t) -> p " + walk, t=PACK))
 
         def quantize_wu(b):
             nc.vector.quantize_mx(
@@ -221,7 +228,7 @@ def tile_list_gmlpt_gelu_res_res_kernel(
             )
 
         sums = {}
-        late = []
+        late = {}
 
         def finish(y, span, tile_n, j0, width):
             at = span * SPAN + j0
@@ -229,11 +236,12 @@ def tile_list_gmlpt_gelu_res_res_kernel(
             if (span, tile_n) in GPSIMD_ADDS:
                 y_sb = sbuf("y_sb%d" % tile_n, [P, width], F32)
                 nc.scalar.copy(y_sb[:], y[:])
-                if not late:
-                    late.append(sbuf("late", [P, len(GPSIMD_ADDS), width], F32, "h_bf01"))
-                result = late[0][:, GPSIMD_ADDS.index((span, tile_n)), :]
-                nc.gpsimd.tensor_tensor(result, y_sb[:], res_part, ADD)
-                nc.sync.dma_start(out[tile_n * P : (tile_n + 1) * P, at : at + width], result)
+                for at0, at1, tag in GPSIMD_ADDS[span, tile_n]:
+                    if tag not in late:
+                        late[tag] = sbuf("late_" + tag, [P, 2, SPAN], F32, tag)
+                    piece = late[tag][:, tile_n, at0:at1]
+                    nc.gpsimd.tensor_tensor(piece, y_sb[:, at0:at1], res_part[:, at0:at1], ADD)
+                    nc.sync.dma_start(out[tile_n * P : (tile_n + 1) * P, at + at0 : at + at1], piece)
                 return
             result = sbuf("result%d_%d_%d" % (span, tile_n, j0), [P, width], F32)
             nc.vector.tensor_tensor(result[:], y[:], res_part, ADD)
@@ -297,16 +305,15 @@ def tile_list_gmlpt_gelu_res_res_kernel(
                 )
             finish(y, span, tile_n, j0, width)
 
-        round_wu(0, nc.scalar.copy, 0, 320)
-        round_wu(1, nc.scalar.copy, 320, 384)
-        round_wu(1, gpsimd_round, 384, 512)
+        round_wu(0, nc.scalar.copy, 0, 304)
+        round_wu(1, nc.vector.tensor_copy, 304, 512)
         for g in range(8):
             gate(g, g)
-        quantize_wu(0)
         reorder_wg_words(1)
+        quantize_wu(0)
         wu_bf.append(sbuf("wu_bf1", [P, PACK, P, PACK], BF16, "wu_bf0"))
-        round_wu(2, gpsimd_round, 512, 768)
-        round_wu(3, gpsimd_round, 768, 1024)
+        round_wu(2, gpsimd_round, 512, 768, "m t i")
+        round_wu(3, gpsimd_round, 768, 1024, "m t i")
         for u in range(4):
             up(u, u)
         up(4, 0)
@@ -339,10 +346,10 @@ def tile_list_gmlpt_gelu_res_res_kernel(
         down(1, 0, 1)
         up(13, 4)
         up(14, 2)
-        down(1, 0, 2)
         up(15, 6)
         quantize_h(1, 1, 0, SPAN // 2)
         quantize_h(1, 1, SPAN // 2, SPAN)
+        down(1, 0, 2)
         down(1, 0, 3)
         down(0, 1, 0, 1)
         down(0, 1, 1, 5)

@@ -24,15 +24,18 @@ HALVES = R // PASS
 QUADRANT = 32
 BLOCKS = 4
 LIST_ROWS = 16
+BANKS = 8
 SLICE = 256
 UNIT = 128
 SPAN = 512
-SPANS = J // SPAN
-WU_CHUNKS = [(0, 304), (304, 512), (512, 768), (768, 1024)]
+TILES = N // P
+PER_HALF = J // UNIT
+WU_CHUNK = 256
 WG_ROW = 4
 WD8_ROW = 4
+SCALAR_COLUMNS = 64
+GPSIMD_UNIT = 6
 LAST_WIDTH = SPAN // 2
-GPSIMD_ADDS = {(0, 0): [(0, 512, "h_bf01")]}
 
 
 def tile_list_gmlpt_gelu_res_res_kernel(
@@ -41,7 +44,6 @@ def tile_list_gmlpt_gelu_res_res_kernel(
     nc = tc.nc
     with ExitStack() as ctx:
         keep = ctx.enter_context(tc.tile_pool(name="keep", bufs=1))
-        shared = ctx.enter_context(tc.tile_pool(name="shared", bufs=1))
         psum = ctx.enter_context(tc.psum_pool(name="psum", bufs=1))
 
         def sbuf(name, shape, dtype, tag=None):
@@ -53,37 +55,21 @@ def tile_list_gmlpt_gelu_res_res_kernel(
         wg_w_raw = [sbuf("wg_w_raw%d" % b, [P, PASS], I32) for b in range(HALVES)]
         wg_s_raw = sbuf("wg_s_raw", [P, PASS], U8)
         wg_w = [sbuf("wg_w%d" % b, [P, PACK, P], I32) for b in range(HALVES)]
-        gate_bytes = 4 * PACK * SLICE
-        gate_offsets = {}
-        wu_raw = []
-        place = 0
-        for c, (c0, c1) in enumerate(WU_CHUNKS[:2]):
-            gate_offsets[4 * c] = place
-            wu_raw.append(
-                shared.tile([P, PACK, c1 - c0], F32, name="wu_raw%d" % c, align_bytes=64, offset=place + gate_bytes - 64)
-            )
-            gate_offsets[4 * c + 2] = place + gate_bytes + 4 * PACK * (c1 - c0) - 128
-            place = gate_offsets[4 * c + 2] + gate_bytes
-        for c, (c0, c1) in enumerate(WU_CHUNKS[2:]):
-            wu_raw.append(sbuf("wu_raw%d" % (c + 2), [P, PACK, c1 - c0], F32))
-        wu_bf = [sbuf("wu_bf0", [P, PACK, P, PACK], BF16)]
+        wg_s = sbuf("wg_s", [P, PACK, P], U8)
+        wu_raw = [sbuf("wu_raw%d" % c, [P, PACK, WU_CHUNK], F32) for c in range(R // WU_CHUNK)]
         wu_w = [sbuf("wu_w%d" % b, [P, PASS], U32) for b in range(HALVES)]
         wu_s = [sbuf("wu_s%d" % b, [P, PASS], U8) for b in range(HALVES)]
         wd4_w = sbuf("wd4_w", [P, HALVES, 2 * N], U8)
         wd8_w = [sbuf("wd8_w%d" % b, [P, N], U32) for b in range(HALVES)]
         wd4_s = sbuf("wd4_s", [P, HALVES, N], U8)
         wd8_s = sbuf("wd8_s", [P, HALVES, N], U8)
-        res_sb = [sbuf("res%d" % span, [P, N // P, SPAN], F32) for span in range(SPANS)]
+        res_sb = [sbuf("res%d" % span, [P, TILES, SPAN], F32) for span in range(J // SPAN)]
         v_s = sbuf("v_s", [P, J], U8)
         v_w = sbuf("v_w", [P, J], U32)
-        h_bf = {}
-        h_w = {}
-        h_s = {}
-        for b in range(HALVES):
-            for span in range(SPANS):
-                h_bf[b, span] = sbuf("h_bf%d%d" % (b, span), [P, SPAN, PACK], BF16)
-                h_w[b, span] = sbuf("h_w%d%d" % (b, span), [P, SPAN], U32)
-                h_s[b, span] = sbuf("h_s%d%d" % (b, span), [P, SPAN], U8)
+        groups = [(b, span) for b in range(HALVES) for span in range(J // SPAN)]
+        h_bf = {g: sbuf("h_bf%d%d" % g, [P, SPAN, PACK], BF16) for g in groups}
+        h_w = {g: sbuf("h_w%d%d" % g, [P, SPAN], U32) for g in groups}
+        h_s = {g: sbuf("h_s%d%d" % g, [P, SPAN], U8) for g in groups}
         warm = sbuf("warm", [P, 2, 8], F32)
 
         def load_wg(b):
@@ -92,20 +78,20 @@ def tile_list_gmlpt_gelu_res_res_kernel(
 
         def load_wu(c):
             src = wu.rearrange("(p i) r -> p i r", i=PACK)
-            nc.sync.dma_start(wu_raw[c][:], src[:, :, WU_CHUNKS[c][0] : WU_CHUNKS[c][1]])
+            nc.sync.dma_start(wu_raw[c][:], src[:, :, c * WU_CHUNK : (c + 1) * WU_CHUNK])
 
-        def load_wd_scales(engines, wd_s, scales, row):
-            for block, engine in enumerate(engines):
-                src = scales.rearrange("a (quad block) n -> block quad a n", block=BLOCKS)[block]
-                engine.dma_start(wd_s[row + block : P : QUADRANT, :, :].bitcast(I32), src.bitcast(I32))
+        def load_wd8(b):
+            nc.sync.dma_start(wd8_w[b][:].bitcast(I32), wd8_words[b].rearrange("p n i -> p (n i)").bitcast(I32))
 
         def load_wg_scales(engine, quad):
             src = wg_scales[0][BLOCKS * quad : BLOCKS * (quad + 1), :].rearrange("block (b c) -> b block c", b=HALVES)
             partition = QUADRANT * quad + WG_ROW
             engine.dma_start(wg_s_raw[partition : partition + BLOCKS * HALVES, :].bitcast(I32), src.bitcast(I32))
 
-        def load_wd8(b):
-            nc.sync.dma_start(wd8_w[b][:].bitcast(I32), wd8_words[b].rearrange("p n i -> p (n i)").bitcast(I32))
+        def load_wd_scales(engines, wd_s, scales, row):
+            for block, engine in enumerate(engines):
+                src = scales.rearrange("a (quad block) n -> block quad a n", block=BLOCKS)[block]
+                engine.dma_start(wd_s[row + block : P : QUADRANT, :, :].bitcast(I32), src.bitcast(I32))
 
         nc.vector.memset(wg_s_raw[:].bitcast(I32), 0)
         nc.vector.memset(tab_s[:].bitcast(I32), 0)
@@ -119,7 +105,7 @@ def tile_list_gmlpt_gelu_res_res_kernel(
         for block, engine in enumerate((nc.scalar, nc.scalar, nc.sync, nc.scalar)):
             src = tab_scales[0].rearrange("(quad block) col -> block quad col", block=BLOCKS)[block]
             engine.dma_start(tab_s[block:P:QUADRANT, :].bitcast(I32), src.bitcast(I32))
-        load_wg_scales(nc.sync, 3)
+        load_wg_scales(nc.sync, P // QUADRANT - 1)
         nc.sync.dma_start(tab_w[:].bitcast(I32), tab_words[0].rearrange("p col i -> p (col i)").bitcast(I32))
         nc.scalar.activation(warm[:, 1, :], warm[:, 0, :], GELU)
         load_wd_scales((nc.gpsimd, nc.gpsimd, nc.scalar, nc.scalar), wd8_s, wd8_scales, WD8_ROW)
@@ -132,127 +118,109 @@ def tile_list_gmlpt_gelu_res_res_kernel(
         nc.sync.dma_start(wd4_w[:].bitcast(I32), wd4_words.rearrange("a p c -> p a c").bitcast(I32))
         load_wd_scales((nc.sync,) * BLOCKS, wd4_s, wd4_scales, 0)
         load_wd8(1)
-        for span in range(SPANS):
+        for span in range(J // SPAN):
             src = res.rearrange("(tile p) j -> p tile j", p=P)
             nc.sync.dma_start(res_sb[span][:], src[:, :, span * SPAN : (span + 1) * SPAN])
 
-        def entries(j0, j1):
-            return offsets[:, j0 // LIST_ROWS : j1 // LIST_ROWS]
+        def gather(dst, table, width):
+            for j0 in range(0, J, width):
+                entries = offsets[:, j0 // LIST_ROWS : (j0 + width) // LIST_ROWS]
+                nc.vector.tensor_copy(dst[:, j0 : j0 + width], table[:].indirect(entries))
 
         def reorder_wg_words(b):
             src = wg_w_raw[b][:].rearrange("p (m t) -> p m t", t=PACK)
             nc.vector.tensor_copy(wg_w[b][:].rearrange("p t m -> p m t"), src)
 
-        def round_wu(c, copy, c0, c1, walk="m i t"):
-            b, first = divmod(c0, PASS)
-            at = c0 - WU_CHUNKS[c][0]
-            dst = wu_bf[b][:, :, first // PACK : (first + c1 - c0) // PACK, :].rearrange("p t m i -> p " + walk)
-            copy(dst, wu_raw[c][:, :, at : at + c1 - c0].rearrange("p i (m t) -> p " + walk, t=PACK))
+        def rounding(wu_bf, c0, c1, walk):
+            c, at = divmod(c0, WU_CHUNK)
+            first = c0 % PASS // PACK
+            dst = wu_bf[:, :, first : first + (c1 - c0) // PACK, :].rearrange("p t m i -> p " + walk)
+            src = wu_raw[c][:, :, at : at + c1 - c0].rearrange("p i (m t) -> p " + walk, t=PACK)
+            return dst, src
 
-        def quantize_wu(b):
+        def quantize_wu(b, wu_bf):
             nc.vector.quantize_mx(
                 out=wu_w[b][:].bitcast(FP8X4),
                 scales=wu_s[b][:],
-                in_=wu_bf[b][:].rearrange("p t m i -> p (t m i)"),
+                in_=wu_bf[:].rearrange("p t m i -> p (t m i)"),
             )
 
-        def gather_words(dst, j0):
-            nc.vector.tensor_copy(dst, tab_w[:].indirect(entries(j0, j0 + SLICE)))
-
-        reorder_wg_words(0)
-        for j0 in range(0, J, SPAN):
-            nc.vector.tensor_copy(v_s[:, j0 : j0 + SPAN], tab_s[:].indirect(entries(j0, j0 + SPAN)))
-        wg_s = sbuf("wg_s", [P, PACK, P], U8, "tab_s")
-        nc.vector.tensor_copy(wg_s[:], wg_s_raw[:].rearrange("p (m t) -> p t m", t=PACK))
-        for j0 in range(0, J, SLICE):
-            gather_words(v_w[:, j0 : j0 + SLICE], j0)
-
-        def words(j0, width):
-            return v_w[:, j0 : j0 + width].bitcast(FP8X4)
-
-        def scales(j0, width):
-            return v_s[:, j0 : j0 + width]
-
-        def gpsimd_round(dst, src):
-            nc.gpsimd.tensor_scalar(dst, src, 1.0, 0.0, MULT, ADD)
-
+        banks = {}
         gates = {}
+        sums = {}
 
         def gate(g, bank):
-            b, rest = divmod(g, 8)
-            s, pair = divmod(rest, 2)
+            b, rest = divmod(g, PER_HALF)
+            s, pair = divmod(rest, SLICE // UNIT)
+            banks["gate", g] = bank
             ga = psum.tile([P, 2, SLICE], F32, name="ga", tag="bank%d" % bank)
             for e in range(2):
                 nc.tensor.matmul_mx(
                     out=ga[:, e, :],
                     lhsT=wg_w[b][:, 2 * pair + e, :].bitcast(FP8X4),
                     lhsT_scale=wg_s[WG_ROW + BLOCKS * b : P, 2 * pair + e, :],
-                    rhs=words(s * SLICE, SLICE),
-                    rhs_scale=scales(s * SLICE, SLICE),
+                    rhs=v_w[:, s * SLICE : (s + 1) * SLICE].bitcast(FP8X4),
+                    rhs_scale=v_s[:, s * SLICE : (s + 1) * SLICE],
                     start=True,
                     stop=True,
                 )
-            if g in gate_offsets:
-                gates[b, s] = shared.tile(
-                    [P, 2, SLICE, 2], F32, name="gate%d%d" % (b, s), align_bytes=64, offset=gate_offsets[g]
-                )
-            elif pair == 0:
+            if pair == 0:
                 gates[b, s] = sbuf("gate%d%d" % (b, s), [P, 2, SLICE, 2], F32)
             nc.scalar.activation(gates[b, s][:, pair, :, :], ga[:].rearrange("p e j -> p j e"), GELU)
 
         def up(u, bank):
-            b, tile_j = divmod(u, 8)
+            b, tile_j = divmod(u, PER_HALF)
             j0 = tile_j * UNIT
             s, at = divmod(j0, SLICE)
             span, first = divmod(j0, SPAN)
+            banks["up", u] = bank
             ub = psum.tile([P, PACK, UNIT], F32, name="ub", tag="bank%d" % bank)
             for t in range(PACK):
                 nc.tensor.matmul_mx(
                     out=ub[:, t, :],
                     lhsT=wu_w[b][:, t * P : (t + 1) * P].bitcast(FP8X4),
                     lhsT_scale=wu_s[b][:, t * P : (t + 1) * P],
-                    rhs=words(j0, UNIT),
-                    rhs_scale=scales(j0, UNIT),
+                    rhs=v_w[:, j0 : j0 + UNIT].bitcast(FP8X4),
+                    rhs_scale=v_s[:, j0 : j0 + UNIT],
                     start=True,
                     stop=True,
                 )
             h = h_bf[b, span][:, first : first + UNIT, :].rearrange("p j (pair e) -> p j pair e", e=2)
             gelus = gates[b, s][:, :, at : at + UNIT, :].rearrange("p pair j e -> p j pair e")
-            nc.vector.tensor_tensor(h, ub[:].rearrange("p (pair e) j -> p j pair e", e=2), gelus, MULT)
+            if u == GPSIMD_UNIT:
+                ub_sb = sbuf("ub_sb", [P, UNIT, PACK], F32, "wu_bf")
+                nc.scalar.copy(ub_sb[:], ub[:].rearrange("p t j -> p j t"))
+                nc.gpsimd.tensor_tensor(h, ub_sb[:].rearrange("p j (pair e) -> p j pair e", e=2), gelus, MULT)
+            else:
+                nc.vector.tensor_tensor(h, ub[:].rearrange("p (pair e) j -> p j pair e", e=2), gelus, MULT)
 
-        def quantize_h(b, span, j0=0, j1=SPAN):
-            nc.vector.quantize_mx(
-                out=h_w[b, span][:, j0:j1].bitcast(FP8X4),
-                scales=h_s[b, span][:, j0:j1],
-                in_=h_bf[b, span][:, j0:j1, :].rearrange("p j t -> p (j t)"),
-            )
+        def quantize_h(b, span, pieces):
+            width = SPAN // pieces
+            for j0 in range(0, SPAN, width):
+                nc.vector.quantize_mx(
+                    out=h_w[b, span][:, j0 : j0 + width].bitcast(FP8X4),
+                    scales=h_s[b, span][:, j0 : j0 + width],
+                    in_=h_bf[b, span][:, j0 : j0 + width, :].rearrange("p j t -> p (j t)"),
+                )
 
-        sums = {}
-        late = {}
-
-        def finish(y, span, tile_n, j0, width):
-            at = span * SPAN + j0
+        def add_and_store(y, span, tile_n, j0, width):
             res_part = res_sb[span][:, tile_n, j0 : j0 + width]
-            if (span, tile_n) in GPSIMD_ADDS:
-                y_sb = sbuf("y_sb%d" % tile_n, [P, width], F32)
+            if (span, tile_n) == (0, 0):
+                y_sb = sbuf("y_sb", [P, width], F32)
                 nc.scalar.copy(y_sb[:], y[:])
-                for at0, at1, tag in GPSIMD_ADDS[span, tile_n]:
-                    if tag not in late:
-                        late[tag] = sbuf("late_" + tag, [P, 2, SPAN], F32, tag)
-                    piece = late[tag][:, tile_n, at0:at1]
-                    nc.gpsimd.tensor_tensor(piece, y_sb[:, at0:at1], res_part[:, at0:at1], ADD)
-                    nc.sync.dma_start(out[tile_n * P : (tile_n + 1) * P, at + at0 : at + at1], piece)
-                return
-            result = sbuf("result%d_%d_%d" % (span, tile_n, j0), [P, width], F32)
-            nc.vector.tensor_tensor(result[:], y[:], res_part, ADD)
+                result = sbuf("result_first", [P, width], F32, "h_bf01")
+                nc.gpsimd.tensor_tensor(result[:], y_sb[:], res_part, ADD)
+            else:
+                result = sbuf("result%d_%d_%d" % (span, tile_n, j0), [P, width], F32)
+                nc.vector.tensor_tensor(result[:], y[:], res_part, ADD)
+            at = span * SPAN + j0
             nc.sync.dma_start(out[tile_n * P : (tile_n + 1) * P, at : at + width], result[:])
 
-        def down8(b, span, tile_n, bank=None):
-            if b == 0:
-                sums[span, tile_n] = psum.tile([P, SPAN], F32, name="y", tag="bank%d" % bank)
+        def down(b, span, tile_n):
+            y = sums[span, tile_n]
             rows = slice(tile_n * P, (tile_n + 1) * P)
             nc.tensor.matmul_mx(
-                out=sums[span, tile_n][:],
+                out=y[:],
                 lhsT=wd8_w[b][:, rows].bitcast(FP8X4),
                 lhsT_scale=wd8_s[WD8_ROW:P, b, rows],
                 rhs=h_w[b, span][:].bitcast(FP8X4),
@@ -260,11 +228,8 @@ def tile_list_gmlpt_gelu_res_res_kernel(
                 start=(b == 0),
                 stop=False,
             )
-
-        def down4(b, span, tile_n):
-            rows = slice(tile_n * P, (tile_n + 1) * P)
             nc.tensor.matmul_mx(
-                out=sums[span, tile_n][:],
+                out=y[:],
                 lhsT=wd4_w[:, b, 2 * tile_n * P : 2 * (tile_n + 1) * P].bitcast(FP4X4),
                 lhsT_scale=wd4_s[:, b, rows],
                 rhs=h_w[b, span][:].bitcast(FP8X4),
@@ -272,19 +237,22 @@ def tile_list_gmlpt_gelu_res_res_kernel(
                 start=False,
                 stop=(b == HALVES - 1),
             )
-            if b == HALVES - 1:
-                finish(sums[span, tile_n], span, tile_n, 0, SPAN)
 
-        def down(b, span, tile_n, bank=None):
-            down8(b, span, tile_n, bank)
-            down4(b, span, tile_n)
+        def open_sum(span, tile_n, bank):
+            banks["sum", span, tile_n] = bank
+            sums[span, tile_n] = psum.tile([P, SPAN], F32, name="y", tag="bank%d" % bank)
+            down(0, span, tile_n)
+
+        def close_sum(span, tile_n):
+            down(1, span, tile_n)
+            add_and_store(sums[span, tile_n], span, tile_n, 0, SPAN)
 
         def last_tile(j0, bank):
-            span, tile_n, width = SPANS - 1, N // P - 1, LAST_WIDTH
-            y = psum.tile([P, width], F32, name="y_last", tag="bank%d" % bank)
+            span, tile_n = J // SPAN - 1, TILES - 1
+            y = psum.tile([P, LAST_WIDTH], F32, name="y_last", tag="bank%d" % bank)
             rows = slice(tile_n * P, (tile_n + 1) * P)
             for b in range(HALVES):
-                for at in range(0, width, UNIT):
+                for at in range(0, LAST_WIDTH, UNIT):
                     nc.tensor.matmul_mx(
                         out=y[:, at : at + UNIT],
                         lhsT=wd4_w[:, b, 2 * tile_n * P : 2 * (tile_n + 1) * P].bitcast(FP4X4),
@@ -298,64 +266,74 @@ def tile_list_gmlpt_gelu_res_res_kernel(
                     out=y[:],
                     lhsT=wd8_w[b][:, rows].bitcast(FP8X4),
                     lhsT_scale=wd8_s[WD8_ROW:P, b, rows],
-                    rhs=h_w[b, span][:, j0 : j0 + width].bitcast(FP8X4),
-                    rhs_scale=h_s[b, span][:, j0 : j0 + width],
+                    rhs=h_w[b, span][:, j0 : j0 + LAST_WIDTH].bitcast(FP8X4),
+                    rhs_scale=h_s[b, span][:, j0 : j0 + LAST_WIDTH],
                     start=False,
                     stop=(b == HALVES - 1),
                 )
-            finish(y, span, tile_n, j0, width)
+            add_and_store(y, span, tile_n, j0, LAST_WIDTH)
 
-        round_wu(0, nc.scalar.copy, 0, 304)
-        round_wu(1, nc.vector.tensor_copy, 304, 512)
-        for g in range(8):
+        reorder_wg_words(0)
+        gather(v_s, tab_s, SPAN)
+        nc.vector.tensor_copy(wg_s[:], wg_s_raw[:].rearrange("p (m t) -> p t m", t=PACK))
+        gather(v_w, tab_w, SLICE)
+
+        wu_bf = sbuf("wu_bf", [P, PACK, P, PACK], BF16)
+        nc.scalar.copy(*rounding(wu_bf, 0, SCALAR_COLUMNS, "m i t"))
+        for g in range(BANKS):
             gate(g, g)
+        nc.vector.tensor_copy(*rounding(wu_bf, SCALAR_COLUMNS, WU_CHUNK, "m i t"))
+        nc.vector.tensor_copy(*rounding(wu_bf, WU_CHUNK, PASS, "m i t"))
         reorder_wg_words(1)
-        quantize_wu(0)
-        wu_bf.append(sbuf("wu_bf1", [P, PACK, P, PACK], BF16, "wu_bf0"))
-        round_wu(2, gpsimd_round, 512, 768, "m t i")
-        round_wu(3, gpsimd_round, 768, 1024, "m t i")
-        for u in range(4):
-            up(u, u)
-        up(4, 0)
-        quantize_wu(1)
-        quantize_h(0, 0)
-        gate(8, 4)
-        up(5, 1)
-        gate(9, 5)
-        gate(10, 2)
-        gate(11, 6)
-        gate(12, 3)
-        gate(13, 7)
-        gate(14, 0)
-        gate(15, 4)
-        up(8, 5)
-        up(9, 2)
-        up(10, 6)
-        up(11, 3)
-        quantize_h(1, 0, 0, SPAN // 2)
-        quantize_h(1, 0, SPAN // 2, SPAN)
-        up(6, 2)
-        up(7, 6)
-        down(0, 0, 0, 1)
-        down(0, 0, 1, 5)
-        down(0, 0, 2, 7)
-        down(0, 0, 3, 0)
-        down(1, 0, 0)
-        up(12, 3)
-        quantize_h(0, 1)
-        down(1, 0, 1)
-        up(13, 4)
-        up(14, 2)
-        up(15, 6)
-        quantize_h(1, 1, 0, SPAN // 2)
-        quantize_h(1, 1, SPAN // 2, SPAN)
-        down(1, 0, 2)
-        down(1, 0, 3)
-        down(0, 1, 0, 1)
-        down(0, 1, 1, 5)
-        down(0, 1, 2, 3)
-        down(1, 1, 0)
-        down(1, 1, 1)
-        down(1, 1, 2)
-        last_tile(0, 0)
-        last_tile(LAST_WIDTH, 1)
+        quantize_wu(0, wu_bf)
+        wu_bf = sbuf("wu_bf1", [P, PACK, P, PACK], BF16, "wu_bf")
+        for c0 in range(PASS, R, WU_CHUNK):
+            nc.gpsimd.tensor_scalar(*rounding(wu_bf, c0, c0 + WU_CHUNK, "m t i"), 1.0, 0.0, MULT, ADD)
+
+        gate(8, banks["gate", 0])
+        gate(9, banks["gate", 1])
+        for u in range(3):
+            up(u, banks["gate", 2 + u])
+        gate(10, banks["gate", 5])
+        gate(11, banks["gate", 6])
+        up(3, banks["gate", 7])
+
+        up(4, banks["up", 0])
+        quantize_wu(1, wu_bf)
+        quantize_h(0, 0, 1)
+        gate(12, banks["gate", 8])
+        up(5, banks["up", 1])
+        gate(13, banks["gate", 9])
+        up(6, banks["up", 3])
+        gate(14, banks["up", 2])
+        gate(15, banks["gate", 10])
+
+        up(8, banks["gate", 11])
+        up(9, banks["up", 4])
+        up(10, banks["gate", 12])
+        up(11, banks["gate", 13])
+        quantize_h(1, 0, 2)
+        open_sum(0, 0, banks["up", 5])
+        open_sum(0, 1, banks["up", 6])
+        up(7, banks["up", 8])
+        open_sum(0, 2, banks["gate", 14])
+        open_sum(0, 3, banks["gate", 15])
+
+        up(12, banks["up", 9])
+        quantize_h(0, 1, 1)
+        close_sum(0, 0)
+        up(13, banks["up", 10])
+        close_sum(0, 1)
+        up(14, banks["up", 11])
+        up(15, banks["up", 7])
+        quantize_h(1, 1, 2)
+        close_sum(0, 2)
+        close_sum(0, 3)
+
+        open_sum(1, 0, banks["sum", 0, 0])
+        open_sum(1, 1, banks["sum", 0, 1])
+        open_sum(1, 2, banks["up", 12])
+        for tile_n in range(TILES - 1):
+            close_sum(1, tile_n)
+        last_tile(0, banks["sum", 0, 3])
+        last_tile(LAST_WIDTH, banks["sum", 1, 0])

@@ -34,7 +34,8 @@ WU_CHUNK = 256
 WG_ROW = 4
 WD8_ROW = 4
 SCALAR_COLUMNS = 64
-GPSIMD_UNIT = 6
+PIECE = SPAN // 2
+GPSIMD_UNITS = (6, 7)
 LAST_WIDTH = SPAN // 2
 
 
@@ -149,6 +150,11 @@ def tile_list_gmlpt_gelu_res_res_kernel(
         gates = {}
         sums = {}
 
+        def h_part(b, span, j0, width):
+            if (b, span) == (0, 1) and j0 >= PIECE:
+                return h_gpsimd[:, j0 - PIECE : j0 - PIECE + width, :]
+            return h_bf[b, span][:, j0 : j0 + width, :]
+
         def gate(g, bank):
             b, rest = divmod(g, PER_HALF)
             s, pair = divmod(rest, SLICE // UNIT)
@@ -185,34 +191,26 @@ def tile_list_gmlpt_gelu_res_res_kernel(
                     start=True,
                     stop=True,
                 )
-            h = h_bf[b, span][:, first : first + UNIT, :].rearrange("p j (pair e) -> p j pair e", e=2)
+            h = h_part(b, span, first, UNIT).rearrange("p j (pair e) -> p j pair e", e=2)
             gelus = gates[b, s][:, :, at : at + UNIT, :].rearrange("p pair j e -> p j pair e")
-            if u == GPSIMD_UNIT:
-                ub_sb = sbuf("ub_sb", [P, UNIT, PACK], F32, "wu_bf")
+            if u in GPSIMD_UNITS:
+                ub_sb = sbuf("ub_sb%d" % u, [P, UNIT, PACK], F32)
                 nc.scalar.copy(ub_sb[:], ub[:].rearrange("p t j -> p j t"))
                 nc.gpsimd.tensor_tensor(h, ub_sb[:].rearrange("p j (pair e) -> p j pair e", e=2), gelus, MULT)
             else:
                 nc.vector.tensor_tensor(h, ub[:].rearrange("p (pair e) j -> p j pair e", e=2), gelus, MULT)
 
-        def quantize_h(b, span, pieces):
-            width = SPAN // pieces
+        def quantize_h(b, span, width):
             for j0 in range(0, SPAN, width):
                 nc.vector.quantize_mx(
                     out=h_w[b, span][:, j0 : j0 + width].bitcast(FP8X4),
                     scales=h_s[b, span][:, j0 : j0 + width],
-                    in_=h_bf[b, span][:, j0 : j0 + width, :].rearrange("p j t -> p (j t)"),
+                    in_=h_part(b, span, j0, width).rearrange("p j t -> p (j t)"),
                 )
 
         def add_and_store(y, span, tile_n, j0, width):
-            res_part = res_sb[span][:, tile_n, j0 : j0 + width]
-            if (span, tile_n) == (0, 0):
-                y_sb = sbuf("y_sb", [P, width], F32)
-                nc.scalar.copy(y_sb[:], y[:])
-                result = sbuf("result_first", [P, width], F32, "h_bf01")
-                nc.gpsimd.tensor_tensor(result[:], y_sb[:], res_part, ADD)
-            else:
-                result = sbuf("result%d_%d_%d" % (span, tile_n, j0), [P, width], F32)
-                nc.vector.tensor_tensor(result[:], y[:], res_part, ADD)
+            result = sbuf("result%d_%d_%d" % (span, tile_n, j0), [P, width], F32)
+            nc.vector.tensor_tensor(result[:], y[:], res_sb[span][:, tile_n, j0 : j0 + width], ADD)
             at = span * SPAN + j0
             nc.sync.dma_start(out[tile_n * P : (tile_n + 1) * P, at : at + width], result[:])
 
@@ -292,41 +290,40 @@ def tile_list_gmlpt_gelu_res_res_kernel(
 
         gate(8, banks["gate", 0])
         gate(9, banks["gate", 1])
-        for u in range(3):
+        for u in range(4):
             up(u, banks["gate", 2 + u])
-        gate(10, banks["gate", 5])
-        gate(11, banks["gate", 6])
-        up(3, banks["gate", 7])
+        gate(10, banks["gate", 6])
+        gate(11, banks["gate", 7])
 
         up(4, banks["up", 0])
         quantize_wu(1, wu_bf)
-        quantize_h(0, 0, 1)
-        gate(12, banks["gate", 8])
+        quantize_h(0, 0, SPAN)
+        h_gpsimd = sbuf("h_gpsimd", [P, PIECE, PACK], BF16, "wu_bf")
         up(5, banks["up", 1])
-        gate(13, banks["gate", 9])
-        up(6, banks["up", 3])
-        gate(14, banks["up", 2])
-        gate(15, banks["gate", 10])
+        up(6, banks["gate", 8])
+        gate(12, banks["gate", 9])
+        up(7, banks["up", 2])
+        gate(13, banks["up", 3])
+        gate(14, banks["gate", 10])
+        gate(15, banks["gate", 11])
 
-        up(8, banks["gate", 11])
-        up(9, banks["up", 4])
+        up(8, banks["up", 4])
+        up(9, banks["up", 6])
         up(10, banks["gate", 12])
-        up(11, banks["gate", 13])
-        quantize_h(1, 0, 2)
+        up(11, banks["up", 7])
+        quantize_h(1, 0, PIECE)
         open_sum(0, 0, banks["up", 5])
-        open_sum(0, 1, banks["up", 6])
-        up(7, banks["up", 8])
-        open_sum(0, 2, banks["gate", 14])
-        open_sum(0, 3, banks["gate", 15])
+        for tile_n in range(1, TILES):
+            open_sum(0, tile_n, banks["gate", 12 + tile_n])
 
-        up(12, banks["up", 9])
-        quantize_h(0, 1, 1)
+        up(12, banks["up", 8])
+        quantize_h(0, 1, PIECE)
+        up(13, banks["up", 9])
         close_sum(0, 0)
-        up(13, banks["up", 10])
+        up(14, banks["up", 10])
         close_sum(0, 1)
-        up(14, banks["up", 11])
-        up(15, banks["up", 7])
-        quantize_h(1, 1, 2)
+        up(15, banks["up", 11])
+        quantize_h(1, 1, PIECE)
         close_sum(0, 2)
         close_sum(0, 3)
 

@@ -36,6 +36,8 @@ WD8_ROW = 4
 SCALAR_COLUMNS = 64
 PIECE = SPAN // 2
 GPSIMD_UNITS = (6, 7)
+PASSES_AHEAD = 4
+PASSES_BETWEEN = 2
 LAST_WIDTH = SPAN // 2
 
 
@@ -271,6 +273,19 @@ def tile_list_gmlpt_gelu_res_res_kernel(
                 )
             add_and_store(y, span, tile_n, j0, LAST_WIDTH)
 
+        def warm_tensor(count, bank):
+            unread = psum.tile([P, PASS], F32, name="unread", tag="bank%d" % bank)
+            for t in range(count):
+                nc.tensor.matmul_mx(
+                    out=unread[:],
+                    lhsT=wg_w[0][:, t, :].bitcast(FP8X4),
+                    lhsT_scale=v_s[:, 0:P],
+                    rhs=wg_w[0][:].rearrange("p t m -> p (t m)").bitcast(FP8X4),
+                    rhs_scale=v_s[:, 0:PASS],
+                    start=True,
+                    stop=True,
+                )
+
         reorder_wg_words(0)
         gather(v_s, tab_s, SPAN)
         nc.vector.tensor_copy(wg_s[:], wg_s_raw[:].rearrange("p (m t) -> p t m", t=PACK))
@@ -278,6 +293,7 @@ def tile_list_gmlpt_gelu_res_res_kernel(
 
         wu_bf = sbuf("wu_bf", [P, PACK, P, PACK], BF16)
         nc.scalar.copy(*rounding(wu_bf, 0, SCALAR_COLUMNS, "m i t"))
+        warm_tensor(PASSES_AHEAD, BANKS - 1)
         for g in range(BANKS):
             gate(g, g)
         nc.vector.tensor_copy(*rounding(wu_bf, SCALAR_COLUMNS, WU_CHUNK, "m i t"))
@@ -288,6 +304,7 @@ def tile_list_gmlpt_gelu_res_res_kernel(
         for c0 in range(PASS, R, WU_CHUNK):
             nc.gpsimd.tensor_scalar(*rounding(wu_bf, c0, c0 + WU_CHUNK, "m t i"), 1.0, 0.0, MULT, ADD)
 
+        warm_tensor(PASSES_BETWEEN, banks["gate", 1])
         gate(8, banks["gate", 0])
         gate(9, banks["gate", 1])
         for u in range(4):

@@ -50,7 +50,7 @@ def tile_list_gmlpt_gelu_res_res_kernel(
         psum = ctx.enter_context(tc.psum_pool(name="psum", bufs=1))
 
         def sbuf(name, shape, dtype, tag=None):
-            return keep.tile(shape, dtype, name=name, tag=tag or name, align_bytes=64)
+            return keep.tile(shape, dtype, name=name, tag=tag or name, align_bytes=256)
 
         offsets = keep.tile([P, J // LIST_ROWS], U16, name="offsets")
         tab_w = sbuf("tab_w", [P, T], U32)

@@ -300,9 +300,9 @@ def tile_list_gmlpt_gelu_res_res_kernel(
         nc.vector.tensor_copy(*rounding(wu_bf, WU_CHUNK, PASS, "m i t"))
         reorder_wg_words(1)
         quantize_wu(0, wu_bf)
-        wu_bf = sbuf("wu_bf1", [P, PACK, P, PACK], BF16, "wu_bf")
-        for c0 in range(PASS, R, WU_CHUNK):
-            nc.gpsimd.tensor_scalar(*rounding(wu_bf, c0, c0 + WU_CHUNK, "m t i"), 1.0, 0.0, MULT, ADD)
+        wu_bf = sbuf("wu_bf1", [P, PACK, P, PACK], BF16)
+        nc.vector.tensor_copy(*rounding(wu_bf, PASS, PASS + WU_CHUNK, "m i t"))
+        nc.gpsimd.tensor_scalar(*rounding(wu_bf, PASS + WU_CHUNK, R, "m t i"), 1.0, 0.0, MULT, ADD)
 
         warm_tensor(PASSES_BETWEEN, banks["gate", 1])
         gate(8, banks["gate", 0])
@@ -315,7 +315,7 @@ def tile_list_gmlpt_gelu_res_res_kernel(
         up(4, banks["up", 0])
         quantize_wu(1, wu_bf)
         quantize_h(0, 0, SPAN)
-        h_gpsimd = sbuf("h_gpsimd", [P, PIECE, PACK], BF16, "wu_bf")
+        h_gpsimd = sbuf("h_gpsimd", [P, PIECE, PACK], BF16, "wu_bf1")
         up(5, banks["up", 1])
         up(6, banks["gate", 8])
         gate(12, banks["gate", 9])

@@ -252,16 +252,15 @@ def tile_list_gmlpt_gelu_res_res_kernel(
             y = psum.tile([P, LAST_WIDTH], F32, name="y_last", tag="bank%d" % bank)
             rows = slice(tile_n * P, (tile_n + 1) * P)
             for b in range(HALVES):
-                for at in range(0, LAST_WIDTH, UNIT):
-                    nc.tensor.matmul_mx(
-                        out=y[:, at : at + UNIT],
-                        lhsT=wd4_w[:, b, 2 * tile_n * P : 2 * (tile_n + 1) * P].bitcast(FP4X4),
-                        lhsT_scale=wd4_s[:, b, rows],
-                        rhs=h_w[b, span][:, j0 + at : j0 + at + UNIT].bitcast(FP8X4),
-                        rhs_scale=h_s[b, span][:, j0 + at : j0 + at + UNIT],
-                        start=(b == 0 and at == 0),
-                        stop=False,
-                    )
+                nc.tensor.matmul_mx(
+                    out=y[:],
+                    lhsT=wd4_w[:, b, 2 * tile_n * P : 2 * (tile_n + 1) * P].bitcast(FP4X4),
+                    lhsT_scale=wd4_s[:, b, rows],
+                    rhs=h_w[b, span][:, j0 : j0 + LAST_WIDTH].bitcast(FP8X4),
+                    rhs_scale=h_s[b, span][:, j0 : j0 + LAST_WIDTH],
+                    start=(b == 0),
+                    stop=False,
+                )
                 nc.tensor.matmul_mx(
                     out=y[:],
                     lhsT=wd8_w[b][:, rows].bitcast(FP8X4),
@@ -312,42 +311,43 @@ def tile_list_gmlpt_gelu_res_res_kernel(
         gate(10, banks["gate", 6])
         gate(11, banks["gate", 7])
 
-        up(4, banks["up", 0])
         quantize_wu(1, wu_bf)
         quantize_h(0, 0, SPAN)
-        h_gpsimd = sbuf("h_gpsimd", [P, PIECE, PACK], BF16, "wu_bf1")
-        up(5, banks["up", 1])
-        up(6, banks["gate", 8])
-        gate(12, banks["gate", 9])
+        h_gpsimd = sbuf("h_gpsimd", [P, PIECE, PACK], BF16, "h_bf00")
+        up(4, banks["up", 0])
+        up(6, banks["up", 1])
+        gate(12, banks["gate", 8])
         up(7, banks["up", 2])
-        gate(13, banks["up", 3])
-        gate(14, banks["gate", 10])
-        gate(15, banks["gate", 11])
+        gate(13, banks["gate", 9])
+        gate(14, banks["up", 3])
+        gate(15, banks["gate", 10])
 
-        up(8, banks["up", 4])
+        up(8, banks["gate", 11])
         up(9, banks["up", 6])
-        up(10, banks["gate", 12])
-        up(11, banks["up", 7])
+        open_sum(0, 0, banks["gate", 12])
+        up(10, banks["up", 4])
+        up(5, banks["up", 7])
+        up(11, banks["up", 8])
         quantize_h(1, 0, PIECE)
-        open_sum(0, 0, banks["up", 5])
-        for tile_n in range(1, TILES):
-            open_sum(0, tile_n, banks["gate", 12 + tile_n])
+        open_sum(0, 1, banks["gate", 13])
+        open_sum(0, 2, banks["gate", 14])
+        up(12, banks["up", 9])
+        open_sum(0, 3, banks["gate", 15])
 
-        up(12, banks["up", 8])
         quantize_h(0, 1, PIECE)
-        up(13, banks["up", 9])
+        up(13, banks["up", 10])
         close_sum(0, 0)
-        up(14, banks["up", 10])
+        up(14, banks["up", 5])
         close_sum(0, 1)
         up(15, banks["up", 11])
         quantize_h(1, 1, PIECE)
         close_sum(0, 2)
         close_sum(0, 3)
 
-        open_sum(1, 0, banks["sum", 0, 0])
-        open_sum(1, 1, banks["sum", 0, 1])
-        open_sum(1, 2, banks["up", 12])
+        open_sum(1, 0, banks["up", 12])
+        open_sum(1, 1, banks["sum", 0, 0])
+        open_sum(1, 2, banks["up", 13])
         for tile_n in range(TILES - 1):
             close_sum(1, tile_n)
-        last_tile(0, banks["sum", 0, 3])
-        last_tile(LAST_WIDTH, banks["sum", 1, 0])
+        last_tile(0, banks["up", 14])
+        last_tile(LAST_WIDTH, banks["up", 15])

@@ -24,21 +24,14 @@ HALVES = R // PASS
 QUADRANT = 32
 BLOCKS = 4
 LIST_ROWS = 16
-BANKS = 8
 SLICE = 256
 UNIT = 128
 SPAN = 512
 TILES = N // P
-PER_HALF = J // UNIT
-WU_CHUNK = 256
-WG_ROW = 4
+CHUNK = 256
+CM = CHUNK // PACK
+TAB_ROW = 12
 WD8_ROW = 4
-SCALAR_COLUMNS = 64
-PIECE = SPAN // 2
-GPSIMD_UNITS = (6, 7)
-PASSES_AHEAD = 4
-PASSES_BETWEEN = 2
-LAST_WIDTH = SPAN // 2
 
 
 def tile_list_gmlpt_gelu_res_res_kernel(
@@ -55,222 +48,246 @@ def tile_list_gmlpt_gelu_res_res_kernel(
         offsets = keep.tile([P, J // LIST_ROWS], U16, name="offsets")
         tab_w = sbuf("tab_w", [P, T], U32)
         tab_s = sbuf("tab_s", [P, T], U8)
-        wg_w_raw = [sbuf("wg_w_raw%d" % b, [P, PASS], I32) for b in range(HALVES)]
-        wg_s_raw = sbuf("wg_s_raw", [P, PASS], U8)
-        wg_w = [sbuf("wg_w%d" % b, [P, PACK, P], I32) for b in range(HALVES)]
-        wg_s = sbuf("wg_s", [P, PACK, P], U8)
-        wu_raw = [sbuf("wu_raw%d" % c, [P, PACK, WU_CHUNK], F32) for c in range(R // WU_CHUNK)]
+        wg_w_raw = sbuf("wg_w_raw", [P, HALVES, PASS], U32)
+        wg_s_stage = sbuf("wg_s_stage", [P, 2, R], U8)
+        wg_s_raw = sbuf("wg_s_raw", [P, R], U8)
+        wg_w = [sbuf("wg_w%d" % b, [P, PACK, P], U32) for b in range(HALVES)]
+        wg_s = sbuf("wg_s", [P, HALVES, PACK, P], U8)
+        wu_raw = [sbuf("wu_raw%d" % c, [P, PACK, CHUNK], F32) for c in range(R // CHUNK)]
         wu_w = [sbuf("wu_w%d" % b, [P, PASS], U32) for b in range(HALVES)]
         wu_s = [sbuf("wu_s%d" % b, [P, PASS], U8) for b in range(HALVES)]
         wd4_w = sbuf("wd4_w", [P, HALVES, 2 * N], U8)
         wd8_w = [sbuf("wd8_w%d" % b, [P, N], U32) for b in range(HALVES)]
         wd4_s = sbuf("wd4_s", [P, HALVES, N], U8)
-        wd8_s = sbuf("wd8_s", [P, HALVES, N], U8)
         res_sb = [sbuf("res%d" % span, [P, TILES, SPAN], F32) for span in range(J // SPAN)]
         v_s = sbuf("v_s", [P, J], U8)
-        v_w = sbuf("v_w", [P, J], U32)
-        groups = [(b, span) for b in range(HALVES) for span in range(J // SPAN)]
-        h_bf = {g: sbuf("h_bf%d%d" % g, [P, SPAN, PACK], BF16) for g in groups}
-        h_w = {g: sbuf("h_w%d%d" % g, [P, SPAN], U32) for g in groups}
-        h_s = {g: sbuf("h_s%d%d" % g, [P, SPAN], U8) for g in groups}
+        v_w = {}
+        h_w = [sbuf("h_w%d" % b, [P, J], U32) for b in range(HALVES)]
+        h_s = [sbuf("h_s%d" % b, [P, J], U8) for b in range(HALVES)]
         warm = sbuf("warm", [P, 2, 8], F32)
 
-        def load_wg(b):
+        def load_wg():
             words = wg_words[0].rearrange("p r i -> p (r i)").bitcast(I32)
-            nc.sync.dma_start(wg_w_raw[b][:], words[:, b * PASS : (b + 1) * PASS])
+            nc.sync.dma_start(wg_w_raw[:].rearrange("p b c -> p (b c)").bitcast(I32), words)
 
         def load_wu(c):
             src = wu.rearrange("(p i) r -> p i r", i=PACK)
-            nc.sync.dma_start(wu_raw[c][:], src[:, :, c * WU_CHUNK : (c + 1) * WU_CHUNK])
+            nc.sync.dma_start(wu_raw[c][:], src[:, :, c * CHUNK : (c + 1) * CHUNK])
 
         def load_wd8(b):
             nc.sync.dma_start(wd8_w[b][:].bitcast(I32), wd8_words[b].rearrange("p n i -> p (n i)").bitcast(I32))
 
-        def load_wg_scales(engine, quad):
-            src = wg_scales[0][BLOCKS * quad : BLOCKS * (quad + 1), :].rearrange("block (b c) -> b block c", b=HALVES)
-            partition = QUADRANT * quad + WG_ROW
-            engine.dma_start(wg_s_raw[partition : partition + BLOCKS * HALVES, :].bitcast(I32), src.bitcast(I32))
+        def load_wg_scales(side):
+            src = wg_scales[0].rearrange("(side quad block) c -> side block quad c", side=2, block=BLOCKS)[side]
+            nc.sync.dma_start(wg_s_stage[64 * side : 64 * side + BLOCKS, :, :].bitcast(I32), src.bitcast(I32))
 
-        def load_wd_scales(engines, wd_s, scales, row):
-            for block, engine in enumerate(engines):
-                src = scales.rearrange("a (quad block) n -> block quad a n", block=BLOCKS)[block]
-                engine.dma_start(wd_s[row + block : P : QUADRANT, :, :].bitcast(I32), src.bitcast(I32))
+        def spread_wg_scales():
+            for quad in range(P // QUADRANT):
+                side, at = divmod(quad, 2)
+                nc.vector.tensor_copy(
+                    wg_s_raw[QUADRANT * quad : QUADRANT * quad + BLOCKS, :].bitcast(I32),
+                    wg_s_stage[64 * side : 64 * side + BLOCKS, at, :].bitcast(I32),
+                )
 
-        nc.vector.memset(wg_s_raw[:].bitcast(I32), 0)
-        nc.vector.memset(tab_s[:].bitcast(I32), 0)
-        nc.vector.memset(wd8_s[:].rearrange("p a n -> p (a n)").bitcast(I32), 0)
-        nc.vector.memset(wd4_s[:].rearrange("p a n -> p (a n)").bitcast(I32), 0)
-        nc.vector.memset(warm[:, 0, :], 0.0)
-        nc.sync.dma_start(offsets[:], offs)
-        for quad, engine in enumerate((nc.scalar, nc.sync, nc.gpsimd)):
-            load_wg_scales(engine, quad)
-        load_wg(0)
-        for block, engine in enumerate((nc.scalar, nc.scalar, nc.sync, nc.scalar)):
-            src = tab_scales[0].rearrange("(quad block) col -> block quad col", block=BLOCKS)[block]
-            engine.dma_start(tab_s[block:P:QUADRANT, :].bitcast(I32), src.bitcast(I32))
-        load_wg_scales(nc.sync, P // QUADRANT - 1)
-        nc.sync.dma_start(tab_w[:].bitcast(I32), tab_words[0].rearrange("p col i -> p (col i)").bitcast(I32))
-        nc.scalar.activation(warm[:, 1, :], warm[:, 0, :], GELU)
-        load_wd_scales((nc.gpsimd, nc.gpsimd, nc.scalar, nc.scalar), wd8_s, wd8_scales, WD8_ROW)
-        load_wu(0)
-        load_wu(1)
-        load_wg(1)
-        load_wu(2)
-        load_wu(3)
-        load_wd8(0)
-        nc.sync.dma_start(wd4_w[:].bitcast(I32), wd4_words.rearrange("a p c -> p a c").bitcast(I32))
-        load_wd_scales((nc.sync,) * BLOCKS, wd4_s, wd4_scales, 0)
-        load_wd8(1)
-        for span in range(J // SPAN):
+        def load_wd_scales(engine, wd_s, scales, row, block):
+            src = scales.rearrange("a (quad block) n -> block quad a n", block=BLOCKS)[block]
+            engine.dma_start(wd_s[row + block : P : QUADRANT, :, :].bitcast(I32), src.bitcast(I32))
+
+        def load_res(span):
             src = res.rearrange("(tile p) j -> p tile j", p=P)
             nc.sync.dma_start(res_sb[span][:], src[:, :, span * SPAN : (span + 1) * SPAN])
 
-        def gather(dst, table, width):
-            for j0 in range(0, J, width):
-                entries = offsets[:, j0 // LIST_ROWS : (j0 + width) // LIST_ROWS]
-                nc.vector.tensor_copy(dst[:, j0 : j0 + width], table[:].indirect(entries))
+        nc.vector.memset(tab_s[:].bitcast(I32), 0)
+        nc.vector.memset(wg_s_raw[:].bitcast(I32), 0)
+        nc.vector.memset(wd4_s[:].rearrange("p a n -> p (a n)").bitcast(I32), 0)
+        nc.vector.memset(warm[:, 0, :], 0.0)
+        nc.sync.dma_start(offsets[:], offs)
+        load_wg_scales(0)
+        load_wg_scales(1)
+        load_wg()
+        for block, engine in enumerate((nc.sync,) * BLOCKS + ()):
+            src = tab_scales[0].rearrange("(quad block) col -> block quad col", block=BLOCKS)[block]
+            engine.dma_start(tab_s[TAB_ROW + block : P : QUADRANT, :].bitcast(I32), src.bitcast(I32))
+        nc.sync.dma_start(tab_w[:].bitcast(I32), tab_words[0].rearrange("p col i -> p (col i)").bitcast(I32))
+        nc.scalar.activation(warm[:, 1, :], warm[:, 0, :], GELU)
+        spread_wg_scales()
+        nc.scalar.copy(wg_w[0][:].rearrange("p t m -> p m t"), wg_w_raw[:, 0, :].rearrange("p (m t) -> p m t", t=PACK))
+        nc.scalar.copy(wg_w[1][:].rearrange("p t m -> p m t"), wg_w_raw[:, 1, :].rearrange("p (m t) -> p m t", t=PACK))
+        wd8_s = sbuf("wd8_s", [P, HALVES, N], U8, "wg_s_stage")
+        nc.vector.memset(wd8_s[:].rearrange("p a n -> p (a n)").bitcast(I32), 0)
+        nc.vector.tensor_copy(wg_s[:], wg_s_raw[:].rearrange("p (b m t) -> p b t m", b=HALVES, t=PACK))
+        for block in range(2):
+            load_wd_scales(nc.scalar, wd8_s, wd8_scales, WD8_ROW, block)
+        load_wu(0)
+        for block in range(2, 4):
+            load_wd_scales(nc.scalar, wd8_s, wd8_scales, WD8_ROW, block)
+        load_wu(1)
+        load_wu(2)
+        load_wd8(0)
+        load_wu(3)
+        nc.sync.dma_start(wd4_w[:].bitcast(I32), wd4_words.rearrange("a p c -> p a c").bitcast(I32))
+        for block in range(BLOCKS):
+            load_wd_scales(nc.sync, wd4_s, wd4_scales, 0, block)
+        load_wd8(1)
+        load_res(0)
+        load_res(1)
+        def gather(dst, table, j0, width):
+            entries = offsets[:, j0 // LIST_ROWS : (j0 + width) // LIST_ROWS]
+            nc.vector.tensor_copy(dst[:, j0 : j0 + width], table[:].indirect(entries))
 
-        def reorder_wg_words(b):
-            src = wg_w_raw[b][:].rearrange("p (m t) -> p m t", t=PACK)
-            nc.vector.tensor_copy(wg_w[b][:].rearrange("p t m -> p m t"), src)
+        def gather_words(q, tag=None):
+            v_w[q] = sbuf("v_w%d" % q, [P, SLICE], U32, tag)
+            entries = offsets[:, q * SLICE // LIST_ROWS : (q + 1) * SLICE // LIST_ROWS]
+            nc.vector.tensor_copy(v_w[q][:], tab_w[:].indirect(entries))
 
-        def rounding(wu_bf, c0, c1, walk):
-            c, at = divmod(c0, WU_CHUNK)
-            first = c0 % PASS // PACK
-            dst = wu_bf[:, :, first : first + (c1 - c0) // PACK, :].rearrange("p t m i -> p " + walk)
-            src = wu_raw[c][:, :, at : at + c1 - c0].rearrange("p i (m t) -> p " + walk, t=PACK)
+        def wg_reorder(b):
+            return wg_w[b][:].rearrange("p t m -> p m t"), wg_w_raw[:, b, :].rearrange("p (m t) -> p m t", t=PACK)
+
+        wu_bf = {}
+
+        def rounding(c, walk, tag=None, m0=0, m1=CM):
+            if m0 == 0:
+                wu_bf[c] = sbuf("wu_bf%d" % c, [P, PACK, CM, PACK], BF16, tag)
+            dst = wu_bf[c][:, :, m0:m1, :].rearrange("p t m i -> p " + walk)
+            src = wu_raw[c][:, :, PACK * m0 : PACK * m1].rearrange("p i (m t) -> p " + walk, t=PACK)
             return dst, src
 
-        def quantize_wu(b, wu_bf):
-            nc.vector.quantize_mx(
-                out=wu_w[b][:].bitcast(FP8X4),
-                scales=wu_s[b][:],
-                in_=wu_bf[:].rearrange("p t m i -> p (t m i)"),
-            )
+        def quantize_wu(c):
+            b, part = divmod(c, PASS // CHUNK)
+            for t in range(PACK):
+                cols = slice(t * P + part * CM, t * P + (part + 1) * CM)
+                nc.vector.quantize_mx(
+                    out=wu_w[b][:, cols].bitcast(FP8X4),
+                    scales=wu_s[b][:, cols],
+                    in_=wu_bf[c][:, t, :, :].rearrange("p m i -> p (m i)"),
+                )
 
-        banks = {}
         gates = {}
+        h_bf = {}
         sums = {}
+        ubs = {}
 
-        def h_part(b, span, j0, width):
-            if (b, span) == (0, 1) and j0 >= PIECE:
-                return h_gpsimd[:, j0 - PIECE : j0 - PIECE + width, :]
-            return h_bf[b, span][:, j0 : j0 + width, :]
-
-        def gate(g, bank):
-            b, rest = divmod(g, PER_HALF)
-            s, pair = divmod(rest, SLICE // UNIT)
-            banks["gate", g] = bank
-            ga = psum.tile([P, 2, SLICE], F32, name="ga", tag="bank%d" % bank)
+        def gate(b, q, pair, bank):
+            ga = psum.tile([P, 2, SLICE], F32, name="ga%d%d%d" % (b, q, pair), tag="bank%d" % bank)
             for e in range(2):
                 nc.tensor.matmul_mx(
                     out=ga[:, e, :],
                     lhsT=wg_w[b][:, 2 * pair + e, :].bitcast(FP8X4),
-                    lhsT_scale=wg_s[WG_ROW + BLOCKS * b : P, 2 * pair + e, :],
-                    rhs=v_w[:, s * SLICE : (s + 1) * SLICE].bitcast(FP8X4),
-                    rhs_scale=v_s[:, s * SLICE : (s + 1) * SLICE],
+                    lhsT_scale=wg_s[:, b, 2 * pair + e, :],
+                    rhs=v_w[q][:].bitcast(FP8X4),
+                    rhs_scale=v_s[TAB_ROW:P, q * SLICE : (q + 1) * SLICE],
                     start=True,
                     stop=True,
                 )
             if pair == 0:
-                gates[b, s] = sbuf("gate%d%d" % (b, s), [P, 2, SLICE, 2], F32)
-            nc.scalar.activation(gates[b, s][:, pair, :, :], ga[:].rearrange("p e j -> p j e"), GELU)
+                gates[b, q] = sbuf("gate%d%d" % (b, q), [P, 2, SLICE, 2], F32)
+            nc.scalar.activation(gates[b, q][:, pair, :, :], ga[:].rearrange("p e j -> p j e"), GELU)
 
-        def up(u, bank):
-            b, tile_j = divmod(u, PER_HALF)
-            j0 = tile_j * UNIT
-            s, at = divmod(j0, SLICE)
-            span, first = divmod(j0, SPAN)
-            banks["up", u] = bank
-            ub = psum.tile([P, PACK, UNIT], F32, name="ub", tag="bank%d" % bank)
+        def up(b, u, bank):
+            j0 = u * UNIT
+            ub = psum.tile([P, PACK, UNIT], F32, name="ub%d%d" % (b, u), tag="bank%d" % bank)
             for t in range(PACK):
                 nc.tensor.matmul_mx(
                     out=ub[:, t, :],
                     lhsT=wu_w[b][:, t * P : (t + 1) * P].bitcast(FP8X4),
                     lhsT_scale=wu_s[b][:, t * P : (t + 1) * P],
-                    rhs=v_w[:, j0 : j0 + UNIT].bitcast(FP8X4),
-                    rhs_scale=v_s[:, j0 : j0 + UNIT],
+                    rhs=v_w[j0 // SLICE][:, j0 % SLICE : j0 % SLICE + UNIT].bitcast(FP8X4),
+                    rhs_scale=v_s[TAB_ROW:P, j0 : j0 + UNIT],
                     start=True,
                     stop=True,
                 )
-            h = h_part(b, span, first, UNIT).rearrange("p j (pair e) -> p j pair e", e=2)
-            gelus = gates[b, s][:, :, at : at + UNIT, :].rearrange("p pair j e -> p j pair e")
-            if u in GPSIMD_UNITS:
-                ub_sb = sbuf("ub_sb%d" % u, [P, UNIT, PACK], F32)
+            ubs[b, u] = ub
+
+        def mult(b, u, by_gpsimd=None):
+            q, part = divmod(u, SLICE // UNIT)
+            ub = ubs[b, u]
+            gelus = gates[b, q][:, :, part * UNIT : (part + 1) * UNIT, :].rearrange("p pair j e -> p j pair e")
+            if by_gpsimd:
+                h_bf[b, u] = sbuf("h_g%d%d" % (b, u), [P, UNIT, PACK], BF16, by_gpsimd)[:]
+                ub_sb = sbuf("ub_sb%d%d" % (b, u), [P, UNIT, PACK], F32)
                 nc.scalar.copy(ub_sb[:], ub[:].rearrange("p t j -> p j t"))
-                nc.gpsimd.tensor_tensor(h, ub_sb[:].rearrange("p j (pair e) -> p j pair e", e=2), gelus, MULT)
+                nc.gpsimd.tensor_tensor(
+                    h_bf[b, u].rearrange("p j (pair e) -> p j pair e", e=2),
+                    ub_sb[:].rearrange("p j (pair e) -> p j pair e", e=2), gelus, MULT)
             else:
-                nc.vector.tensor_tensor(h, ub[:].rearrange("p (pair e) j -> p j pair e", e=2), gelus, MULT)
+                if ("tile", b, q) not in h_bf:
+                    h_bf["tile", b, q] = sbuf("h_bf%d%d" % (b, q), [P, SLICE, PACK], BF16)
+                h_bf[b, u] = h_bf["tile", b, q][:, part * UNIT : (part + 1) * UNIT, :]
+                nc.vector.tensor_tensor(
+                    h_bf[b, u].rearrange("p j (pair e) -> p j pair e", e=2),
+                    ub[:].rearrange("p (pair e) j -> p j pair e", e=2), gelus, MULT)
 
-        def quantize_h(b, span, width):
-            for j0 in range(0, SPAN, width):
-                nc.vector.quantize_mx(
-                    out=h_w[b, span][:, j0 : j0 + width].bitcast(FP8X4),
-                    scales=h_s[b, span][:, j0 : j0 + width],
-                    in_=h_part(b, span, j0, width).rearrange("p j t -> p (j t)"),
-                )
+        def quantize_h(b, q):
+            j0 = q * SLICE
+            nc.vector.quantize_mx(
+                out=h_w[b][:, j0 : j0 + SLICE].bitcast(FP8X4),
+                scales=h_s[b][:, j0 : j0 + SLICE],
+                in_=h_bf["tile", b, q][:].rearrange("p j t -> p (j t)"),
+            )
 
-        def add_and_store(y, span, tile_n, j0, width):
-            result = sbuf("result%d_%d_%d" % (span, tile_n, j0), [P, width], F32)
-            nc.vector.tensor_tensor(result[:], y[:], res_sb[span][:, tile_n, j0 : j0 + width], ADD)
-            at = span * SPAN + j0
-            nc.sync.dma_start(out[tile_n * P : (tile_n + 1) * P, at : at + width], result[:])
+        def quantize_unit(b, u):
+            j0 = u * UNIT
+            nc.vector.quantize_mx(
+                out=h_w[b][:, j0 : j0 + UNIT].bitcast(FP8X4),
+                scales=h_s[b][:, j0 : j0 + UNIT],
+                in_=h_bf[b, u].rearrange("p j t -> p (j t)"),
+            )
 
-        def down(b, span, tile_n):
-            y = sums[span, tile_n]
+        def pass8(y, b, tile_n, j0, width, start):
             rows = slice(tile_n * P, (tile_n + 1) * P)
             nc.tensor.matmul_mx(
-                out=y[:],
+                out=y,
                 lhsT=wd8_w[b][:, rows].bitcast(FP8X4),
                 lhsT_scale=wd8_s[WD8_ROW:P, b, rows],
-                rhs=h_w[b, span][:].bitcast(FP8X4),
-                rhs_scale=h_s[b, span][:],
-                start=(b == 0),
+                rhs=h_w[b][:, j0 : j0 + width].bitcast(FP8X4),
+                rhs_scale=h_s[b][:, j0 : j0 + width],
+                start=start,
                 stop=False,
             )
+
+        def pass4(y, b, tile_n, j0, width, stop):
+            rows = slice(tile_n * P, (tile_n + 1) * P)
             nc.tensor.matmul_mx(
-                out=y[:],
+                out=y,
                 lhsT=wd4_w[:, b, 2 * tile_n * P : 2 * (tile_n + 1) * P].bitcast(FP4X4),
                 lhsT_scale=wd4_s[:, b, rows],
-                rhs=h_w[b, span][:].bitcast(FP8X4),
-                rhs_scale=h_s[b, span][:],
+                rhs=h_w[b][:, j0 : j0 + width].bitcast(FP8X4),
+                rhs_scale=h_s[b][:, j0 : j0 + width],
                 start=False,
-                stop=(b == HALVES - 1),
+                stop=stop,
             )
 
-        def open_sum(span, tile_n, bank):
-            banks["sum", span, tile_n] = bank
-            sums[span, tile_n] = psum.tile([P, SPAN], F32, name="y", tag="bank%d" % bank)
-            down(0, span, tile_n)
+        def passes(y, b, tile_n, j0, width, start, stop):
+            pass8(y, b, tile_n, j0, width, start)
+            pass4(y, b, tile_n, j0, width, stop)
 
-        def close_sum(span, tile_n):
-            down(1, span, tile_n)
-            add_and_store(sums[span, tile_n], span, tile_n, 0, SPAN)
+        def open_first(tile_n, j0, width, bank):
+            sums[tile_n, j0] = psum.tile([P, width], F32, name="y%d_%d" % (tile_n, j0), tag="bank%d" % bank)
+            pass8(sums[tile_n, j0][:], 0, tile_n, j0, width, True)
 
-        def last_tile(j0, bank):
-            span, tile_n = J // SPAN - 1, TILES - 1
-            y = psum.tile([P, LAST_WIDTH], F32, name="y_last", tag="bank%d" % bank)
-            rows = slice(tile_n * P, (tile_n + 1) * P)
-            for b in range(HALVES):
-                nc.tensor.matmul_mx(
-                    out=y[:],
-                    lhsT=wd4_w[:, b, 2 * tile_n * P : 2 * (tile_n + 1) * P].bitcast(FP4X4),
-                    lhsT_scale=wd4_s[:, b, rows],
-                    rhs=h_w[b, span][:, j0 : j0 + LAST_WIDTH].bitcast(FP8X4),
-                    rhs_scale=h_s[b, span][:, j0 : j0 + LAST_WIDTH],
-                    start=(b == 0),
-                    stop=False,
-                )
-                nc.tensor.matmul_mx(
-                    out=y[:],
-                    lhsT=wd8_w[b][:, rows].bitcast(FP8X4),
-                    lhsT_scale=wd8_s[WD8_ROW:P, b, rows],
-                    rhs=h_w[b, span][:, j0 : j0 + LAST_WIDTH].bitcast(FP8X4),
-                    rhs_scale=h_s[b, span][:, j0 : j0 + LAST_WIDTH],
-                    start=False,
-                    stop=(b == HALVES - 1),
-                )
-            add_and_store(y, span, tile_n, j0, LAST_WIDTH)
+        def open_second(tile_n, j0, width):
+            pass4(sums[tile_n, j0][:], 0, tile_n, j0, width, False)
+
+        def open_sum(tile_n, j0, width, bank):
+            sums[tile_n, j0] = psum.tile([P, width], F32, name="y%d_%d" % (tile_n, j0), tag="bank%d" % bank)
+            passes(sums[tile_n, j0][:], 0, tile_n, j0, width, True, False)
+
+        def close_sum(tile_n, j0, width):
+            passes(sums[tile_n, j0][:], 1, tile_n, j0, width, False, True)
+
+        def close_part(tile_n, base, j0, last):
+            passes(sums[tile_n, base][:, j0 - base : j0 - base + SLICE], 1, tile_n, j0, SLICE, False, last)
+
+        def add_and_store(tile_n, j0, width, by_gpsimd=None):
+            span, at = divmod(j0, SPAN)
+            result = sbuf("result%d_%d" % (tile_n, j0), [P, width], F32, by_gpsimd)
+            if by_gpsimd:
+                y_sb = sbuf("y_sb%d_%d" % (tile_n, j0), [P, width], F32)
+                nc.scalar.copy(y_sb[:], sums[tile_n, j0][:])
+                nc.gpsimd.tensor_tensor(result[:], y_sb[:], res_sb[span][:, tile_n, at : at + width], ADD)
+            else:
+                nc.vector.tensor_tensor(result[:], sums[tile_n, j0][:], res_sb[span][:, tile_n, at : at + width], ADD)
+            nc.sync.dma_start(out[tile_n * P : (tile_n + 1) * P, j0 : j0 + width], result[:])
 
         def warm_tensor(count, bank):
             unread = psum.tile([P, PASS], F32, name="unread", tag="bank%d" % bank)
@@ -278,76 +295,110 @@ def tile_list_gmlpt_gelu_res_res_kernel(
                 nc.tensor.matmul_mx(
                     out=unread[:],
                     lhsT=wg_w[0][:, t, :].bitcast(FP8X4),
-                    lhsT_scale=v_s[:, 0:P],
+                    lhsT_scale=wg_s[:, 0, t, :],
                     rhs=wg_w[0][:].rearrange("p t m -> p (t m)").bitcast(FP8X4),
-                    rhs_scale=v_s[:, 0:PASS],
+                    rhs_scale=wg_s[:, 0, :, :].rearrange("p t m -> p (t m)"),
                     start=True,
                     stop=True,
                 )
 
-        reorder_wg_words(0)
-        gather(v_s, tab_s, SPAN)
-        nc.vector.tensor_copy(wg_s[:], wg_s_raw[:].rearrange("p (m t) -> p t m", t=PACK))
-        gather(v_w, tab_w, SLICE)
-
-        wu_bf = sbuf("wu_bf", [P, PACK, P, PACK], BF16)
-        nc.scalar.copy(*rounding(wu_bf, 0, SCALAR_COLUMNS, "m i t"))
-        warm_tensor(PASSES_AHEAD, BANKS - 1)
-        for g in range(BANKS):
-            gate(g, g)
-        nc.vector.tensor_copy(*rounding(wu_bf, SCALAR_COLUMNS, WU_CHUNK, "m i t"))
-        nc.vector.tensor_copy(*rounding(wu_bf, WU_CHUNK, PASS, "m i t"))
-        reorder_wg_words(1)
-        quantize_wu(0, wu_bf)
-        wu_bf = sbuf("wu_bf1", [P, PACK, P, PACK], BF16)
-        nc.vector.tensor_copy(*rounding(wu_bf, PASS, PASS + WU_CHUNK, "m i t"))
-        nc.gpsimd.tensor_scalar(*rounding(wu_bf, PASS + WU_CHUNK, R, "m t i"), 1.0, 0.0, MULT, ADD)
-
-        warm_tensor(PASSES_BETWEEN, banks["gate", 1])
-        gate(8, banks["gate", 0])
-        gate(9, banks["gate", 1])
-        for u in range(4):
-            up(u, banks["gate", 2 + u])
-        gate(10, banks["gate", 6])
-        gate(11, banks["gate", 7])
-
-        quantize_wu(1, wu_bf)
-        quantize_h(0, 0, SPAN)
-        h_gpsimd = sbuf("h_gpsimd", [P, PIECE, PACK], BF16, "h_bf00")
-        up(4, banks["up", 0])
-        up(6, banks["up", 1])
-        gate(12, banks["gate", 8])
-        up(7, banks["up", 2])
-        gate(13, banks["gate", 9])
-        gate(14, banks["up", 3])
-        gate(15, banks["gate", 10])
-
-        up(8, banks["gate", 11])
-        up(9, banks["up", 6])
-        open_sum(0, 0, banks["gate", 12])
-        up(10, banks["up", 4])
-        up(5, banks["up", 7])
-        up(11, banks["up", 8])
-        quantize_h(1, 0, PIECE)
-        open_sum(0, 1, banks["gate", 13])
-        open_sum(0, 2, banks["gate", 14])
-        up(12, banks["up", 9])
-        open_sum(0, 3, banks["gate", 15])
-
-        quantize_h(0, 1, PIECE)
-        up(13, banks["up", 10])
-        close_sum(0, 0)
-        up(14, banks["up", 5])
-        close_sum(0, 1)
-        up(15, banks["up", 11])
-        quantize_h(1, 1, PIECE)
-        close_sum(0, 2)
-        close_sum(0, 3)
-
-        open_sum(1, 0, banks["up", 12])
-        open_sum(1, 1, banks["sum", 0, 0])
-        open_sum(1, 2, banks["up", 13])
-        for tile_n in range(TILES - 1):
-            close_sum(1, tile_n)
-        last_tile(0, banks["up", 14])
-        last_tile(LAST_WIDTH, banks["up", 15])
+        gather(v_s, tab_s, 0, SPAN)
+        gather(v_s, tab_s, SPAN, SPAN)
+        warm_tensor(4, 7)
+        for q in range(3):
+            gather_words(q)
+        gate(0, 0, 0, 0)
+        gate(0, 0, 1, 1)
+        gate(0, 1, 0, 2)
+        gate(0, 1, 1, 3)
+        gate(1, 0, 0, 4)
+        gate(1, 0, 1, 5)
+        gate(0, 2, 0, 6)
+        gate(0, 2, 1, 7)
+        gate(1, 1, 0, 0)
+        gate(1, 1, 1, 1)
+        nc.vector.tensor_copy(*rounding(0, "m i t"))
+        nc.vector.tensor_copy(*rounding(1, "m i t"))
+        quantize_wu(0)
+        quantize_wu(1)
+        gather_words(3, "wu_raw1")
+        nc.gpsimd.tensor_scalar(*rounding(2, "m t i", "tab_w"), 1.0, 0.0, MULT, ADD)
+        up(0, 0, 2)
+        up(0, 1, 3)
+        mult(0, 0)
+        gate(0, 3, 0, 4)
+        up(0, 2, 5)
+        mult(0, 1)
+        up(0, 3, 2)
+        gate(0, 3, 1, 6)
+        mult(0, 2)
+        quantize_h(0, 0)
+        nc.gpsimd.tensor_scalar(*rounding(3, "m t i", "h_bf00", 0, CM // 2), 1.0, 0.0, MULT, ADD)
+        up(0, 4, 3)
+        gate(1, 2, 0, 7)
+        mult(0, 3)
+        gate(1, 2, 1, 0)
+        up(0, 5, 5)
+        mult(0, 4)
+        quantize_h(0, 1)
+        quantize_wu(2)
+        nc.gpsimd.tensor_scalar(*rounding(3, "m t i", None, CM // 2, CM), 1.0, 0.0, MULT, ADD)
+        gate(1, 3, 0, 1)
+        up(0, 6, 2)
+        mult(0, 5)
+        gate(1, 3, 1, 4)
+        up(0, 7, 3)
+        open_sum(0, 0, SPAN, 6)
+        mult(0, 6)
+        quantize_wu(3)
+        open_sum(1, 0, SPAN, 5)
+        open_first(2, 0, SPAN, 7)
+        mult(0, 7)
+        quantize_h(0, 2)
+        quantize_h(0, 3)
+        up(1, 6, 0)
+        mult(1, 6, "h_bf03")
+        up(1, 0, 2)
+        up(1, 1, 1)
+        open_second(2, 0, SPAN)
+        up(1, 2, 3)
+        mult(1, 0)
+        open_sum(3, 0, SPAN, 4)
+        mult(1, 1)
+        up(1, 3, 0)
+        up(1, 7, 2)
+        mult(1, 2)
+        up(1, 4, 1)
+        open_sum(0, SPAN, SPAN, 3)
+        mult(1, 3)
+        quantize_h(1, 0)
+        quantize_h(1, 1)
+        mult(1, 7, "h_bf11")
+        up(1, 5, 0)
+        mult(1, 4)
+        open_sum(1, SPAN, SPAN, 2)
+        close_sum(0, 0, SPAN)
+        mult(1, 5)
+        close_sum(1, 0, SPAN)
+        add_and_store(0, 0, SPAN)
+        quantize_h(1, 2)
+        quantize_unit(1, 6)
+        quantize_unit(1, 7)
+        close_sum(2, 0, SPAN)
+        add_and_store(1, 0, SPAN)
+        close_sum(3, 0, SPAN)
+        add_and_store(2, 0, SPAN)
+        close_sum(0, SPAN, SPAN)
+        add_and_store(3, 0, SPAN)
+        close_sum(1, SPAN, SPAN)
+        add_and_store(0, SPAN, SPAN)
+        open_sum(2, SPAN, SPAN, 1)
+        close_sum(2, SPAN, SPAN)
+        add_and_store(1, SPAN, SPAN)
+        add_and_store(2, SPAN, SPAN)
+        open_sum(3, SPAN, SLICE, 0)
+        close_sum(3, SPAN, SLICE)
+        add_and_store(3, SPAN, SLICE)
+        open_sum(3, SPAN + SLICE, SLICE, 6)
+        close_sum(3, SPAN + SLICE, SLICE)
+        add_and_store(3, SPAN + SLICE, SLICE)

@@ -30,7 +30,7 @@ SPAN = 512
 TILES = N // P
 CHUNK = 256
 CM = CHUNK // PACK
-TAB_ROW = 12
+WG_ROW = 4
 WD8_ROW = 4
 
 
@@ -48,17 +48,17 @@ def tile_list_gmlpt_gelu_res_res_kernel(
         offsets = keep.tile([P, J // LIST_ROWS], U16, name="offsets")
         tab_w = sbuf("tab_w", [P, T], U32)
         tab_s = sbuf("tab_s", [P, T], U8)
-        wg_w_raw = sbuf("wg_w_raw", [P, HALVES, PASS], U32)
-        wg_s_stage = sbuf("wg_s_stage", [P, 2, R], U8)
-        wg_s_raw = sbuf("wg_s_raw", [P, R], U8)
+        wg_w_raw = [sbuf("wg_w_raw%d" % b, [P, PASS], U32) for b in range(HALVES)]
+        wg_s_raw = sbuf("wg_s_raw", [P, PASS], U8)
         wg_w = [sbuf("wg_w%d" % b, [P, PACK, P], U32) for b in range(HALVES)]
-        wg_s = sbuf("wg_s", [P, HALVES, PACK, P], U8)
+        wg_s = sbuf("wg_s", [P, PACK, P], U8)
         wu_raw = [sbuf("wu_raw%d" % c, [P, PACK, CHUNK], F32) for c in range(R // CHUNK)]
         wu_w = [sbuf("wu_w%d" % b, [P, PASS], U32) for b in range(HALVES)]
         wu_s = [sbuf("wu_s%d" % b, [P, PASS], U8) for b in range(HALVES)]
         wd4_w = sbuf("wd4_w", [P, HALVES, 2 * N], U8)
         wd8_w = [sbuf("wd8_w%d" % b, [P, N], U32) for b in range(HALVES)]
         wd4_s = sbuf("wd4_s", [P, HALVES, N], U8)
+        wd8_s = sbuf("wd8_s", [P, HALVES, N], U8)
         res_sb = [sbuf("res%d" % span, [P, TILES, SPAN], F32) for span in range(J // SPAN)]
         v_s = sbuf("v_s", [P, J], U8)
         v_w = {}
@@ -66,9 +66,9 @@ def tile_list_gmlpt_gelu_res_res_kernel(
         h_s = [sbuf("h_s%d" % b, [P, J], U8) for b in range(HALVES)]
         warm = sbuf("warm", [P, 2, 8], F32)
 
-        def load_wg():
+        def load_wg(b):
             words = wg_words[0].rearrange("p r i -> p (r i)").bitcast(I32)
-            nc.sync.dma_start(wg_w_raw[:].rearrange("p b c -> p (b c)").bitcast(I32), words)
+            nc.sync.dma_start(wg_w_raw[b][:].bitcast(I32), words[:, b * PASS : (b + 1) * PASS])
 
         def load_wu(c):
             src = wu.rearrange("(p i) r -> p i r", i=PACK)
@@ -77,17 +77,10 @@ def tile_list_gmlpt_gelu_res_res_kernel(
         def load_wd8(b):
             nc.sync.dma_start(wd8_w[b][:].bitcast(I32), wd8_words[b].rearrange("p n i -> p (n i)").bitcast(I32))
 
-        def load_wg_scales(side):
-            src = wg_scales[0].rearrange("(side quad block) c -> side block quad c", side=2, block=BLOCKS)[side]
-            nc.sync.dma_start(wg_s_stage[64 * side : 64 * side + BLOCKS, :, :].bitcast(I32), src.bitcast(I32))
-
-        def spread_wg_scales():
-            for quad in range(P // QUADRANT):
-                side, at = divmod(quad, 2)
-                nc.vector.tensor_copy(
-                    wg_s_raw[QUADRANT * quad : QUADRANT * quad + BLOCKS, :].bitcast(I32),
-                    wg_s_stage[64 * side : 64 * side + BLOCKS, at, :].bitcast(I32),
-                )
+        def load_wg_scales(engine, quad):
+            src = wg_scales[0][BLOCKS * quad : BLOCKS * (quad + 1), :].rearrange("block (b c) -> b block c", b=HALVES)
+            partition = QUADRANT * quad + WG_ROW
+            engine.dma_start(wg_s_raw[partition : partition + BLOCKS * HALVES, :].bitcast(I32), src.bitcast(I32))
 
         def load_wd_scales(engine, wd_s, scales, row, block):
             src = scales.rearrange("a (quad block) n -> block quad a n", block=BLOCKS)[block]
@@ -99,38 +92,9 @@ def tile_list_gmlpt_gelu_res_res_kernel(
 
         nc.vector.memset(tab_s[:].bitcast(I32), 0)
         nc.vector.memset(wg_s_raw[:].bitcast(I32), 0)
+        nc.vector.memset(wd8_s[:].rearrange("p a n -> p (a n)").bitcast(I32), 0)
         nc.vector.memset(wd4_s[:].rearrange("p a n -> p (a n)").bitcast(I32), 0)
         nc.vector.memset(warm[:, 0, :], 0.0)
-        nc.sync.dma_start(offsets[:], offs)
-        load_wg_scales(0)
-        load_wg_scales(1)
-        load_wg()
-        for block, engine in enumerate((nc.sync,) * BLOCKS + ()):
-            src = tab_scales[0].rearrange("(quad block) col -> block quad col", block=BLOCKS)[block]
-            engine.dma_start(tab_s[TAB_ROW + block : P : QUADRANT, :].bitcast(I32), src.bitcast(I32))
-        nc.sync.dma_start(tab_w[:].bitcast(I32), tab_words[0].rearrange("p col i -> p (col i)").bitcast(I32))
-        nc.scalar.activation(warm[:, 1, :], warm[:, 0, :], GELU)
-        spread_wg_scales()
-        nc.scalar.copy(wg_w[0][:].rearrange("p t m -> p m t"), wg_w_raw[:, 0, :].rearrange("p (m t) -> p m t", t=PACK))
-        nc.scalar.copy(wg_w[1][:].rearrange("p t m -> p m t"), wg_w_raw[:, 1, :].rearrange("p (m t) -> p m t", t=PACK))
-        wd8_s = sbuf("wd8_s", [P, HALVES, N], U8, "wg_s_stage")
-        nc.vector.memset(wd8_s[:].rearrange("p a n -> p (a n)").bitcast(I32), 0)
-        nc.vector.tensor_copy(wg_s[:], wg_s_raw[:].rearrange("p (b m t) -> p b t m", b=HALVES, t=PACK))
-        for block in range(2):
-            load_wd_scales(nc.scalar, wd8_s, wd8_scales, WD8_ROW, block)
-        load_wu(0)
-        for block in range(2, 4):
-            load_wd_scales(nc.scalar, wd8_s, wd8_scales, WD8_ROW, block)
-        load_wu(1)
-        load_wu(2)
-        load_wd8(0)
-        load_wu(3)
-        nc.sync.dma_start(wd4_w[:].bitcast(I32), wd4_words.rearrange("a p c -> p a c").bitcast(I32))
-        for block in range(BLOCKS):
-            load_wd_scales(nc.sync, wd4_s, wd4_scales, 0, block)
-        load_wd8(1)
-        load_res(0)
-        load_res(1)
         def gather(dst, table, j0, width):
             entries = offsets[:, j0 // LIST_ROWS : (j0 + width) // LIST_ROWS]
             nc.vector.tensor_copy(dst[:, j0 : j0 + width], table[:].indirect(entries))
@@ -141,26 +105,26 @@ def tile_list_gmlpt_gelu_res_res_kernel(
             nc.vector.tensor_copy(v_w[q][:], tab_w[:].indirect(entries))
 
         def wg_reorder(b):
-            return wg_w[b][:].rearrange("p t m -> p m t"), wg_w_raw[:, b, :].rearrange("p (m t) -> p m t", t=PACK)
+            return wg_w[b][:].rearrange("p t m -> p m t"), wg_w_raw[b][:].rearrange("p (m t) -> p m t", t=PACK)
 
         wu_bf = {}
 
-        def rounding(c, walk, tag=None, m0=0, m1=CM):
-            if m0 == 0:
-                wu_bf[c] = sbuf("wu_bf%d" % c, [P, PACK, CM, PACK], BF16, tag)
-            dst = wu_bf[c][:, :, m0:m1, :].rearrange("p t m i -> p " + walk)
-            src = wu_raw[c][:, :, PACK * m0 : PACK * m1].rearrange("p i (m t) -> p " + walk, t=PACK)
+        def rounding(c0, c1, walk, tag=None):
+            b = c0 // PASS
+            if b not in wu_bf:
+                wu_bf[b] = sbuf("wu_bf%d" % b, [P, PACK, P, PACK], BF16, tag)
+            c, at = divmod(c0, CHUNK)
+            first = c0 % PASS // PACK
+            dst = wu_bf[b][:, :, first : first + (c1 - c0) // PACK, :].rearrange("p t m i -> p " + walk)
+            src = wu_raw[c][:, :, at : at + c1 - c0].rearrange("p i (m t) -> p " + walk, t=PACK)
             return dst, src
 
-        def quantize_wu(c):
-            b, part = divmod(c, PASS // CHUNK)
-            for t in range(PACK):
-                cols = slice(t * P + part * CM, t * P + (part + 1) * CM)
-                nc.vector.quantize_mx(
-                    out=wu_w[b][:, cols].bitcast(FP8X4),
-                    scales=wu_s[b][:, cols],
-                    in_=wu_bf[c][:, t, :, :].rearrange("p m i -> p (m i)"),
-                )
+        def quantize_wu(b, t0=0, t1=PACK):
+            nc.vector.quantize_mx(
+                out=wu_w[b][:, t0 * P : t1 * P].bitcast(FP8X4),
+                scales=wu_s[b][:, t0 * P : t1 * P],
+                in_=wu_bf[b][:, t0:t1, :, :].rearrange("p t m i -> p (t m i)"),
+            )
 
         gates = {}
         h_bf = {}
@@ -173,9 +137,9 @@ def tile_list_gmlpt_gelu_res_res_kernel(
                 nc.tensor.matmul_mx(
                     out=ga[:, e, :],
                     lhsT=wg_w[b][:, 2 * pair + e, :].bitcast(FP8X4),
-                    lhsT_scale=wg_s[:, b, 2 * pair + e, :],
+                    lhsT_scale=wg_s[WG_ROW + BLOCKS * b : P, 2 * pair + e, :],
                     rhs=v_w[q][:].bitcast(FP8X4),
-                    rhs_scale=v_s[TAB_ROW:P, q * SLICE : (q + 1) * SLICE],
+                    rhs_scale=v_s[:, q * SLICE : (q + 1) * SLICE],
                     start=True,
                     stop=True,
                 )
@@ -192,45 +156,44 @@ def tile_list_gmlpt_gelu_res_res_kernel(
                     lhsT=wu_w[b][:, t * P : (t + 1) * P].bitcast(FP8X4),
                     lhsT_scale=wu_s[b][:, t * P : (t + 1) * P],
                     rhs=v_w[j0 // SLICE][:, j0 % SLICE : j0 % SLICE + UNIT].bitcast(FP8X4),
-                    rhs_scale=v_s[TAB_ROW:P, j0 : j0 + UNIT],
+                    rhs_scale=v_s[:, j0 : j0 + UNIT],
                     start=True,
                     stop=True,
                 )
             ubs[b, u] = ub
 
-        def mult(b, u, by_gpsimd=None):
+        def h_tile(b, u0, units, tag=None):
+            tile_h = sbuf("h_bf%d%d" % (b, u0), [P, units * UNIT, PACK], BF16, tag)
+            for u in range(u0, u0 + units):
+                h_bf[b, u] = (tile_h, u0)
+
+        def h_part(b, u, units):
+            tile_h, u0 = h_bf[b, u]
+            return tile_h[:, (u - u0) * UNIT : (u - u0 + units) * UNIT, :]
+
+        def gelus(b, u):
             q, part = divmod(u, SLICE // UNIT)
-            ub = ubs[b, u]
-            gelus = gates[b, q][:, :, part * UNIT : (part + 1) * UNIT, :].rearrange("p pair j e -> p j pair e")
-            if by_gpsimd:
-                h_bf[b, u] = sbuf("h_g%d%d" % (b, u), [P, UNIT, PACK], BF16, by_gpsimd)[:]
-                ub_sb = sbuf("ub_sb%d%d" % (b, u), [P, UNIT, PACK], F32)
-                nc.scalar.copy(ub_sb[:], ub[:].rearrange("p t j -> p j t"))
-                nc.gpsimd.tensor_tensor(
-                    h_bf[b, u].rearrange("p j (pair e) -> p j pair e", e=2),
-                    ub_sb[:].rearrange("p j (pair e) -> p j pair e", e=2), gelus, MULT)
-            else:
-                if ("tile", b, q) not in h_bf:
-                    h_bf["tile", b, q] = sbuf("h_bf%d%d" % (b, q), [P, SLICE, PACK], BF16)
-                h_bf[b, u] = h_bf["tile", b, q][:, part * UNIT : (part + 1) * UNIT, :]
-                nc.vector.tensor_tensor(
-                    h_bf[b, u].rearrange("p j (pair e) -> p j pair e", e=2),
-                    ub[:].rearrange("p (pair e) j -> p j pair e", e=2), gelus, MULT)
+            return gates[b, q][:, :, part * UNIT : (part + 1) * UNIT, :].rearrange("p pair j e -> p j pair e")
 
-        def quantize_h(b, q):
-            j0 = q * SLICE
-            nc.vector.quantize_mx(
-                out=h_w[b][:, j0 : j0 + SLICE].bitcast(FP8X4),
-                scales=h_s[b][:, j0 : j0 + SLICE],
-                in_=h_bf["tile", b, q][:].rearrange("p j t -> p (j t)"),
-            )
+        def mult(b, u):
+            h = h_part(b, u, 1).rearrange("p j (pair e) -> p j pair e", e=2)
+            nc.vector.tensor_tensor(h, ubs[b, u][:].rearrange("p (pair e) j -> p j pair e", e=2), gelus(b, u), MULT)
 
-        def quantize_unit(b, u):
-            j0 = u * UNIT
+        def copy_up(b, u):
+            ub_sb = sbuf("ub_sb%d%d" % (b, u), [P, UNIT, PACK], F32)
+            nc.scalar.copy(ub_sb[:], ubs[b, u][:].rearrange("p t j -> p j t"))
+            ubs[b, u] = ub_sb
+
+        def mult_gpsimd(b, u):
+            h = h_part(b, u, 1).rearrange("p j (pair e) -> p j pair e", e=2)
+            nc.gpsimd.tensor_tensor(h, ubs[b, u][:].rearrange("p j (pair e) -> p j pair e", e=2), gelus(b, u), MULT)
+
+        def quantize_h(b, u, units):
+            cols = slice(u * UNIT, (u + units) * UNIT)
             nc.vector.quantize_mx(
-                out=h_w[b][:, j0 : j0 + UNIT].bitcast(FP8X4),
-                scales=h_s[b][:, j0 : j0 + UNIT],
-                in_=h_bf[b, u].rearrange("p j t -> p (j t)"),
+                out=h_w[b][:, cols].bitcast(FP8X4),
+                scales=h_s[b][:, cols],
+                in_=h_part(b, u, units).rearrange("p j t -> p (j t)"),
             )
 
         def pass8(y, b, tile_n, j0, width, start):
@@ -278,16 +241,25 @@ def tile_list_gmlpt_gelu_res_res_kernel(
         def close_part(tile_n, base, j0, last):
             passes(sums[tile_n, base][:, j0 - base : j0 - base + SLICE], 1, tile_n, j0, SLICE, False, last)
 
-        def add_and_store(tile_n, j0, width, by_gpsimd=None):
-            span, at = divmod(j0, SPAN)
-            result = sbuf("result%d_%d" % (tile_n, j0), [P, width], F32, by_gpsimd)
-            if by_gpsimd:
-                y_sb = sbuf("y_sb%d_%d" % (tile_n, j0), [P, width], F32)
-                nc.scalar.copy(y_sb[:], sums[tile_n, j0][:])
-                nc.gpsimd.tensor_tensor(result[:], y_sb[:], res_sb[span][:, tile_n, at : at + width], ADD)
-            else:
-                nc.vector.tensor_tensor(result[:], sums[tile_n, j0][:], res_sb[span][:, tile_n, at : at + width], ADD)
+        def store(result, tile_n, j0, width):
             nc.sync.dma_start(out[tile_n * P : (tile_n + 1) * P, j0 : j0 + width], result[:])
+
+        def add_and_store(tile_n, j0, width):
+            span, at = divmod(j0, SPAN)
+            result = sbuf("result%d_%d" % (tile_n, j0), [P, width], F32)
+            nc.vector.tensor_tensor(result[:], sums[tile_n, j0][:], res_sb[span][:, tile_n, at : at + width], ADD)
+            store(result, tile_n, j0, width)
+
+        def copy_sum(tile_n, j0, width):
+            y_sb = sbuf("y_sb%d_%d" % (tile_n, j0), [P, width], F32)
+            nc.scalar.copy(y_sb[:], sums[tile_n, j0][:])
+            sums[tile_n, j0] = y_sb
+
+        def add_gpsimd(tile_n, j0, width, tag):
+            span, at = divmod(j0, SPAN)
+            result = sbuf("result%d_%d" % (tile_n, j0), [P, width], F32, tag)
+            nc.gpsimd.tensor_tensor(result[:], sums[tile_n, j0][:], res_sb[span][:, tile_n, at : at + width], ADD)
+            store(result, tile_n, j0, width)
 
         def warm_tensor(count, bank):
             unread = psum.tile([P, PASS], F32, name="unread", tag="bank%d" % bank)
@@ -295,110 +267,126 @@ def tile_list_gmlpt_gelu_res_res_kernel(
                 nc.tensor.matmul_mx(
                     out=unread[:],
                     lhsT=wg_w[0][:, t, :].bitcast(FP8X4),
-                    lhsT_scale=wg_s[:, 0, t, :],
+                    lhsT_scale=v_s[:, 0:P],
                     rhs=wg_w[0][:].rearrange("p t m -> p (t m)").bitcast(FP8X4),
-                    rhs_scale=wg_s[:, 0, :, :].rearrange("p t m -> p (t m)"),
+                    rhs_scale=v_s[:, 0:PASS],
                     start=True,
                     stop=True,
                 )
 
+        nc.sync.dma_start(offsets[:], offs)
+        load_wg(0)
+        load_wg_scales(nc.gpsimd, 0)
+        for block, engine in enumerate((nc.scalar, nc.scalar, nc.sync, nc.scalar)):
+            src = tab_scales[0].rearrange("(quad block) col -> block quad col", block=BLOCKS)[block]
+            engine.dma_start(tab_s[block : P : QUADRANT, :].bitcast(I32), src.bitcast(I32))
+        load_wg_scales(nc.sync, 1)
+        load_wg_scales(nc.scalar, 2)
+        load_wg_scales(nc.sync, 3)
+        nc.sync.dma_start(tab_w[:].bitcast(I32), tab_words[0].rearrange("p col i -> p (col i)").bitcast(I32))
+        nc.scalar.activation(warm[:, 1, :], warm[:, 0, :], GELU)
+        for block, engine in enumerate((nc.gpsimd, nc.gpsimd, nc.scalar, nc.scalar)):
+            load_wd_scales(engine, wd8_s, wd8_scales, WD8_ROW, block)
+        for block in range(2):
+            load_wd_scales(nc.scalar, wd4_s, wd4_scales, 0, block)
+        load_wg(1)
+        load_wu(0)
+        load_wu(1)
+        load_wu(2)
+        load_wu(3)
+        load_wd8(0)
+        nc.sync.dma_start(wd4_w[:].bitcast(I32), wd4_words.rearrange("a p c -> p a c").bitcast(I32))
+        for block in range(2, BLOCKS):
+            load_wd_scales(nc.sync, wd4_s, wd4_scales, 0, block)
+        load_wd8(1)
+        load_res(0)
+        load_res(1)
+        nc.vector.tensor_copy(*wg_reorder(0))
+        nc.scalar.copy(*wg_reorder(1))
         gather(v_s, tab_s, 0, SPAN)
         gather(v_s, tab_s, SPAN, SPAN)
-        warm_tensor(4, 7)
-        for q in range(3):
+        nc.vector.tensor_copy(wg_s[:], wg_s_raw[:].rearrange("p (m t) -> p t m", t=PACK))
+        for q in range(4):
             gather_words(q)
-        gate(0, 0, 0, 0)
-        gate(0, 0, 1, 1)
-        gate(0, 1, 0, 2)
-        gate(0, 1, 1, 3)
-        gate(1, 0, 0, 4)
-        gate(1, 0, 1, 5)
-        gate(0, 2, 0, 6)
-        gate(0, 2, 1, 7)
-        gate(1, 1, 0, 0)
-        gate(1, 1, 1, 1)
-        nc.vector.tensor_copy(*rounding(0, "m i t"))
-        nc.vector.tensor_copy(*rounding(1, "m i t"))
-        quantize_wu(0)
+        warm_tensor(4, 7)
+        for g in range(8):
+            gate(0, g // 2, g % 2, g)
+        for g in range(4):
+            gate(1, g // 2, g % 2, g)
+        nc.vector.tensor_copy(*rounding(0, CHUNK, "m i t"))
+        nc.vector.tensor_copy(*rounding(CHUNK, PASS, "m i t"))
+        quantize_wu(0, 0, 2)
+        quantize_wu(0, 2, 4)
+        nc.vector.tensor_copy(*rounding(PASS, PASS + CHUNK, "m i t"))
+        nc.gpsimd.tensor_scalar(*rounding(PASS + CHUNK, R, "m t i"), 1.0, 0.0, MULT, ADD)
+        h_tile(0, 0, 4)
+        h_tile(0, 4, 2)
+        h_tile(1, 0, 4)
+        h_tile(1, 4, 2)
+        for u in range(4):
+            up(0, u, 4 + u)
+            mult(0, u)
+        quantize_h(0, 0, 2)
+        quantize_h(0, 2, 2)
         quantize_wu(1)
-        gather_words(3, "wu_raw1")
-        nc.gpsimd.tensor_scalar(*rounding(2, "m t i", "tab_w"), 1.0, 0.0, MULT, ADD)
-        up(0, 0, 2)
-        up(0, 1, 3)
-        mult(0, 0)
-        gate(0, 3, 0, 4)
-        up(0, 2, 5)
-        mult(0, 1)
-        up(0, 3, 2)
-        gate(0, 3, 1, 6)
-        mult(0, 2)
-        quantize_h(0, 0)
-        nc.gpsimd.tensor_scalar(*rounding(3, "m t i", "h_bf00", 0, CM // 2), 1.0, 0.0, MULT, ADD)
-        up(0, 4, 3)
-        gate(1, 2, 0, 7)
-        mult(0, 3)
-        gate(1, 2, 1, 0)
+        up(0, 4, 4)
+        gate(1, 2, 0, 0)
         up(0, 5, 5)
+        gate(1, 2, 1, 1)
+        up(0, 6, 6)
+        copy_up(0, 6)
+        up(0, 7, 2)
+        copy_up(0, 7)
+        gate(1, 3, 0, 7)
+        h_tile(0, 6, 2, "wu_bf1")
+        mult_gpsimd(0, 6)
+        mult_gpsimd(0, 7)
         mult(0, 4)
-        quantize_h(0, 1)
-        quantize_wu(2)
-        nc.gpsimd.tensor_scalar(*rounding(3, "m t i", None, CM // 2, CM), 1.0, 0.0, MULT, ADD)
-        gate(1, 3, 0, 1)
-        up(0, 6, 2)
         mult(0, 5)
-        gate(1, 3, 1, 4)
-        up(0, 7, 3)
-        open_sum(0, 0, SPAN, 6)
-        mult(0, 6)
-        quantize_wu(3)
-        open_sum(1, 0, SPAN, 5)
-        open_first(2, 0, SPAN, 7)
-        mult(0, 7)
-        quantize_h(0, 2)
-        quantize_h(0, 3)
-        up(1, 6, 0)
-        mult(1, 6, "h_bf03")
-        up(1, 0, 2)
-        up(1, 1, 1)
-        open_second(2, 0, SPAN)
-        up(1, 2, 3)
+        open_sum(0, 0, SPAN, 3)
+        up(1, 0, 0)
         mult(1, 0)
-        open_sum(3, 0, SPAN, 4)
+        up(1, 1, 1)
         mult(1, 1)
-        up(1, 3, 0)
-        up(1, 7, 2)
+        open_sum(1, 0, SPAN, 4)
+        up(1, 2, 6)
         mult(1, 2)
-        up(1, 4, 1)
-        open_sum(0, SPAN, SPAN, 3)
+        up(1, 3, 2)
         mult(1, 3)
-        quantize_h(1, 0)
-        quantize_h(1, 1)
-        mult(1, 7, "h_bf11")
-        up(1, 5, 0)
+        open_sum(2, 0, SPAN, 5)
+        up(1, 4, 0)
         mult(1, 4)
-        open_sum(1, SPAN, SPAN, 2)
-        close_sum(0, 0, SPAN)
+        quantize_h(1, 0, 4)
+        quantize_h(0, 4, 2)
+        quantize_h(0, 6, 2)
+        gate(1, 3, 1, 7)
+        open_sum(3, 0, SPAN, 1)
+        up(1, 7, 6)
+        copy_up(1, 7)
+        h_tile(1, 6, 2, "wu_bf1")
+        mult_gpsimd(1, 7)
+        up(1, 5, 2)
         mult(1, 5)
-        close_sum(1, 0, SPAN)
+        up(1, 6, 0)
+        mult(1, 6)
+        close_sum(0, 0, SPAN)
         add_and_store(0, 0, SPAN)
-        quantize_h(1, 2)
-        quantize_unit(1, 6)
-        quantize_unit(1, 7)
-        close_sum(2, 0, SPAN)
-        add_and_store(1, 0, SPAN)
-        close_sum(3, 0, SPAN)
-        add_and_store(2, 0, SPAN)
-        close_sum(0, SPAN, SPAN)
-        add_and_store(3, 0, SPAN)
-        close_sum(1, SPAN, SPAN)
-        add_and_store(0, SPAN, SPAN)
-        open_sum(2, SPAN, SPAN, 1)
+        quantize_h(1, 4, 2)
+        quantize_h(1, 6, 2)
+        for n in range(1, 4):
+            close_sum(n, 0, SPAN)
+            add_and_store(n, 0, SPAN)
+        open_sum(0, SPAN, SPAN, 7)
+        open_sum(1, SPAN, SPAN, 6)
+        for n in range(2):
+            close_sum(n, SPAN, SPAN)
+            add_and_store(n, SPAN, SPAN)
+        open_sum(2, SPAN, SPAN, 2)
         close_sum(2, SPAN, SPAN)
-        add_and_store(1, SPAN, SPAN)
         add_and_store(2, SPAN, SPAN)
         open_sum(3, SPAN, SLICE, 0)
         close_sum(3, SPAN, SLICE)
         add_and_store(3, SPAN, SLICE)
-        open_sum(3, SPAN + SLICE, SLICE, 6)
+        open_sum(3, SPAN + SLICE, SLICE, 3)
         close_sum(3, SPAN + SLICE, SLICE)
         add_and_store(3, SPAN + SLICE, SLICE)

@@ -289,9 +289,9 @@ def tile_list_gmlpt_gelu_res_res_kernel(
             load_wd_scales(engine, wd8_s, wd8_scales, WD8_ROW, block)
         for block in range(2):
             load_wd_scales(nc.scalar, wd4_s, wd4_scales, 0, block)
-        load_wg(1)
         load_wu(0)
         load_wu(1)
+        load_wg(1)
         load_wu(2)
         load_wu(3)
         load_wd8(0)
@@ -302,7 +302,6 @@ def tile_list_gmlpt_gelu_res_res_kernel(
         load_res(0)
         load_res(1)
         nc.vector.tensor_copy(*wg_reorder(0))
-        nc.scalar.copy(*wg_reorder(1))
         gather(v_s, tab_s, 0, SPAN)
         gather(v_s, tab_s, SPAN, SPAN)
         nc.vector.tensor_copy(wg_s[:], wg_s_raw[:].rearrange("p (m t) -> p t m", t=PACK))
@@ -311,63 +310,72 @@ def tile_list_gmlpt_gelu_res_res_kernel(
         warm_tensor(4, 7)
         for g in range(8):
             gate(0, g // 2, g % 2, g)
-        for g in range(4):
-            gate(1, g // 2, g % 2, g)
         nc.vector.tensor_copy(*rounding(0, CHUNK, "m i t"))
         nc.vector.tensor_copy(*rounding(CHUNK, PASS, "m i t"))
+        nc.vector.tensor_copy(*wg_reorder(1))
         quantize_wu(0, 0, 2)
         quantize_wu(0, 2, 4)
         nc.vector.tensor_copy(*rounding(PASS, PASS + CHUNK, "m i t"))
         nc.gpsimd.tensor_scalar(*rounding(PASS + CHUNK, R, "m t i"), 1.0, 0.0, MULT, ADD)
+        warm_tensor(2, 1)
         h_tile(0, 0, 4)
         h_tile(0, 4, 2)
         h_tile(1, 0, 4)
         h_tile(1, 4, 2)
-        for u in range(4):
-            up(0, u, 4 + u)
-            mult(0, u)
+        gate(1, 0, 0, 0)
+        up(0, 0, 2)
+        mult(0, 0)
+        up(0, 1, 3)
+        mult(0, 1)
+        gate(1, 0, 1, 1)
+        up(0, 2, 4)
+        mult(0, 2)
+        up(0, 3, 5)
+        mult(0, 3)
         quantize_h(0, 0, 2)
         quantize_h(0, 2, 2)
         quantize_wu(1)
-        up(0, 4, 4)
+        gate(1, 1, 0, 6)
+        up(0, 4, 2)
+        gate(1, 1, 1, 7)
+        up(0, 5, 3)
         gate(1, 2, 0, 0)
-        up(0, 5, 5)
-        gate(1, 2, 1, 1)
-        up(0, 6, 6)
+        up(0, 6, 4)
         copy_up(0, 6)
-        up(0, 7, 2)
+        gate(1, 2, 1, 1)
+        up(0, 7, 5)
         copy_up(0, 7)
-        gate(1, 3, 0, 7)
         h_tile(0, 6, 2, "wu_bf1")
         mult_gpsimd(0, 6)
         mult_gpsimd(0, 7)
         mult(0, 4)
         mult(0, 5)
-        open_sum(0, 0, SPAN, 3)
-        up(1, 0, 0)
+        open_sum(0, 0, SPAN, 6)
+        up(1, 0, 7)
         mult(1, 0)
-        up(1, 1, 1)
+        up(1, 1, 0)
         mult(1, 1)
-        open_sum(1, 0, SPAN, 4)
-        up(1, 2, 6)
+        open_sum(1, 0, SPAN, 2)
+        up(1, 2, 4)
         mult(1, 2)
-        up(1, 3, 2)
+        up(1, 3, 3)
         mult(1, 3)
-        open_sum(2, 0, SPAN, 5)
-        up(1, 4, 0)
+        up(1, 4, 7)
         mult(1, 4)
+        gate(1, 3, 0, 1)
+        open_sum(2, 0, SPAN, 5)
         quantize_h(1, 0, 4)
         quantize_h(0, 4, 2)
         quantize_h(0, 6, 2)
-        gate(1, 3, 1, 7)
-        open_sum(3, 0, SPAN, 1)
-        up(1, 7, 6)
+        gate(1, 3, 1, 0)
+        open_sum(3, 0, SPAN, 4)
+        up(1, 7, 1)
         copy_up(1, 7)
         h_tile(1, 6, 2, "wu_bf1")
         mult_gpsimd(1, 7)
-        up(1, 5, 2)
+        up(1, 5, 3)
         mult(1, 5)
-        up(1, 6, 0)
+        up(1, 6, 7)
         mult(1, 6)
         close_sum(0, 0, SPAN)
         add_and_store(0, 0, SPAN)
@@ -376,17 +384,17 @@ def tile_list_gmlpt_gelu_res_res_kernel(
         for n in range(1, 4):
             close_sum(n, 0, SPAN)
             add_and_store(n, 0, SPAN)
-        open_sum(0, SPAN, SPAN, 7)
-        open_sum(1, SPAN, SPAN, 6)
+        open_sum(0, SPAN, SPAN, 0)
+        open_sum(1, SPAN, SPAN, 1)
         for n in range(2):
             close_sum(n, SPAN, SPAN)
             add_and_store(n, SPAN, SPAN)
-        open_sum(2, SPAN, SPAN, 2)
+        open_sum(2, SPAN, SPAN, 3)
         close_sum(2, SPAN, SPAN)
         add_and_store(2, SPAN, SPAN)
-        open_sum(3, SPAN, SLICE, 0)
+        open_sum(3, SPAN, SLICE, 7)
         close_sum(3, SPAN, SLICE)
         add_and_store(3, SPAN, SLICE)
-        open_sum(3, SPAN + SLICE, SLICE, 3)
+        open_sum(3, SPAN + SLICE, SLICE, 6)
         close_sum(3, SPAN + SLICE, SLICE)
         add_and_store(3, SPAN + SLICE, SLICE)

@@ -90,8 +90,8 @@ def tile_list_gmlpt_gelu_res_res_kernel(
             src = res.rearrange("(tile p) j -> p tile j", p=P)
             nc.sync.dma_start(res_sb[span][:], src[:, :, span * SPAN : (span + 1) * SPAN])
 
-        nc.vector.memset(tab_s[:].bitcast(I32), 0)
         nc.vector.memset(wg_s_raw[:].bitcast(I32), 0)
+        nc.vector.memset(tab_s[:].bitcast(I32), 0)
         nc.vector.memset(wd8_s[:].rearrange("p a n -> p (a n)").bitcast(I32), 0)
         nc.vector.memset(wd4_s[:].rearrange("p a n -> p (a n)").bitcast(I32), 0)
         nc.vector.memset(warm[:, 0, :], 0.0)
@@ -127,6 +127,7 @@ def tile_list_gmlpt_gelu_res_res_kernel(
             )
 
         gates = {}
+        unit_gates = {}
         h_bf = {}
         sums = {}
         ubs = {}
@@ -146,6 +147,22 @@ def tile_list_gmlpt_gelu_res_res_kernel(
             if pair == 0:
                 gates[b, q] = sbuf("gate%d%d" % (b, q), [P, 2, SLICE, 2], F32)
             nc.scalar.activation(gates[b, q][:, pair, :, :], ga[:].rearrange("p e j -> p j e"), GELU)
+
+        def gate_unit(b, u, bank):
+            j0 = u * UNIT
+            ga = psum.tile([P, PACK, UNIT], F32, name="gu%d%d" % (b, u), tag="bank%d" % bank)
+            for t in range(PACK):
+                nc.tensor.matmul_mx(
+                    out=ga[:, t, :],
+                    lhsT=wg_w[b][:, t, :].bitcast(FP8X4),
+                    lhsT_scale=wg_s[WG_ROW + BLOCKS * b : P, t, :],
+                    rhs=v_w[j0 // SLICE][:, j0 % SLICE : j0 % SLICE + UNIT].bitcast(FP8X4),
+                    rhs_scale=v_s[:, j0 : j0 + UNIT],
+                    start=True,
+                    stop=True,
+                )
+            unit_gates[b, u] = sbuf("gate_unit%d%d" % (b, u), [P, UNIT, PACK], F32)
+            nc.scalar.activation(unit_gates[b, u][:], ga[:].rearrange("p t j -> p j t"), GELU)
 
         def up(b, u, bank):
             j0 = u * UNIT
@@ -172,6 +189,8 @@ def tile_list_gmlpt_gelu_res_res_kernel(
             return tile_h[:, (u - u0) * UNIT : (u - u0 + units) * UNIT, :]
 
         def gelus(b, u):
+            if (b, u) in unit_gates:
+                return unit_gates[b, u][:].rearrange("p j (pair e) -> p j pair e", e=2)
             q, part = divmod(u, SLICE // UNIT)
             return gates[b, q][:, :, part * UNIT : (part + 1) * UNIT, :].rearrange("p pair j e -> p j pair e")
 
@@ -185,8 +204,9 @@ def tile_list_gmlpt_gelu_res_res_kernel(
             ubs[b, u] = ub_sb
 
         def mult_gpsimd(b, u):
-            h = h_part(b, u, 1).rearrange("p j (pair e) -> p j pair e", e=2)
-            nc.gpsimd.tensor_tensor(h, ubs[b, u][:].rearrange("p j (pair e) -> p j pair e", e=2), gelus(b, u), MULT)
+            flat = "p j t -> p (j t)"
+            h = h_part(b, u, 1).rearrange(flat)
+            nc.gpsimd.tensor_tensor(h, ubs[b, u][:].rearrange(flat), unit_gates[b, u][:].rearrange(flat), MULT)
 
         def quantize_h(b, u, units):
             cols = slice(u * UNIT, (u + units) * UNIT)
@@ -308,8 +328,10 @@ def tile_list_gmlpt_gelu_res_res_kernel(
         for q in range(4):
             gather_words(q)
         warm_tensor(4, 7)
-        for g in range(8):
+        for g in range(6):
             gate(0, g // 2, g % 2, g)
+        gate_unit(0, 6, 6)
+        gate_unit(0, 7, 7)
         nc.vector.tensor_copy(*rounding(0, CHUNK, "m i t"))
         nc.vector.tensor_copy(*rounding(CHUNK, PASS, "m i t"))
         nc.vector.tensor_copy(*wg_reorder(1))
@@ -317,7 +339,8 @@ def tile_list_gmlpt_gelu_res_res_kernel(
         quantize_wu(0, 2, 4)
         nc.vector.tensor_copy(*rounding(PASS, PASS + CHUNK, "m i t"))
         nc.gpsimd.tensor_scalar(*rounding(PASS + CHUNK, R, "m t i"), 1.0, 0.0, MULT, ADD)
-        warm_tensor(2, 1)
+        for bank in range(1, 3):
+            warm_tensor(1, bank)
         h_tile(0, 0, 4)
         h_tile(0, 4, 2)
         h_tile(1, 0, 4)
@@ -362,18 +385,18 @@ def tile_list_gmlpt_gelu_res_res_kernel(
         mult(1, 3)
         up(1, 4, 7)
         mult(1, 4)
-        gate(1, 3, 0, 1)
+        gate_unit(1, 7, 1)
+        gate_unit(1, 6, 0)
         open_sum(2, 0, SPAN, 5)
         quantize_h(1, 0, 4)
         quantize_h(0, 4, 2)
         quantize_h(0, 6, 2)
-        gate(1, 3, 1, 0)
-        open_sum(3, 0, SPAN, 4)
-        up(1, 7, 1)
+        up(1, 7, 4)
         copy_up(1, 7)
+        open_sum(3, 0, SPAN, 3)
         h_tile(1, 6, 2, "wu_bf1")
         mult_gpsimd(1, 7)
-        up(1, 5, 3)
+        up(1, 5, 1)
         mult(1, 5)
         up(1, 6, 7)
         mult(1, 6)
@@ -385,11 +408,11 @@ def tile_list_gmlpt_gelu_res_res_kernel(
             close_sum(n, 0, SPAN)
             add_and_store(n, 0, SPAN)
         open_sum(0, SPAN, SPAN, 0)
-        open_sum(1, SPAN, SPAN, 1)
+        open_sum(1, SPAN, SPAN, 4)
         for n in range(2):
             close_sum(n, SPAN, SPAN)
             add_and_store(n, SPAN, SPAN)
-        open_sum(2, SPAN, SPAN, 3)
+        open_sum(2, SPAN, SPAN, 1)
         close_sum(2, SPAN, SPAN)
         add_and_store(2, SPAN, SPAN)
         open_sum(3, SPAN, SLICE, 7)

@@ -412,12 +412,13 @@ def tile_list_gmlpt_gelu_res_res_kernel(
         for n in range(2):
             close_sum(n, SPAN, SPAN)
             add_and_store(n, SPAN, SPAN)
-        open_sum(2, SPAN, SPAN, 1)
-        close_sum(2, SPAN, SPAN)
-        add_and_store(2, SPAN, SPAN)
-        open_sum(3, SPAN, SLICE, 7)
-        close_sum(3, SPAN, SLICE)
-        add_and_store(3, SPAN, SLICE)
-        open_sum(3, SPAN + SLICE, SLICE, 6)
-        close_sum(3, SPAN + SLICE, SLICE)
-        add_and_store(3, SPAN + SLICE, SLICE)
+        for tile_n, j0, width, bank in (
+            (2, SPAN, SLICE, 1),
+            (2, SPAN + SLICE, SLICE, 7),
+            (3, SPAN, SLICE, 6),
+            (3, SPAN + SLICE, UNIT, 2),
+            (3, J - UNIT, UNIT, 5),
+        ):
+            open_sum(tile_n, j0, width, bank)
+            close_sum(tile_n, j0, width)
+            add_and_store(tile_n, j0, width)

@@ -400,20 +400,21 @@ def tile_list_gmlpt_gelu_res_res_kernel(
         mult(1, 5)
         up(1, 6, 7)
         mult(1, 6)
-        close_sum(0, 0, SPAN)
-        add_and_store(0, 0, SPAN)
+        for n in range(2):
+            close_sum(n, 0, SPAN)
+            add_and_store(n, 0, SPAN)
         quantize_h(1, 4, 2)
         quantize_h(1, 6, 2)
-        for n in range(1, 4):
+        for n in range(2, 4):
             close_sum(n, 0, SPAN)
             add_and_store(n, 0, SPAN)
         open_sum(0, SPAN, SPAN, 0)
         open_sum(1, SPAN, SPAN, 4)
-        for n in range(2):
-            close_sum(n, SPAN, SPAN)
-            add_and_store(n, SPAN, SPAN)
+        open_sum(2, SPAN, SLICE, 1)
+        for tile_n, width in ((0, SPAN), (1, SPAN), (2, SLICE)):
+            close_sum(tile_n, SPAN, width)
+            add_and_store(tile_n, SPAN, width)
         for tile_n, j0, width, bank in (
-            (2, SPAN, SLICE, 1),
             (2, SPAN + SLICE, SLICE, 7),
             (3, SPAN, SLICE, 6),
             (3, SPAN + SLICE, UNIT, 2),

from contextlib import ExitStack

import concourse.mybir as mybir

K, R, N, T, J = 512, 1024, 512, 2048, 1024
FLOPS = 2 * K * R * J * 2 + 2 * R * N * J * 2

F32 = mybir.dt.float32
BF16 = mybir.dt.bfloat16
I32 = mybir.dt.int32
U32 = mybir.dt.uint32
U16 = mybir.dt.uint16
U8 = mybir.dt.uint8
FP8X4 = mybir.dt.float8_e4m3fn_x4
FP4X4 = mybir.dt.float4_e2m1fn_x4
GELU = mybir.ActivationFunctionType.Gelu_apprx_tanh
MULT = mybir.AluOpType.mult
ADD = mybir.AluOpType.add

P = 128
PACK = 4
PASS = P * PACK
HALVES = R // PASS
QUADRANT = 32
BLOCKS = 4
LIST_ROWS = 16
SLICE = 256
UNIT = 128
SPAN = 512
TILES = N // P
CHUNK = 256
CM = CHUNK // PACK
WG_ROW = 4
WD8_ROW = 4


def tile_list_gmlpt_gelu_res_res_kernel(
    tc, tab_words, tab_scales, wg_words, wg_scales, wu, wd4_words, wd4_scales, wd8_words, wd8_scales, res, offs, out
):
    nc = tc.nc
    with ExitStack() as ctx:
        keep = ctx.enter_context(tc.tile_pool(name="keep", bufs=1))
        psum = ctx.enter_context(tc.psum_pool(name="psum", bufs=1))

        def sbuf(name, shape, dtype, tag=None):
            return keep.tile(shape, dtype, name=name, tag=tag or name, align_bytes=256)

        offsets = keep.tile([P, J // LIST_ROWS], U16, name="offsets")
        tab_w = sbuf("tab_w", [P, T], U32)
        tab_s = sbuf("tab_s", [P, T], U8)
        wg_w_raw = [sbuf("wg_w_raw%d" % b, [P, PASS], U32) for b in range(HALVES)]
        wg_s_raw = sbuf("wg_s_raw", [P, PASS], U8)
        wg_w = [sbuf("wg_w%d" % b, [P, PACK, P], U32) for b in range(HALVES)]
        wg_s = sbuf("wg_s", [P, PACK, P], U8)
        wu_raw = [sbuf("wu_raw%d" % c, [P, PACK, CHUNK], F32) for c in range(R // CHUNK)]
        wu_w = [sbuf("wu_w%d" % b, [P, PASS], U32) for b in range(HALVES)]
        wu_s = [sbuf("wu_s%d" % b, [P, PASS], U8) for b in range(HALVES)]
        wd4_w = sbuf("wd4_w", [P, HALVES, 2 * N], U8)
        wd8_w = [sbuf("wd8_w%d" % b, [P, N], U32) for b in range(HALVES)]
        wd4_s = sbuf("wd4_s", [P, HALVES, N], U8)
        wd8_s = sbuf("wd8_s", [P, HALVES, N], U8)
        res_sb = [sbuf("res%d" % span, [P, TILES, SPAN], F32) for span in range(J // SPAN)]
        v_s = sbuf("v_s", [P, J], U8)
        v_w = {}
        h_w = [sbuf("h_w%d" % b, [P, J], U32) for b in range(HALVES)]
        h_s = [sbuf("h_s%d" % b, [P, J], U8) for b in range(HALVES)]
        warm = sbuf("warm", [P, 2, 8], F32)

        def load_wg(b):
            words = wg_words[0].rearrange("p r i -> p (r i)").bitcast(I32)
            nc.sync.dma_start(wg_w_raw[b][:].bitcast(I32), words[:, b * PASS : (b + 1) * PASS])

        def load_wu(c):
            src = wu.rearrange("(p i) r -> p i r", i=PACK)
            nc.sync.dma_start(wu_raw[c][:], src[:, :, c * CHUNK : (c + 1) * CHUNK])

        def load_wd8(b):
            nc.sync.dma_start(wd8_w[b][:].bitcast(I32), wd8_words[b].rearrange("p n i -> p (n i)").bitcast(I32))

        def load_wg_scales(engine, quad):
            src = wg_scales[0][BLOCKS * quad : BLOCKS * (quad + 1), :].rearrange("block (b c) -> b block c", b=HALVES)
            partition = QUADRANT * quad + WG_ROW
            engine.dma_start(wg_s_raw[partition : partition + BLOCKS * HALVES, :].bitcast(I32), src.bitcast(I32))

        def load_wd_scales(engine, wd_s, scales, row, block):
            src = scales.rearrange("a (quad block) n -> block quad a n", block=BLOCKS)[block]
            engine.dma_start(wd_s[row + block : P : QUADRANT, :, :].bitcast(I32), src.bitcast(I32))

        def load_res(span):
            src = res.rearrange("(tile p) j -> p tile j", p=P)
            nc.sync.dma_start(res_sb[span][:], src[:, :, span * SPAN : (span + 1) * SPAN])

        nc.vector.memset(wg_s_raw[:].bitcast(I32), 0)
        nc.vector.memset(tab_s[:].bitcast(I32), 0)
        nc.vector.memset(wd8_s[:].rearrange("p a n -> p (a n)").bitcast(I32), 0)
        nc.vector.memset(wd4_s[:].rearrange("p a n -> p (a n)").bitcast(I32), 0)
        nc.vector.memset(warm[:, 0, :], 0.0)
        def gather(dst, table, j0, width):
            entries = offsets[:, j0 // LIST_ROWS : (j0 + width) // LIST_ROWS]
            nc.vector.tensor_copy(dst[:, j0 : j0 + width], table[:].indirect(entries))

        def gather_words(q, tag=None):
            v_w[q] = sbuf("v_w%d" % q, [P, SLICE], U32, tag)
            entries = offsets[:, q * SLICE // LIST_ROWS : (q + 1) * SLICE // LIST_ROWS]
            nc.vector.tensor_copy(v_w[q][:], tab_w[:].indirect(entries))

        def wg_reorder(b):
            return wg_w[b][:].rearrange("p t m -> p m t"), wg_w_raw[b][:].rearrange("p (m t) -> p m t", t=PACK)

        wu_bf = {}

        def rounding(c0, c1, walk, tag=None):
            b = c0 // PASS
            if b not in wu_bf:
                wu_bf[b] = sbuf("wu_bf%d" % b, [P, PACK, P, PACK], BF16, tag)
            c, at = divmod(c0, CHUNK)
            first = c0 % PASS // PACK
            dst = wu_bf[b][:, :, first : first + (c1 - c0) // PACK, :].rearrange("p t m i -> p " + walk)
            src = wu_raw[c][:, :, at : at + c1 - c0].rearrange("p i (m t) -> p " + walk, t=PACK)
            return dst, src

        def quantize_wu(b, t0=0, t1=PACK):
            nc.vector.quantize_mx(
                out=wu_w[b][:, t0 * P : t1 * P].bitcast(FP8X4),
                scales=wu_s[b][:, t0 * P : t1 * P],
                in_=wu_bf[b][:, t0:t1, :, :].rearrange("p t m i -> p (t m i)"),
            )

        gates = {}
        unit_gates = {}
        h_bf = {}
        sums = {}
        ubs = {}

        def gate(b, q, pair, bank):
            ga = psum.tile([P, 2, SLICE], F32, name="ga%d%d%d" % (b, q, pair), tag="bank%d" % bank)
            for e in range(2):
                nc.tensor.matmul_mx(
                    out=ga[:, e, :],
                    lhsT=wg_w[b][:, 2 * pair + e, :].bitcast(FP8X4),
                    lhsT_scale=wg_s[WG_ROW + BLOCKS * b : P, 2 * pair + e, :],
                    rhs=v_w[q][:].bitcast(FP8X4),
                    rhs_scale=v_s[:, q * SLICE : (q + 1) * SLICE],
                    start=True,
                    stop=True,
                )
            if pair == 0:
                gates[b, q] = sbuf("gate%d%d" % (b, q), [P, 2, SLICE, 2], F32)
            nc.scalar.activation(gates[b, q][:, pair, :, :], ga[:].rearrange("p e j -> p j e"), GELU)

        def gate_unit(b, u, bank):
            j0 = u * UNIT
            ga = psum.tile([P, PACK, UNIT], F32, name="gu%d%d" % (b, u), tag="bank%d" % bank)
            for t in range(PACK):
                nc.tensor.matmul_mx(
                    out=ga[:, t, :],
                    lhsT=wg_w[b][:, t, :].bitcast(FP8X4),
                    lhsT_scale=wg_s[WG_ROW + BLOCKS * b : P, t, :],
                    rhs=v_w[j0 // SLICE][:, j0 % SLICE : j0 % SLICE + UNIT].bitcast(FP8X4),
                    rhs_scale=v_s[:, j0 : j0 + UNIT],
                    start=True,
                    stop=True,
                )
            unit_gates[b, u] = sbuf("gate_unit%d%d" % (b, u), [P, UNIT, PACK], F32)
            nc.scalar.activation(unit_gates[b, u][:], ga[:].rearrange("p t j -> p j t"), GELU)

        def up(b, u, bank):
            j0 = u * UNIT
            ub = psum.tile([P, PACK, UNIT], F32, name="ub%d%d" % (b, u), tag="bank%d" % bank)
            for t in range(PACK):
                nc.tensor.matmul_mx(
                    out=ub[:, t, :],
                    lhsT=wu_w[b][:, t * P : (t + 1) * P].bitcast(FP8X4),
                    lhsT_scale=wu_s[b][:, t * P : (t + 1) * P],
                    rhs=v_w[j0 // SLICE][:, j0 % SLICE : j0 % SLICE + UNIT].bitcast(FP8X4),
                    rhs_scale=v_s[:, j0 : j0 + UNIT],
                    start=True,
                    stop=True,
                )
            ubs[b, u] = ub

        def h_tile(b, u0, units, tag=None):
            tile_h = sbuf("h_bf%d%d" % (b, u0), [P, units * UNIT, PACK], BF16, tag)
            for u in range(u0, u0 + units):
                h_bf[b, u] = (tile_h, u0)

        def h_part(b, u, units):
            tile_h, u0 = h_bf[b, u]
            return tile_h[:, (u - u0) * UNIT : (u - u0 + units) * UNIT, :]

        def gelus(b, u):
            if (b, u) in unit_gates:
                return unit_gates[b, u][:].rearrange("p j (pair e) -> p j pair e", e=2)
            q, part = divmod(u, SLICE // UNIT)
            return gates[b, q][:, :, part * UNIT : (part + 1) * UNIT, :].rearrange("p pair j e -> p j pair e")

        def mult(b, u):
            h = h_part(b, u, 1).rearrange("p j (pair e) -> p j pair e", e=2)
            nc.vector.tensor_tensor(h, ubs[b, u][:].rearrange("p (pair e) j -> p j pair e", e=2), gelus(b, u), MULT)

        def copy_up(b, u):
            ub_sb = sbuf("ub_sb%d%d" % (b, u), [P, UNIT, PACK], F32)
            nc.scalar.copy(ub_sb[:], ubs[b, u][:].rearrange("p t j -> p j t"))
            ubs[b, u] = ub_sb

        def mult_gpsimd(b, u):
            flat = "p j t -> p (j t)"
            h = h_part(b, u, 1).rearrange(flat)
            nc.gpsimd.tensor_tensor(h, ubs[b, u][:].rearrange(flat), unit_gates[b, u][:].rearrange(flat), MULT)

        def quantize_h(b, u, units):
            cols = slice(u * UNIT, (u + units) * UNIT)
            nc.vector.quantize_mx(
                out=h_w[b][:, cols].bitcast(FP8X4),
                scales=h_s[b][:, cols],
                in_=h_part(b, u, units).rearrange("p j t -> p (j t)"),
            )

        def pass8(y, b, tile_n, j0, width, start):
            rows = slice(tile_n * P, (tile_n + 1) * P)
            nc.tensor.matmul_mx(
                out=y,
                lhsT=wd8_w[b][:, rows].bitcast(FP8X4),
                lhsT_scale=wd8_s[WD8_ROW:P, b, rows],
                rhs=h_w[b][:, j0 : j0 + width].bitcast(FP8X4),
                rhs_scale=h_s[b][:, j0 : j0 + width],
                start=start,
                stop=False,
            )

        def pass4(y, b, tile_n, j0, width, stop):
            rows = slice(tile_n * P, (tile_n + 1) * P)
            nc.tensor.matmul_mx(
                out=y,
                lhsT=wd4_w[:, b, 2 * tile_n * P : 2 * (tile_n + 1) * P].bitcast(FP4X4),
                lhsT_scale=wd4_s[:, b, rows],
                rhs=h_w[b][:, j0 : j0 + width].bitcast(FP8X4),
                rhs_scale=h_s[b][:, j0 : j0 + width],
                start=False,
                stop=stop,
            )

        def passes(y, b, tile_n, j0, width, start, stop):
            pass8(y, b, tile_n, j0, width, start)
            pass4(y, b, tile_n, j0, width, stop)

        def open_first(tile_n, j0, width, bank):
            sums[tile_n, j0] = psum.tile([P, width], F32, name="y%d_%d" % (tile_n, j0), tag="bank%d" % bank)
            pass8(sums[tile_n, j0][:], 0, tile_n, j0, width, True)

        def open_second(tile_n, j0, width):
            pass4(sums[tile_n, j0][:], 0, tile_n, j0, width, False)

        def open_sum(tile_n, j0, width, bank):
            sums[tile_n, j0] = psum.tile([P, width], F32, name="y%d_%d" % (tile_n, j0), tag="bank%d" % bank)
            passes(sums[tile_n, j0][:], 0, tile_n, j0, width, True, False)

        def close_sum(tile_n, j0, width):
            passes(sums[tile_n, j0][:], 1, tile_n, j0, width, False, True)

        def close_part(tile_n, base, j0, last):
            passes(sums[tile_n, base][:, j0 - base : j0 - base + SLICE], 1, tile_n, j0, SLICE, False, last)

        def store(result, tile_n, j0, width):
            nc.sync.dma_start(out[tile_n * P : (tile_n + 1) * P, j0 : j0 + width], result[:])

        def add_and_store(tile_n, j0, width):
            span, at = divmod(j0, SPAN)
            result = sbuf("result%d_%d" % (tile_n, j0), [P, width], F32)
            nc.vector.tensor_tensor(result[:], sums[tile_n, j0][:], res_sb[span][:, tile_n, at : at + width], ADD)
            store(result, tile_n, j0, width)

        def copy_sum(tile_n, j0, width):
            y_sb = sbuf("y_sb%d_%d" % (tile_n, j0), [P, width], F32)
            nc.scalar.copy(y_sb[:], sums[tile_n, j0][:])
            sums[tile_n, j0] = y_sb

        def add_gpsimd(tile_n, j0, width, tag):
            span, at = divmod(j0, SPAN)
            result = sbuf("result%d_%d" % (tile_n, j0), [P, width], F32, tag)
            nc.gpsimd.tensor_tensor(result[:], sums[tile_n, j0][:], res_sb[span][:, tile_n, at : at + width], ADD)
            store(result, tile_n, j0, width)

        def warm_tensor(count, bank):
            unread = psum.tile([P, PASS], F32, name="unread", tag="bank%d" % bank)
            for t in range(count):
                nc.tensor.matmul_mx(
                    out=unread[:],
                    lhsT=wg_w[0][:, t, :].bitcast(FP8X4),
                    lhsT_scale=v_s[:, 0:P],
                    rhs=wg_w[0][:].rearrange("p t m -> p (t m)").bitcast(FP8X4),
                    rhs_scale=v_s[:, 0:PASS],
                    start=True,
                    stop=True,
                )

        nc.sync.dma_start(offsets[:], offs)
        load_wg(0)
        load_wg_scales(nc.gpsimd, 0)
        for block, engine in enumerate((nc.scalar, nc.scalar, nc.sync, nc.scalar)):
            src = tab_scales[0].rearrange("(quad block) col -> block quad col", block=BLOCKS)[block]
            engine.dma_start(tab_s[block : P : QUADRANT, :].bitcast(I32), src.bitcast(I32))
        load_wg_scales(nc.sync, 1)
        load_wg_scales(nc.scalar, 2)
        load_wg_scales(nc.sync, 3)
        nc.sync.dma_start(tab_w[:].bitcast(I32), tab_words[0].rearrange("p col i -> p (col i)").bitcast(I32))
        nc.scalar.activation(warm[:, 1, :], warm[:, 0, :], GELU)
        for block, engine in enumerate((nc.gpsimd, nc.gpsimd, nc.scalar, nc.scalar)):
            load_wd_scales(engine, wd8_s, wd8_scales, WD8_ROW, block)
        for block in range(2):
            load_wd_scales(nc.scalar, wd4_s, wd4_scales, 0, block)
        load_wu(0)
        load_wu(1)
        load_wg(1)
        load_wu(2)
        load_wu(3)
        load_wd8(0)
        nc.sync.dma_start(wd4_w[:].bitcast(I32), wd4_words.rearrange("a p c -> p a c").bitcast(I32))
        for block in range(2, BLOCKS):
            load_wd_scales(nc.sync, wd4_s, wd4_scales, 0, block)
        load_wd8(1)
        load_res(0)
        load_res(1)
        nc.vector.tensor_copy(*wg_reorder(0))
        gather(v_s, tab_s, 0, SPAN)
        gather(v_s, tab_s, SPAN, SPAN)
        nc.vector.tensor_copy(wg_s[:], wg_s_raw[:].rearrange("p (m t) -> p t m", t=PACK))
        for q in range(4):
            gather_words(q)
        warm_tensor(4, 7)
        for g in range(6):
            gate(0, g // 2, g % 2, g)
        gate_unit(0, 6, 6)
        gate_unit(0, 7, 7)
        nc.vector.tensor_copy(*rounding(0, CHUNK, "m i t"))
        nc.vector.tensor_copy(*rounding(CHUNK, PASS, "m i t"))
        nc.vector.tensor_copy(*wg_reorder(1))
        quantize_wu(0, 0, 2)
        quantize_wu(0, 2, 4)
        nc.vector.tensor_copy(*rounding(PASS, PASS + CHUNK, "m i t"))
        nc.gpsimd.tensor_scalar(*rounding(PASS + CHUNK, R, "m t i"), 1.0, 0.0, MULT, ADD)
        for bank in range(1, 3):
            warm_tensor(1, bank)
        h_tile(0, 0, 4)
        h_tile(0, 4, 2)
        h_tile(1, 0, 4)
        h_tile(1, 4, 2)
        gate(1, 0, 0, 0)
        up(0, 0, 2)
        mult(0, 0)
        up(0, 1, 3)
        mult(0, 1)
        gate(1, 0, 1, 1)
        up(0, 2, 4)
        mult(0, 2)
        up(0, 3, 5)
        mult(0, 3)
        quantize_h(0, 0, 2)
        quantize_h(0, 2, 2)
        quantize_wu(1)
        gate(1, 1, 0, 6)
        up(0, 4, 2)
        gate(1, 1, 1, 7)
        up(0, 5, 3)
        gate(1, 2, 0, 0)
        up(0, 6, 4)
        copy_up(0, 6)
        gate(1, 2, 1, 1)
        up(0, 7, 5)
        copy_up(0, 7)
        h_tile(0, 6, 2, "wu_bf1")
        mult_gpsimd(0, 6)
        mult_gpsimd(0, 7)
        mult(0, 4)
        mult(0, 5)
        open_sum(0, 0, SPAN, 6)
        up(1, 0, 7)
        mult(1, 0)
        up(1, 1, 0)
        mult(1, 1)
        open_sum(1, 0, SPAN, 2)
        up(1, 2, 4)
        mult(1, 2)
        up(1, 3, 3)
        mult(1, 3)
        up(1, 4, 7)
        mult(1, 4)
        gate_unit(1, 7, 1)
        gate_unit(1, 6, 0)
        open_sum(2, 0, SPAN, 5)
        quantize_h(1, 0, 4)
        quantize_h(0, 4, 2)
        quantize_h(0, 6, 2)
        up(1, 7, 4)
        copy_up(1, 7)
        open_sum(3, 0, SPAN, 3)
        h_tile(1, 6, 2, "wu_bf1")
        mult_gpsimd(1, 7)
        up(1, 5, 1)
        mult(1, 5)
        up(1, 6, 7)
        mult(1, 6)
        for n in range(2):
            close_sum(n, 0, SPAN)
            add_and_store(n, 0, SPAN)
        quantize_h(1, 4, 2)
        quantize_h(1, 6, 2)
        for n in range(2, 4):
            close_sum(n, 0, SPAN)
            add_and_store(n, 0, SPAN)
        open_sum(0, SPAN, SPAN, 0)
        open_sum(1, SPAN, SPAN, 4)
        open_sum(2, SPAN, SLICE, 1)
        for tile_n, width in ((0, SPAN), (1, SPAN), (2, SLICE)):
            close_sum(tile_n, SPAN, width)
            add_and_store(tile_n, SPAN, width)
        for tile_n, j0, width, bank in (
            (2, SPAN + SLICE, SLICE, 7),
            (3, SPAN, SLICE, 6),
            (3, SPAN + SLICE, UNIT, 2),
            (3, J - UNIT, UNIT, 5),
        ):
            open_sum(tile_n, j0, width, bank)
            close_sum(tile_n, j0, width)
            add_and_store(tile_n, j0, width)
